import numpy as np
import ml_dtypes


def mxq(x, axis, fmt="e4m3"):
    dtype, down = {"e4m3": (ml_dtypes.float8_e4m3fn, 7), "e5m2": (ml_dtypes.float8_e5m2, 14)}[fmt]
    v = np.moveaxis(np.asarray(x, np.float32).astype(ml_dtypes.bfloat16).astype(np.float64), axis, -1)
    blocks = v.reshape(v.shape[:-1] + (-1, 32))
    amax = np.abs(blocks).max(-1, keepdims=True)
    byte = np.maximum(np.where(amax > 0, np.frexp(amax)[1] - 1 + 127, 0) - down, 1)
    scale = np.exp2(byte - 127.0)
    codes = (blocks / scale).astype(np.float32).astype(dtype).astype(np.float64)
    return np.moveaxis((codes * scale).reshape(v.shape), -1, axis)


WIDE = False


def mx_kscale(k):
    if not WIDE:
        return np.ones(k)
    levels = np.array([10, -10, 5, -5, 0])
    if k % 512:
        return np.exp2(np.random.permutation(np.resize(levels, k // 32))).repeat(32)
    a = np.empty((k // 512, 16))
    for p in range(k // 512):
        a[p, :8] = np.random.permutation(np.resize(levels, 8))
        for g in range(8):
            far = levels[np.abs(levels - a[p, g]) >= 10]
            a[p, g + 8] = far[np.random.randint(len(far))]
    return np.exp2(a.ravel()).repeat(32)


def f64(x):
    return np.asarray(x).astype(np.float64)


def striped(idx):
    return np.tile(idx.reshape(-1, 16).T, (8, 1)).astype(np.uint16)


def unstriped(offs):
    return offs[:16].T.reshape(-1).astype(np.int64)


E2M1 = np.array([0.0, 0.5, 1.0, 1.5, 2.0, 3.0, 4.0, 6.0, -0.0, -0.5, -1.0, -1.5, -2.0, -3.0, -4.0, -6.0])


def pack_weight(w, fmt):
    k, n = w.shape
    w = f64(np.asarray(w, np.float32).astype(ml_dtypes.bfloat16)).reshape(k // 32, 32, n)
    amax = np.abs(w).max(1)
    if fmt == "e4m3":
        byte = np.frexp(amax)[1] - 1 + 127 - 7
    else:
        mant, ex = np.frexp(amax / 6.0)
        byte = np.where(mant > 0.5, ex, ex - 1) + 127
    byte = np.clip(np.where(amax > 0, byte, 1), 1, 254)
    scaled = (w * np.exp2(127.0 - byte)[:, None, :]).reshape(k, n).astype(np.float32)
    by_word = np.ascontiguousarray(scaled.reshape(k // 512, 128, 4, n).transpose(0, 1, 3, 2))
    if fmt == "e4m3":
        words = by_word.astype(ml_dtypes.float8_e4m3fn).view(np.uint8)
    else:
        c = by_word.astype(ml_dtypes.float4_e2m1fn).view(np.uint8) & 0xF
        words = (c[..., 0::2] | (c[..., 1::2] << 4)).reshape(k // 512, 128, 2 * n)
    return np.ascontiguousarray(words), np.ascontiguousarray(byte.astype(np.uint8).reshape(k // 512, 16, n))


def unpack_weight(words, scales, fmt):
    g, _, n = scales.shape
    words = np.ascontiguousarray(words).reshape(g, 128, n, -1)
    if fmt == "e4m3":
        vals = words.view(ml_dtypes.float8_e4m3fn).astype(np.float64)
    else:
        nib = np.empty((g, 128, n, 4), np.uint8)
        nib[..., 0::2] = words & 0xF
        nib[..., 1::2] = words >> 4
        vals = E2M1[nib]
    vals = vals * np.repeat(np.exp2(scales.astype(np.float64) - 127.0), 8, axis=1)[..., None]
    return vals.transpose(0, 1, 3, 2).reshape(g * 512, n)


def gelu(v):
    return 0.5 * v * (1.0 + np.tanh(np.sqrt(2.0 / np.pi) * (v + 0.044715 * v**3)))


def striped8(idx):
    return np.concatenate([v.reshape(-1, 16).T for v in idx]).astype(np.uint16)


def unstriped8(offs):
    return np.stack([offs[16 * g:16 * g + 16].T.reshape(-1) for g in range(8)]).astype(np.int64)


def runs(v, idx8):
    k = np.arange(v.shape[0])
    return v[k[:, None], idx8[k % 512 // 64]]


K, K2, T, S, H, N = 1024, 512, 2048, 1024, 1024, 256

def setup_inputs():
    n = np.random.standard_normal
    s = mx_kscale(K)[:, None]
    s2 = mx_kscale(K2)[:, None]
    u = mx_kscale(H)[:, None]
    tab_words, tab_scales = pack_weight(n((K, T)) * s, "e4m3")
    tab2_words, tab2_scales = pack_weight(n((K2, T)) * s2, "e4m3")
    w2_words, w2_scales = pack_weight(0.35 * n((K2, H)) / np.sqrt(K2) / s2, "e2m1")
    w3_words, w3_scales = pack_weight(2.0 * n((H, N)) / np.sqrt(H) / u, "e2m1")
    return {
        "tab_words": tab_words, "tab_scales": tab_scales,
        "tab2_words": tab2_words, "tab2_scales": tab2_scales,
        "offs": striped8(np.stack([np.random.permutation(T)[:S] for _ in range(8)])),
        "offs2": striped(np.random.permutation(T)[:S]),
        "w1": (0.35 * n((K, H)) / np.sqrt(K) / s).astype(np.float32),
        "w2_words": w2_words, "w2_scales": w2_scales,
        "w3_words": w3_words, "w3_scales": w3_scales,
        "w4": (n((H, N)) / np.sqrt(H) / u).astype(np.float32),
        "gs": (np.exp(0.3 * n(H)) * u[:, 0]).astype(np.float32),
        "gc": (np.exp(0.3 * n(H)) * u[:, 0]).astype(np.float32),
    }

def reference(tab_words, tab_scales, tab2_words, tab2_scales, offs, offs2, w1,
              w2_words, w2_scales, w3_words, w3_scales, w4, gs, gc):
    v = runs(unpack_weight(tab_words, tab_scales, "e4m3"), unstriped8(offs))
    v2 = unpack_weight(tab2_words, tab2_scales, "e4m3")[:, unstriped(offs2)]
    a = mxq(f64(w1), 0, "e4m3").T @ v
    b = unpack_weight(w2_words, w2_scales, "e2m1").T @ v2
    d = a - b
    zs = f64(gs)[:, None] * np.sin(d)
    zc = f64(gc)[:, None] * np.cos(d)
    ys = unpack_weight(w3_words, w3_scales, "e2m1").T @ mxq(zs, 0, "e4m3")
    yc = mxq(f64(w4), 0, "e4m3").T @ mxq(zc, 0, "e4m3")
    return ys * yc

@@ -1,0 +1,296 @@
+from contextlib import ExitStack
+
+import concourse.mybir as mybir
+
+K, K2, T, S, H, N = 1024, 512, 2048, 1024, 1024, 256
+FLOPS = 2 * S * (K * H + K2 * H + 2 * H * N)
+
+F32 = mybir.dt.float32
+BF16 = mybir.dt.bfloat16
+I32 = mybir.dt.int32
+U32 = mybir.dt.uint32
+U16 = mybir.dt.uint16
+U8 = mybir.dt.uint8
+FP8X4 = mybir.dt.float8_e4m3fn_x4
+FP4X4 = mybir.dt.float4_e2m1fn_x4
+ACT = mybir.ActivationFunctionType
+ALU = mybir.AluOpType
+
+P = 128
+PACK = 4
+K_PASS = P * PACK
+PASSES = K // K_PASS
+BLOCKS = H // K_PASS
+JB = 128
+UNIT = 256
+UNITS = S // UNIT
+
+
+def tile_list_islanding_separation_kernel(
+    tc, tab_words, tab_scales, tab2_words, tab2_scales, offs, offs2, w1,
+    w2_words, w2_scales, w3_words, w3_scales, w4, gs, gc, out,
+):
+    nc = tc.nc
+    with ExitStack() as ctx:
+        keep = ctx.enter_context(tc.tile_pool(name="keep", bufs=1))
+        work = ctx.enter_context(tc.tile_pool(name="work", bufs=3))
+        ring = ctx.enter_context(tc.tile_pool(name="ring", bufs=2))
+        psum_d = ctx.enter_context(tc.psum_pool(name="psum_d", bufs=6))
+        psum_y = ctx.enter_context(tc.psum_pool(name="psum_y", bufs=1))
+
+        def kept(shape, dtype, name):
+            return keep.tile(shape, dtype, name=name, align_bytes=64)
+
+        list8 = keep.tile([P, S // 16], U16, name="list8")
+        list1 = keep.tile([P, S // 16], U16, name="list1")
+        tab_sc = kept([P, T], U8, "tab_sc")
+        tab2_sc = kept([P, T], U8, "tab2_sc")
+        w2_sc_raw = kept([P, H], U8, "w2_sc_raw")
+        w3_sc = kept([P, BLOCKS, N], U8, "w3_sc")
+        tab_w = [kept([P, T], I32, "tab_w%d" % a) for a in range(PASSES)]
+        tab2_w = kept([P, T], I32, "tab2_w")
+        w1_raw = [[ring.tile([P, PACK, K_PASS], F32, name="w1_raw%d%d" % (b, a), tag="raw") for a in range(PASSES)]
+                  for b in range(BLOCKS)]
+        w2_raw = kept([P, 2 * H], U8, "w2_raw")
+        w3_w = kept([P, BLOCKS, 2 * N], U8, "w3_w")
+        w4_raw = ring.tile([P, BLOCKS, PACK, N], F32, name="w4_raw", tag="raw")
+        gs_t = kept([P, BLOCKS, PACK], F32, "gs_t")
+        gc_t = kept([P, BLOCKS, PACK], F32, "gc_t")
+        warm = kept([P, 2], F32, "warm")
+
+        nc.vector.memset(tab_sc[:].bitcast(I32), 0)
+        nc.vector.memset(warm[:, 0:1], 0.0)
+        nc.vector.memset(tab2_sc[:].bitcast(I32), 0)
+        nc.vector.memset(w2_sc_raw[:].bitcast(I32), 0)
+        nc.gpsimd.memset(w3_sc[:].rearrange("p b n -> p (b n)").bitcast(I32), 0)
+        nc.scalar.activation(out=warm[:, 1:2], in_=warm[:, 0:1], func=ACT.Sin)
+
+        def load_w1(b, a):
+            rows = w1[a * K_PASS : (a + 1) * K_PASS, b * K_PASS : (b + 1) * K_PASS]
+            nc.sync.dma_start(out=w1_raw[b][a][:], in_=rows.rearrange("(p i) c -> p i c", i=PACK))
+
+        def load_words(tile, words):
+            nc.sync.dma_start(out=tile[:], in_=words.rearrange("p t i -> p (t i)").bitcast(I32))
+
+        nc.sync.dma_start(list8[:], offs)
+        for a in range(PASSES):
+            rows = tab_scales[a].rearrange("(g e) t -> e g t", e=2)
+            for e in range(2):
+                nc.scalar.dma_start(out=tab_sc[4 * a + e : P : 16, :].bitcast(I32), in_=rows[e].bitcast(I32))
+        load_words(tab_w[0], tab_words[0])
+        nc.sync.dma_start(list1[:], offs2)
+        load_w1(0, 0)
+        for q in range(4):
+            nc.scalar.dma_start(out=tab2_sc[32 * q : 32 * q + 4, :].bitcast(I32),
+                                in_=tab2_scales[0, 4 * q : 4 * q + 4, :].bitcast(I32))
+        load_words(tab_w[1], tab_words[1])
+        nc.sync.dma_start(out=w2_raw[:].bitcast(I32), in_=w2_words[0].bitcast(I32))
+        for q in range(4):
+            nc.scalar.dma_start(out=w2_sc_raw[32 * q : 32 * q + 4, :].bitcast(I32),
+                                in_=w2_scales[0, 4 * q : 4 * q + 4, :].bitcast(I32))
+        load_w1(0, 1)
+        load_words(tab2_w, tab2_words[0])
+        nc.gpsimd.dma_start(out=gs_t[:], in_=gs.rearrange("(b p t) -> p b t", p=P, t=PACK))
+        nc.gpsimd.dma_start(out=gc_t[:], in_=gc.rearrange("(b p t) -> p b t", p=P, t=PACK))
+        nc.gpsimd.dma_start(out=w3_w[:].bitcast(I32), in_=w3_words.rearrange("b p c -> p b c").bitcast(I32))
+        for q in range(4):
+            nc.gpsimd.dma_start(out=w3_sc[32 * q : 32 * q + 4, :, :].bitcast(I32),
+                              in_=w3_scales[:, 4 * q : 4 * q + 4, :].rearrange("b r n -> r b n").bitcast(I32))
+
+        v_sc_picked = kept([P, S], U8, "v_sc_picked")
+        v_sc = kept([P, S], U8, "v_sc")
+        nc.vector.tensor_copy(out=v_sc_picked[:], in_=tab_sc[:].indirect(list8[:]))
+        nc.vector.tensor_copy(out=v_sc[:].bitcast(I32), in_=v_sc_picked[:].bitcast(I32))
+        for a in range(PASSES):
+            for e in range(2):
+                nc.scalar.dma_start(out=v_sc[4 * a + 2 + e : P : 32, :].bitcast(I32),
+                                    in_=v_sc_picked[16 + 4 * a + e : P : 32, :].bitcast(I32))
+
+        def pick(name, dtype, window, offsets, u):
+            dst = kept([P, UNIT], dtype, "%s_%d" % (name, u))
+            cols = slice(u * UNIT // 16, (u + 1) * UNIT // 16)
+            nc.vector.tensor_copy(out=dst[:], in_=window.indirect(offsets[:, cols]))
+            return dst
+
+        v_w = [[None] * UNITS for a in range(PASSES)]
+        v2_w = [None] * UNITS
+        v2_sc = [None] * UNITS
+
+        def pick_tab(a, u):
+            v_w[a][u] = pick("v_w%d" % a, U32, tab_w[a][:].bitcast(U32), list8, u)
+
+        def pick_tab2_scales(u):
+            v2_sc[u] = pick("v2_sc", U8, tab2_sc[:], list1, u)
+
+        def pick_tab2(u):
+            v2_w[u] = pick("v2_w", U32, tab2_w[:].bitcast(U32), list1, u)
+
+        w1_codes = [[kept([P, K_PASS], U32, "w1_codes%d%d" % (b, a)) for a in range(PASSES)] for b in range(BLOCKS)]
+        w1_sc = [[kept([P, K_PASS], U8, "w1_sc%d%d" % (b, a)) for a in range(PASSES)] for b in range(BLOCKS)]
+        w1_bf = [[kept([P, PACK * K_PASS], BF16, "w1_bf%d%d" % (b, a)) for a in range(PASSES)] for b in range(BLOCKS)]
+
+        def round_w1(b, a):
+            dst = w1_bf[b][a][:].rearrange("p (t m i) -> p m i t", t=PACK, i=PACK)
+            src = w1_raw[b][a][:].rearrange("p i (m t) -> p m i t", t=PACK)
+            if (b, a) != (1, 0):
+                nc.scalar.activation(out=dst, in_=src, func=ACT.Copy, scale=-1.0)
+            else:
+                nc.vector.tensor_scalar(out=dst, in0=src, scalar1=-1.0, scalar2=None, op0=ALU.mult)
+
+        def quantize_w1(b, a):
+            nc.vector.quantize_mx(out=w1_codes[b][a][:].bitcast(FP8X4), scales=w1_sc[b][a][:], in_=w1_bf[b][a][:])
+
+        w2_w = kept([P, 2 * H], U8, "w2_w")
+        w2_sc = kept([P, H], U8, "w2_sc")
+
+        pick_tab(0, 0)
+        pick_tab2_scales(0)
+        pick_tab(0, 1)
+        pick_tab2_scales(1)
+        round_w1(0, 0)
+        load_w1(1, 0)
+        quantize_w1(0, 0)
+        pick_tab(1, 0)
+        pick_tab(1, 1)
+        nc.vector.tensor_copy(out=w2_w[:].bitcast(U16).rearrange("p (b t m) -> p b m t", b=BLOCKS, t=PACK),
+                              in_=w2_raw[:].bitcast(U16).rearrange("p (b m t) -> p b m t", b=BLOCKS, t=PACK))
+        nc.vector.tensor_copy(out=w2_sc[:].rearrange("p (b t m) -> p b m t", b=BLOCKS, t=PACK),
+                              in_=w2_sc_raw[:].rearrange("p (b m t) -> p b m t", b=BLOCKS, t=PACK))
+        round_w1(0, 1)
+        load_w1(1, 1)
+        quantize_w1(0, 1)
+        pick_tab2(0)
+        pick_tab2(1)
+        gc_m2 = kept([P, BLOCKS, PACK], F32, "gc_m2")
+        nc.vector.tensor_scalar(out=gc_m2[:], in0=gc_t[:], scalar1=-2.0, scalar2=None, op0=ALU.mult)
+
+        w4_bf = kept([P, BLOCKS * N * PACK], BF16, "w4_bf")
+        w4_codes = kept([P, BLOCKS, N], U32, "w4_codes")
+        w4_sc = kept([P, BLOCKS, N], U8, "w4_sc")
+
+        def angles(b, j0, width, square_on_vector):
+            u = j0 // UNIT
+            sin_d = work.tile([P, width * PACK], F32, name="sin_d")
+            sin_h = work.tile([P, width * PACK], F32, name="sin_h")
+            for jj in range(width // JB):
+                j = j0 + jj * JB
+                c = slice(j % UNIT, j % UNIT + JB)
+                bank = psum_d.tile([P, PACK, JB], F32, name="bank")
+                for a in range(PASSES):
+                    for t in range(PACK):
+                        m = slice(t * P, (t + 1) * P)
+                        nc.tensor.matmul_mx(
+                            out=bank[:, t, :],
+                            lhsT=w1_codes[b][a][:, m].bitcast(FP8X4), lhsT_scale=w1_sc[b][a][:, m],
+                            rhs=v_w[a][u][:, c].bitcast(FP8X4),
+                            rhs_scale=v_sc[4 * a : P, j : j + JB],
+                            start=(a == 0 and t == 0), stop=False)
+                for t in range(PACK):
+                    r0 = b * K_PASS + t * P
+                    nc.tensor.matmul_mx(
+                        out=bank[:, t, :],
+                        lhsT=w2_w[:, 2 * r0 : 2 * (r0 + P)].bitcast(FP4X4), lhsT_scale=w2_sc[:, r0 : r0 + P],
+                        rhs=v2_w[u][:, c].bitcast(FP8X4), rhs_scale=v2_sc[u][:, c],
+                        start=False, stop=(t == PACK - 1))
+                cols = slice(jj * JB * PACK, (jj + 1) * JB * PACK)
+                minus_d = bank[:].rearrange("p t j -> p j t")
+                nc.scalar.activation(out=sin_h[:, cols].rearrange("p (j t) -> p j t", t=PACK), in_=minus_d,
+                                     func=ACT.Sin, scale=0.5)
+                nc.scalar.activation(out=sin_d[:, cols].rearrange("p (j t) -> p j t", t=PACK), in_=minus_d,
+                                     func=ACT.Sin, scale=-1.0)
+            sq = work.tile([P, width * PACK], F32, name="sq")
+            if square_on_vector:
+                nc.vector.tensor_tensor(out=sq[:], in0=sin_h[:], in1=sin_h[:], op=ALU.mult)
+            else:
+                nc.scalar.activation(out=sq[:], in_=sin_h[:], func=ACT.Square)
+            return sin_d, sq
+
+        def gains(b, width, sin_d, sq):
+            z = work.tile([P, 2, width * PACK], BF16, name="z", align_bytes=64)
+            nc.vector.tensor_tensor(
+                out=z[:, 0, :].rearrange("p (j t) -> p j t", t=PACK),
+                in0=sin_d[:].rearrange("p (j t) -> p j t", t=PACK),
+                in1=gs_t[:, b : b + 1, :].to_broadcast([P, width, PACK]), op=ALU.mult)
+            nc.vector.scalar_tensor_tensor(
+                out=z[:, 1, :].rearrange("p (j t) -> p j t", t=PACK),
+                in0=sq[:].rearrange("p (j t) -> p j t", t=PACK), scalar=0.5,
+                in1=gc_m2[:, b : b + 1, :].to_broadcast([P, width, PACK]), op0=ALU.subtract, op1=ALU.mult)
+            return z
+
+        z_codes, z_sc = {}, {}
+
+        def quantize_z(b, j0, width, z):
+            codes = kept([P, 2, width], U32, "z_codes%d_%d" % (b, j0))
+            scales = kept([P, 2, width], U8, "z_sc%d_%d" % (b, j0))
+            nc.vector.quantize_mx(out=codes[:].rearrange("p s j -> p (s j)").bitcast(FP8X4),
+                                  scales=scales[:].rearrange("p s j -> p (s j)"),
+                                  in_=z[:].rearrange("p s c -> p (s c)"))
+            for jj in range(width // JB):
+                c = slice(jj * JB, (jj + 1) * JB)
+                z_codes[b, j0 + jj * JB] = [codes[:, s, c] for s in range(2)]
+                z_sc[b, j0 + jj * JB] = [scales[:, s, c] for s in range(2)]
+
+        def second_stage(j0, width):
+            ys = psum_y.tile([P, N // P, width], F32, name="ys")
+            yc = psum_y.tile([P, N // P, width], F32, name="yc")
+            for n in range(N // P):
+                for jj in range(width // JB):
+                    j = j0 + jj * JB
+                    for b in range(BLOCKS):
+                        nc.tensor.matmul_mx(
+                            out=ys[:, n, jj * JB : (jj + 1) * JB],
+                            lhsT=w3_w[:, b, 2 * n * P : 2 * (n + 1) * P].bitcast(FP4X4),
+                            lhsT_scale=w3_sc[:, b, n * P : (n + 1) * P],
+                            rhs=z_codes[b, j][0].bitcast(FP8X4), rhs_scale=z_sc[b, j][0],
+                            start=(b == 0), stop=(b == BLOCKS - 1))
+            for n in range(N // P):
+                for jj in range(width // JB):
+                    j = j0 + jj * JB
+                    for b in range(BLOCKS):
+                        nc.tensor.matmul_mx(
+                            out=yc[:, n, jj * JB : (jj + 1) * JB],
+                            lhsT=w4_codes[:, b, n * P : (n + 1) * P].bitcast(FP8X4),
+                            lhsT_scale=w4_sc[:, b, n * P : (n + 1) * P],
+                            rhs=z_codes[b, j][1].bitcast(FP8X4), rhs_scale=z_sc[b, j][1],
+                            start=(b == 0), stop=(b == BLOCKS - 1))
+            ys_sb = work.tile([P, N // P, width], F32, name="ys_sb")
+            nc.scalar.copy(out=ys_sb[:], in_=ys[:])
+            res = work.tile([P, N // P, width], F32, name="res")
+            nc.vector.tensor_tensor(out=res[:], in0=yc[:], in1=ys_sb[:], op=ALU.mult)
+            nc.sync.dma_start(out=out[:, j0 : j0 + width].rearrange("(n p) j -> p n j", p=P), in_=res[:])
+
+        def side_work(step):
+            if step == 0:
+                for a in range(PASSES):
+                    round_w1(1, a)
+                nc.sync.dma_start(out=w4_raw[:], in_=w4.rearrange("(b p i) n -> p b i n", p=P, i=PACK))
+            if step == 1:
+                for a in range(PASSES):
+                    quantize_w1(1, a)
+                for b in range(BLOCKS):
+                    nc.vector.tensor_copy(
+                        out=w4_bf[:, b * N * PACK : (b + 1) * N * PACK].rearrange("p (c e i) -> p c i e", e=4, i=PACK),
+                        in_=w4_raw[:, b, :, :].rearrange("p i (c e) -> p c i e", e=4))
+            if step == 2:
+                nc.vector.quantize_mx(out=w4_codes[:].rearrange("p b n -> p (b n)").bitcast(FP8X4),
+                                      scales=w4_sc[:].rearrange("p b n -> p (b n)"), in_=w4_bf[:])
+            if step in (0, 1):
+                pick_tab(0, step + 2)
+                pick_tab(1, step + 2)
+                pick_tab2_scales(step + 2)
+                pick_tab2(step + 2)
+
+        steps = [(0, 0, 256), (0, 256, 256), (1, 0, 256), (1, 256, 256),
+                 (0, 512, 256), (1, 512, 256), (0, 768, 256), (1, 768, 128), (1, 896, 128)]
+        pending = None
+        for step, (b, j0, width) in enumerate(steps):
+            sin_d, sq = angles(b, j0, width, step == len(steps) - 1)
+            side_work(step)
+            z = gains(b, width, sin_d, sq)
+            if pending is not None:
+                quantize_z(*pending)
+                if pending[0] == BLOCKS - 1:
+                    second_stage(pending[1], pending[2])
+            pending = (b, j0, width, z)
+        quantize_z(*pending)
+        second_stage(pending[1], pending[2])

@@ -34,7 +34,6 @@ def tile_list_islanding_separation_kernel(
     with ExitStack() as ctx:
         keep = ctx.enter_context(tc.tile_pool(name="keep", bufs=1))
         work = ctx.enter_context(tc.tile_pool(name="work", bufs=3))
-        ring = ctx.enter_context(tc.tile_pool(name="ring", bufs=2))
         psum_d = ctx.enter_context(tc.psum_pool(name="psum_d", bufs=6))
         psum_y = ctx.enter_context(tc.psum_pool(name="psum_y", bufs=1))
 
@@ -46,84 +45,89 @@ def tile_list_islanding_separation_kernel(
         tab_sc = kept([P, T], U8, "tab_sc")
         tab2_sc = kept([P, T], U8, "tab2_sc")
         w2_sc_raw = kept([P, H], U8, "w2_sc_raw")
-        w3_sc = kept([P, BLOCKS, N], U8, "w3_sc")
+        planes = kept([P, 2 * S + H + BLOCKS * N], U8, "planes")
+        spread = kept([P, 2 * S + H + BLOCKS * N], U8, "spread")
+        v2_sc = planes[:, S : 2 * S]
+        w2_sc = planes[:, 2 * S : 2 * S + H]
+        w3_sc0 = 2 * S + H
         tab_w = [kept([P, T], I32, "tab_w%d" % a) for a in range(PASSES)]
         tab2_w = kept([P, T], I32, "tab2_w")
-        w1_raw = [[ring.tile([P, PACK, K_PASS], F32, name="w1_raw%d%d" % (b, a), tag="raw") for a in range(PASSES)]
-                  for b in range(BLOCKS)]
+        w1_raw = [[kept([P, PACK, K_PASS], F32, "w1_raw0%d" % a)[:] for a in range(PASSES)]]
         w2_raw = kept([P, 2 * H], U8, "w2_raw")
-        w3_w = kept([P, BLOCKS, 2 * N], U8, "w3_w")
-        w4_raw = ring.tile([P, BLOCKS, PACK, N], F32, name="w4_raw", tag="raw")
         gs_t = kept([P, BLOCKS, PACK], F32, "gs_t")
         gc_t = kept([P, BLOCKS, PACK], F32, "gc_t")
         warm = kept([P, 2], F32, "warm")
 
         nc.vector.memset(tab_sc[:].bitcast(I32), 0)
-        nc.vector.memset(warm[:, 0:1], 0.0)
-        nc.vector.memset(tab2_sc[:].bitcast(I32), 0)
+        nc.gpsimd.memset(tab2_sc[:].bitcast(I32), 0)
         nc.vector.memset(w2_sc_raw[:].bitcast(I32), 0)
-        nc.gpsimd.memset(w3_sc[:].rearrange("p b n -> p (b n)").bitcast(I32), 0)
-        nc.scalar.activation(out=warm[:, 1:2], in_=warm[:, 0:1], func=ACT.Sin)
+        nc.gpsimd.memset(planes[:].bitcast(I32), 0)
+        nc.vector.memset(warm[:, 0:1], 0.0)
 
-        def load_w1(b, a):
+        def load_w1(b, a, pieces=1):
             rows = w1[a * K_PASS : (a + 1) * K_PASS, b * K_PASS : (b + 1) * K_PASS]
-            nc.sync.dma_start(out=w1_raw[b][a][:], in_=rows.rearrange("(p i) c -> p i c", i=PACK))
+            rows = rows.rearrange("(p i) c -> p i c", i=PACK)
+            step = PACK // pieces
+            for i in range(0, PACK, step):
+                nc.sync.dma_start(out=w1_raw[b][a][:, i : i + step, :], in_=rows[:, i : i + step, :])
 
-        def load_words(tile, words):
-            nc.sync.dma_start(out=tile[:], in_=words.rearrange("p t i -> p (t i)").bitcast(I32))
+        def load_words(tile, words, pieces):
+            words = words.rearrange("p t i -> p (t i)").bitcast(I32)
+            for c0 in range(0, T, T // pieces):
+                cols = slice(c0, c0 + T // pieces)
+                nc.sync.dma_start(out=tile[:, cols], in_=words[:, cols])
 
+        nc.sync.dma_start(out=tab_sc[0:P:4, :].bitcast(I32), in_=tab_scales.rearrange("a q t -> q a t").bitcast(I32))
+        nc.sync.dma_start(out=tab2_sc[0:P:8, :].bitcast(I32), in_=tab2_scales[0].bitcast(I32))
+        nc.sync.dma_start(out=w2_sc_raw[0:P:8, :].bitcast(I32), in_=w2_scales[0].bitcast(I32))
         nc.sync.dma_start(list8[:], offs)
-        for a in range(PASSES):
-            rows = tab_scales[a].rearrange("(g e) t -> e g t", e=2)
-            for e in range(2):
-                nc.scalar.dma_start(out=tab_sc[4 * a + e : P : 16, :].bitcast(I32), in_=rows[e].bitcast(I32))
-        load_words(tab_w[0], tab_words[0])
         nc.sync.dma_start(list1[:], offs2)
-        load_w1(0, 0)
-        for q in range(4):
-            nc.scalar.dma_start(out=tab2_sc[32 * q : 32 * q + 4, :].bitcast(I32),
-                                in_=tab2_scales[0, 4 * q : 4 * q + 4, :].bitcast(I32))
-        load_words(tab_w[1], tab_words[1])
-        nc.sync.dma_start(out=w2_raw[:].bitcast(I32), in_=w2_words[0].bitcast(I32))
-        for q in range(4):
-            nc.scalar.dma_start(out=w2_sc_raw[32 * q : 32 * q + 4, :].bitcast(I32),
-                                in_=w2_scales[0, 4 * q : 4 * q + 4, :].bitcast(I32))
+        load_words(tab_w[0], tab_words[0], 8)
+        nc.sync.dma_start(out=spread[0:P:8, w3_sc0:].bitcast(I32).rearrange("q (b n) -> q b n", b=BLOCKS),
+                          in_=w3_scales.rearrange("b q n -> q b n").bitcast(I32))
+        for b in range(BLOCKS):
+            cols = slice(b * H, (b + 1) * H)
+            nc.sync.dma_start(out=w2_raw[:, cols].bitcast(I32), in_=w2_words[0][:, cols].bitcast(I32))
+        load_w1(0, 0, 4)
         load_w1(0, 1)
-        load_words(tab2_w, tab2_words[0])
-        nc.gpsimd.dma_start(out=gs_t[:], in_=gs.rearrange("(b p t) -> p b t", p=P, t=PACK))
-        nc.gpsimd.dma_start(out=gc_t[:], in_=gc.rearrange("(b p t) -> p b t", p=P, t=PACK))
-        nc.gpsimd.dma_start(out=w3_w[:].bitcast(I32), in_=w3_words.rearrange("b p c -> p b c").bitcast(I32))
-        for q in range(4):
-            nc.gpsimd.dma_start(out=w3_sc[32 * q : 32 * q + 4, :, :].bitcast(I32),
-                              in_=w3_scales[:, 4 * q : 4 * q + 4, :].rearrange("b r n -> r b n").bitcast(I32))
+        load_words(tab_w[1], tab_words[1], 1)
+        load_words(tab2_w, tab2_words[0], 1)
+        nc.scalar.dma_start(out=gs_t[:], in_=gs.rearrange("(b p t) -> p b t", p=P, t=PACK))
+        nc.scalar.dma_start(out=gc_t[:], in_=gc.rearrange("(b p t) -> p b t", p=P, t=PACK))
 
+        nc.scalar.activation(out=warm[:, 1:2], in_=warm[:, 0:1], func=ACT.Sin)
         v_sc_picked = kept([P, S], U8, "v_sc_picked")
-        v_sc = kept([P, S], U8, "v_sc")
-        nc.vector.tensor_copy(out=v_sc_picked[:], in_=tab_sc[:].indirect(list8[:]))
-        nc.vector.tensor_copy(out=v_sc[:].bitcast(I32), in_=v_sc_picked[:].bitcast(I32))
-        for a in range(PASSES):
-            for e in range(2):
-                nc.scalar.dma_start(out=v_sc[4 * a + 2 + e : P : 32, :].bitcast(I32),
-                                    in_=v_sc_picked[16 + 4 * a + e : P : 32, :].bitcast(I32))
+        v2_sc_picked = kept([P, S], U8, "v2_sc_picked")
+        v0_w = kept([P, S], U32, "v0_w")
+        v1_w = [kept([P, S // 2], U32, "v1_first")]
+        v2_w = kept([P, S], U32, "v2_w")
 
-        def pick(name, dtype, window, offsets, u):
-            dst = kept([P, UNIT], dtype, "%s_%d" % (name, u))
-            cols = slice(u * UNIT // 16, (u + 1) * UNIT // 16)
-            nc.vector.tensor_copy(out=dst[:], in_=window.indirect(offsets[:, cols]))
-            return dst
+        def pick(dst, window, offsets, j0, j1):
+            nc.vector.tensor_copy(out=dst, in_=window.indirect(offsets[:, j0 // 16 : j1 // 16]))
 
-        v_w = [[None] * UNITS for a in range(PASSES)]
-        v2_w = [None] * UNITS
-        v2_sc = [None] * UNITS
+        def v_cols(a, j0, j1):
+            if a == 0:
+                return v0_w[:, j0:j1]
+            h, c0 = divmod(j0, S // 2)
+            return v1_w[h][:, c0 : c0 + j1 - j0]
 
-        def pick_tab(a, u):
-            v_w[a][u] = pick("v_w%d" % a, U32, tab_w[a][:].bitcast(U32), list8, u)
+        def pick_tab(a, j0, j1):
+            pick(v_cols(a, j0, j1), tab_w[a][:].bitcast(U32), list8, j0, j1)
 
-        def pick_tab2_scales(u):
-            v2_sc[u] = pick("v2_sc", U8, tab2_sc[:], list1, u)
+        def pick_tab2(j0, j1):
+            pick(v2_w[:, j0:j1], tab2_w[:].bitcast(U32), list1, j0, j1)
 
-        def pick_tab2(u):
-            v2_w[u] = pick("v2_w", U32, tab2_w[:].bitcast(U32), list1, u)
+        pick(v_sc_picked[:], tab_sc[:], list8, 0, S)
+        for q in range(0, P, 32):
+            nc.gpsimd.dma_start(out=planes[q + 4 : q + 8, 0:S].bitcast(I32),
+                                in_=v_sc_picked[q + 4 : q + 32 : 8, :].bitcast(I32))
+        pick(v2_sc_picked[:], tab2_sc[:], list1, 0, S)
+        nc.vector.tensor_copy(out=spread[:, 0:S].bitcast(I32), in_=v_sc_picked[:].bitcast(I32))
+        nc.vector.tensor_copy(out=spread[:, 2 * S : 2 * S + H].rearrange("p (b t m) -> p b m t", b=BLOCKS, t=PACK),
+                              in_=w2_sc_raw[:].rearrange("p (b m t) -> p b m t", b=BLOCKS, t=PACK))
+        nc.vector.tensor_copy(out=spread[:, S : 2 * S].bitcast(I32), in_=v2_sc_picked[:].bitcast(I32))
+        for q in range(0, P, 32):
+            nc.sync.dma_start(out=planes[q : q + 4, :].bitcast(I32), in_=spread[q : q + 32 : 8, :].bitcast(I32))
 
         w1_codes = [[kept([P, K_PASS], U32, "w1_codes%d%d" % (b, a)) for a in range(PASSES)] for b in range(BLOCKS)]
         w1_sc = [[kept([P, K_PASS], U8, "w1_sc%d%d" % (b, a)) for a in range(PASSES)] for b in range(BLOCKS)]
@@ -131,7 +135,7 @@ def tile_list_islanding_separation_kernel(
 
         def round_w1(b, a):
             dst = w1_bf[b][a][:].rearrange("p (t m i) -> p m i t", t=PACK, i=PACK)
-            src = w1_raw[b][a][:].rearrange("p i (m t) -> p m i t", t=PACK)
+            src = w1_raw[b][a].rearrange("p i (m t) -> p m i t", t=PACK)
             if (b, a) != (1, 0):
                 nc.scalar.activation(out=dst, in_=src, func=ACT.Copy, scale=-1.0)
             else:
@@ -141,26 +145,22 @@ def tile_list_islanding_separation_kernel(
             nc.vector.quantize_mx(out=w1_codes[b][a][:].bitcast(FP8X4), scales=w1_sc[b][a][:], in_=w1_bf[b][a][:])
 
         w2_w = kept([P, 2 * H], U8, "w2_w")
-        w2_sc = kept([P, H], U8, "w2_sc")
 
-        pick_tab(0, 0)
-        pick_tab2_scales(0)
-        pick_tab(0, 1)
-        pick_tab2_scales(1)
+        pick_tab(0, 0, S)
         round_w1(0, 0)
-        load_w1(1, 0)
         quantize_w1(0, 0)
-        pick_tab(1, 0)
-        pick_tab(1, 1)
+        pick_tab(1, 0, S // 2)
         nc.vector.tensor_copy(out=w2_w[:].bitcast(U16).rearrange("p (b t m) -> p b m t", b=BLOCKS, t=PACK),
                               in_=w2_raw[:].bitcast(U16).rearrange("p (b m t) -> p b m t", b=BLOCKS, t=PACK))
-        nc.vector.tensor_copy(out=w2_sc[:].rearrange("p (b t m) -> p b m t", b=BLOCKS, t=PACK),
-                              in_=w2_sc_raw[:].rearrange("p (b m t) -> p b m t", b=BLOCKS, t=PACK))
         round_w1(0, 1)
-        load_w1(1, 1)
         quantize_w1(0, 1)
-        pick_tab2(0)
-        pick_tab2(1)
+        w1_late = keep.tile([P, PASSES * PACK * K_PASS], F32, name="w1_late", tag="w1_bf01", align_bytes=64)
+        w1_raw.append([w1_late[:, a * PACK * K_PASS : (a + 1) * PACK * K_PASS].rearrange("p (i c) -> p i c", i=PACK)
+                       for a in range(PASSES)])
+        load_w1(1, 0)
+        load_w1(1, 1)
+        pick_tab2(0, UNIT)
+        pick_tab2(UNIT, 2 * UNIT)
         gc_m2 = kept([P, BLOCKS, PACK], F32, "gc_m2")
         nc.vector.tensor_scalar(out=gc_m2[:], in0=gc_t[:], scalar1=-2.0, scalar2=None, op0=ALU.mult)
 
@@ -169,12 +169,11 @@ def tile_list_islanding_separation_kernel(
         w4_sc = kept([P, BLOCKS, N], U8, "w4_sc")
 
         def angles(b, j0, width, square_on_vector):
-            u = j0 // UNIT
             sin_d = work.tile([P, width * PACK], F32, name="sin_d")
             sin_h = work.tile([P, width * PACK], F32, name="sin_h")
             for jj in range(width // JB):
                 j = j0 + jj * JB
-                c = slice(j % UNIT, j % UNIT + JB)
+                c = slice(j, j + JB)
                 bank = psum_d.tile([P, PACK, JB], F32, name="bank")
                 for a in range(PASSES):
                     for t in range(PACK):
@@ -182,15 +181,15 @@ def tile_list_islanding_separation_kernel(
                         nc.tensor.matmul_mx(
                             out=bank[:, t, :],
                             lhsT=w1_codes[b][a][:, m].bitcast(FP8X4), lhsT_scale=w1_sc[b][a][:, m],
-                            rhs=v_w[a][u][:, c].bitcast(FP8X4),
-                            rhs_scale=v_sc[4 * a : P, j : j + JB],
+                            rhs=v_cols(a, j, j + JB).bitcast(FP8X4),
+                            rhs_scale=planes[4 * a : P, c],
                             start=(a == 0 and t == 0), stop=False)
                 for t in range(PACK):
                     r0 = b * K_PASS + t * P
                     nc.tensor.matmul_mx(
                         out=bank[:, t, :],
                         lhsT=w2_w[:, 2 * r0 : 2 * (r0 + P)].bitcast(FP4X4), lhsT_scale=w2_sc[:, r0 : r0 + P],
-                        rhs=v2_w[u][:, c].bitcast(FP8X4), rhs_scale=v2_sc[u][:, c],
+                        rhs=v2_w[:, c].bitcast(FP8X4), rhs_scale=v2_sc[:, c],
                         start=False, stop=(t == PACK - 1))
                 cols = slice(jj * JB * PACK, (jj + 1) * JB * PACK)
                 minus_d = bank[:].rearrange("p t j -> p j t")
@@ -217,7 +216,7 @@ def tile_list_islanding_separation_kernel(
                 in1=gc_m2[:, b : b + 1, :].to_broadcast([P, width, PACK]), op0=ALU.subtract, op1=ALU.mult)
             return z
 
-        z_codes, z_sc = {}, {}
+        z_codes, z_sc, late = {}, {}, {}
 
         def quantize_z(b, j0, width, z):
             codes = kept([P, 2, width], U32, "z_codes%d_%d" % (b, j0))
@@ -239,8 +238,8 @@ def tile_list_islanding_separation_kernel(
                     for b in range(BLOCKS):
                         nc.tensor.matmul_mx(
                             out=ys[:, n, jj * JB : (jj + 1) * JB],
-                            lhsT=w3_w[:, b, 2 * n * P : 2 * (n + 1) * P].bitcast(FP4X4),
-                            lhsT_scale=w3_sc[:, b, n * P : (n + 1) * P],
+                            lhsT=late["w3"][:, b, 2 * n * P : 2 * (n + 1) * P].bitcast(FP4X4),
+                            lhsT_scale=planes[:, w3_sc0 + b * N + n * P : w3_sc0 + b * N + (n + 1) * P],
                             rhs=z_codes[b, j][0].bitcast(FP8X4), rhs_scale=z_sc[b, j][0],
                             start=(b == 0), stop=(b == BLOCKS - 1))
             for n in range(N // P):
@@ -260,28 +259,31 @@ def tile_list_islanding_separation_kernel(
             nc.sync.dma_start(out=out[:, j0 : j0 + width].rearrange("(n p) j -> p n j", p=P), in_=res[:])
 
         def side_work(step):
-            if step == 0:
-                for a in range(PASSES):
-                    round_w1(1, a)
-                nc.sync.dma_start(out=w4_raw[:], in_=w4.rearrange("(b p i) n -> p b i n", p=P, i=PACK))
-            if step == 1:
-                for a in range(PASSES):
-                    quantize_w1(1, a)
+            if step in (1, 2):
+                round_w1(1, step - 1)
+            if step in (2, 3):
+                quantize_w1(1, step - 2)
+            if step == 3:
                 for b in range(BLOCKS):
                     nc.vector.tensor_copy(
                         out=w4_bf[:, b * N * PACK : (b + 1) * N * PACK].rearrange("p (c e i) -> p c i e", e=4, i=PACK),
-                        in_=w4_raw[:, b, :, :].rearrange("p i (c e) -> p c i e", e=4))
-            if step == 2:
+                        in_=late["w4"][:, b, :, :].rearrange("p i (c e) -> p c i e", e=4))
+            if step == 4:
                 nc.vector.quantize_mx(out=w4_codes[:].rearrange("p b n -> p (b n)").bitcast(FP8X4),
                                       scales=w4_sc[:].rearrange("p b n -> p (b n)"), in_=w4_bf[:])
-            if step in (0, 1):
-                pick_tab(0, step + 2)
-                pick_tab(1, step + 2)
-                pick_tab2_scales(step + 2)
-                pick_tab2(step + 2)
+            if step == 0:
+                v1_w.append(keep.tile([P, S // 2], U32, name="v1_second", tag="w1_raw01", align_bytes=64))
+                pick_tab(1, S // 2, S)
+                pick_tab2(S // 2, S)
+                late["w4"] = keep.tile([P, BLOCKS, PACK, N], F32, name="w4_raw", tag="tab_w1", align_bytes=64)
+                late["w3"] = keep.tile([P, BLOCKS, 2 * N], U8, name="w3_w", tag="tab2_w", align_bytes=64)
+                nc.sync.dma_start(out=late["w3"][:].bitcast(I32),
+                                  in_=w3_words.rearrange("b p c -> p b c").bitcast(I32))
+                nc.sync.dma_start(out=late["w4"][:], in_=w4.rearrange("(b p i) n -> p b i n", p=P, i=PACK))
 
-        steps = [(0, 0, 256), (0, 256, 256), (1, 0, 256), (1, 256, 256),
-                 (0, 512, 256), (1, 512, 256), (0, 768, 256), (1, 768, 128), (1, 896, 128)]
+
+        steps = [(0, 0, 256), (0, 256, 256), (0, 512, 256), (0, 768, 256),
+                 (1, 0, 256), (1, 256, 256), (1, 512, 256), (1, 768, 128), (1, 896, 128)]
         pending = None
         for step, (b, j0, width) in enumerate(steps):
             sin_d, sq = angles(b, j0, width, step == len(steps) - 1)

@@ -1,6 +1,7 @@
 from contextlib import ExitStack
 
 import concourse.mybir as mybir
+from concourse.masks import make_identity
 
 K, K2, T, S, H, N = 1024, 512, 2048, 1024, 1024, 256
 FLOPS = 2 * S * (K * H + K2 * H + 2 * H * N)
@@ -34,7 +35,7 @@ def tile_list_islanding_separation_kernel(
     with ExitStack() as ctx:
         keep = ctx.enter_context(tc.tile_pool(name="keep", bufs=1))
         work = ctx.enter_context(tc.tile_pool(name="work", bufs=3))
-        psum_d = ctx.enter_context(tc.psum_pool(name="psum_d", bufs=6))
+        psum_d = ctx.enter_context(tc.psum_pool(name="psum_d", bufs=5))
         psum_y = ctx.enter_context(tc.psum_pool(name="psum_y", bufs=1))
 
         def kept(shape, dtype, name):
@@ -54,15 +55,18 @@ def tile_list_islanding_separation_kernel(
         tab2_w = kept([P, T], I32, "tab2_w")
         w1_raw = [[kept([P, PACK, K_PASS], F32, "w1_raw0%d" % a)[:] for a in range(PASSES)]]
         w2_raw = kept([P, 2 * H], U8, "w2_raw")
-        gs_t = kept([P, BLOCKS, PACK], F32, "gs_t")
-        gc_t = kept([P, BLOCKS, PACK], F32, "gc_t")
+        gain_rows = kept([P, K_PASS], F32, "gain_rows")
+        identity = kept([P, P], F32, "identity")
+        gain = psum_y.tile([P, PACK, P], F32, name="gain")
         warm = kept([P, 2], F32, "warm")
 
         nc.vector.memset(tab_sc[:].bitcast(I32), 0)
         nc.gpsimd.memset(tab2_sc[:].bitcast(I32), 0)
         nc.vector.memset(w2_sc_raw[:].bitcast(I32), 0)
-        nc.gpsimd.memset(planes[:].bitcast(I32), 0)
+        nc.vector.memset(planes[:].bitcast(I32), 0)
         nc.vector.memset(warm[:, 0:1], 0.0)
+        nc.gpsimd.memset(gain_rows[:], 0.0)
+        make_identity(nc, identity[:])
 
         def load_w1(b, a, pieces=1):
             rows = w1[a * K_PASS : (a + 1) * K_PASS, b * K_PASS : (b + 1) * K_PASS]
@@ -92,24 +96,25 @@ def tile_list_islanding_separation_kernel(
         load_w1(0, 1)
         load_words(tab_w[1], tab_words[1], 1)
         load_words(tab2_w, tab2_words[0], 1)
-        nc.scalar.dma_start(out=gs_t[:], in_=gs.rearrange("(b p t) -> p b t", p=P, t=PACK))
-        nc.scalar.dma_start(out=gc_t[:], in_=gc.rearrange("(b p t) -> p b t", p=P, t=PACK))
+        nc.scalar.dma_start(out=gain_rows[0:BLOCKS, :], in_=gs.rearrange("(b c) -> b c", b=BLOCKS))
+        nc.scalar.dma_start(out=gain_rows[32 : 32 + BLOCKS, :], in_=gc.rearrange("(b c) -> b c", b=BLOCKS))
+        nc.gpsimd.tensor_scalar(out=gain_rows[32:64, :], in0=gain_rows[32:64, :], scalar1=-2.0, scalar2=0.0,
+                                op0=ALU.mult, op1=ALU.add)
+        for t in range(PACK):
+            nc.tensor.transpose(gain[:, t, :], gain_rows[:, t:K_PASS:PACK], identity[:])
 
         nc.scalar.activation(out=warm[:, 1:2], in_=warm[:, 0:1], func=ACT.Sin)
         v_sc_picked = kept([P, S], U8, "v_sc_picked")
         v2_sc_picked = kept([P, S], U8, "v2_sc_picked")
-        v0_w = kept([P, S], U32, "v0_w")
-        v1_w = [kept([P, S // 2], U32, "v1_first")]
+        v_w = [kept([P, PASSES * S // 2], U32, "v_first")]
         v2_w = kept([P, S], U32, "v2_w")
 
         def pick(dst, window, offsets, j0, j1):
             nc.vector.tensor_copy(out=dst, in_=window.indirect(offsets[:, j0 // 16 : j1 // 16]))
 
         def v_cols(a, j0, j1):
-            if a == 0:
-                return v0_w[:, j0:j1]
             h, c0 = divmod(j0, S // 2)
-            return v1_w[h][:, c0 : c0 + j1 - j0]
+            return v_w[h][:, a * S // 2 + c0 : a * S // 2 + c0 + j1 - j0]
 
         def pick_tab(a, j0, j1):
             pick(v_cols(a, j0, j1), tab_w[a][:].bitcast(U32), list8, j0, j1)
@@ -120,7 +125,7 @@ def tile_list_islanding_separation_kernel(
         pick(v_sc_picked[:], tab_sc[:], list8, 0, S)
         for q in range(0, P, 32):
             nc.gpsimd.dma_start(out=planes[q + 4 : q + 8, 0:S].bitcast(I32),
-                                in_=v_sc_picked[q + 4 : q + 32 : 8, :].bitcast(I32))
+                              in_=v_sc_picked[q + 4 : q + 32 : 8, :].bitcast(I32))
         pick(v2_sc_picked[:], tab2_sc[:], list1, 0, S)
         nc.vector.tensor_copy(out=spread[:, 0:S].bitcast(I32), in_=v_sc_picked[:].bitcast(I32))
         nc.vector.tensor_copy(out=spread[:, 2 * S : 2 * S + H].rearrange("p (b t m) -> p b m t", b=BLOCKS, t=PACK),
@@ -136,7 +141,7 @@ def tile_list_islanding_separation_kernel(
         def round_w1(b, a):
             dst = w1_bf[b][a][:].rearrange("p (t m i) -> p m i t", t=PACK, i=PACK)
             src = w1_raw[b][a].rearrange("p i (m t) -> p m i t", t=PACK)
-            if (b, a) != (1, 0):
+            if b == 0:
                 nc.scalar.activation(out=dst, in_=src, func=ACT.Copy, scale=-1.0)
             else:
                 nc.vector.tensor_scalar(out=dst, in0=src, scalar1=-1.0, scalar2=None, op0=ALU.mult)
@@ -146,7 +151,7 @@ def tile_list_islanding_separation_kernel(
 
         w2_w = kept([P, 2 * H], U8, "w2_w")
 
-        pick_tab(0, 0, S)
+        pick_tab(0, 0, S // 2)
         round_w1(0, 0)
         quantize_w1(0, 0)
         pick_tab(1, 0, S // 2)
@@ -161,16 +166,15 @@ def tile_list_islanding_separation_kernel(
         load_w1(1, 1)
         pick_tab2(0, UNIT)
         pick_tab2(UNIT, 2 * UNIT)
-        gc_m2 = kept([P, BLOCKS, PACK], F32, "gc_m2")
-        nc.vector.tensor_scalar(out=gc_m2[:], in0=gc_t[:], scalar1=-2.0, scalar2=None, op0=ALU.mult)
 
         w4_bf = kept([P, BLOCKS * N * PACK], BF16, "w4_bf")
         w4_codes = kept([P, BLOCKS, N], U32, "w4_codes")
         w4_sc = kept([P, BLOCKS, N], U8, "w4_sc")
 
-        def angles(b, j0, width, square_on_vector):
+        def angles(b, j0, width, last):
             sin_d = work.tile([P, width * PACK], F32, name="sin_d")
             sin_h = work.tile([P, width * PACK], F32, name="sin_h")
+            sq = work.tile([P, width * PACK], F32, name="sq")
             for jj in range(width // JB):
                 j = j0 + jj * JB
                 c = slice(j, j + JB)
@@ -195,12 +199,11 @@ def tile_list_islanding_separation_kernel(
                 minus_d = bank[:].rearrange("p t j -> p j t")
                 nc.scalar.activation(out=sin_h[:, cols].rearrange("p (j t) -> p j t", t=PACK), in_=minus_d,
                                      func=ACT.Sin, scale=0.5)
+                if not last:
+                    nc.gpsimd.tensor_tensor(out=sq[:, cols], in0=sin_h[:, cols], in1=sin_h[:, cols], op=ALU.mult)
                 nc.scalar.activation(out=sin_d[:, cols].rearrange("p (j t) -> p j t", t=PACK), in_=minus_d,
                                      func=ACT.Sin, scale=-1.0)
-            sq = work.tile([P, width * PACK], F32, name="sq")
-            if square_on_vector:
-                nc.vector.tensor_tensor(out=sq[:], in0=sin_h[:], in1=sin_h[:], op=ALU.mult)
-            else:
+            if last:
                 nc.scalar.activation(out=sq[:], in_=sin_h[:], func=ACT.Square)
             return sin_d, sq
 
@@ -209,11 +212,11 @@ def tile_list_islanding_separation_kernel(
             nc.vector.tensor_tensor(
                 out=z[:, 0, :].rearrange("p (j t) -> p j t", t=PACK),
                 in0=sin_d[:].rearrange("p (j t) -> p j t", t=PACK),
-                in1=gs_t[:, b : b + 1, :].to_broadcast([P, width, PACK]), op=ALU.mult)
+                in1=gain[:, :, b : b + 1].rearrange("p t o -> p o t").to_broadcast([P, width, PACK]), op=ALU.mult)
             nc.vector.scalar_tensor_tensor(
                 out=z[:, 1, :].rearrange("p (j t) -> p j t", t=PACK),
                 in0=sq[:].rearrange("p (j t) -> p j t", t=PACK), scalar=0.5,
-                in1=gc_m2[:, b : b + 1, :].to_broadcast([P, width, PACK]), op0=ALU.subtract, op1=ALU.mult)
+                in1=gain[:, :, 32 + b : 33 + b].rearrange("p t o -> p o t").to_broadcast([P, width, PACK]), op0=ALU.subtract, op1=ALU.mult)
             return z
 
         z_codes, z_sc, late = {}, {}, {}
@@ -264,15 +267,16 @@ def tile_list_islanding_separation_kernel(
             if step in (2, 3):
                 quantize_w1(1, step - 2)
             if step == 3:
-                for b in range(BLOCKS):
-                    nc.vector.tensor_copy(
+                for b, copy in enumerate((nc.vector.tensor_copy, nc.scalar.copy)):
+                    copy(
                         out=w4_bf[:, b * N * PACK : (b + 1) * N * PACK].rearrange("p (c e i) -> p c i e", e=4, i=PACK),
                         in_=late["w4"][:, b, :, :].rearrange("p i (c e) -> p c i e", e=4))
             if step == 4:
                 nc.vector.quantize_mx(out=w4_codes[:].rearrange("p b n -> p (b n)").bitcast(FP8X4),
                                       scales=w4_sc[:].rearrange("p b n -> p (b n)"), in_=w4_bf[:])
             if step == 0:
-                v1_w.append(keep.tile([P, S // 2], U32, name="v1_second", tag="w1_raw01", align_bytes=64))
+                v_w.append(keep.tile([P, PASSES * S // 2], U32, name="v_second", tag="spread", align_bytes=64))
+                pick_tab(0, S // 2, S)
                 pick_tab(1, S // 2, S)
                 pick_tab2(S // 2, S)
                 late["w4"] = keep.tile([P, BLOCKS, PACK, N], F32, name="w4_raw", tag="tab_w1", align_bytes=64)
@@ -286,7 +290,7 @@ def tile_list_islanding_separation_kernel(
                  (1, 0, 256), (1, 256, 256), (1, 512, 256), (1, 768, 128), (1, 896, 128)]
         pending = None
         for step, (b, j0, width) in enumerate(steps):
-            sin_d, sq = angles(b, j0, width, step == len(steps) - 1)
+            sin_d, sq = angles(b, j0, width, True)
             side_work(step)
             z = gains(b, width, sin_d, sq)
             if pending is not None:

@@ -1,7 +1,6 @@
 from contextlib import ExitStack
 
 import concourse.mybir as mybir
-from concourse.masks import make_identity
 
 K, K2, T, S, H, N = 1024, 512, 2048, 1024, 1024, 256
 FLOPS = 2 * S * (K * H + K2 * H + 2 * H * N)
@@ -23,8 +22,11 @@ K_PASS = P * PACK
 PASSES = K // K_PASS
 BLOCKS = H // K_PASS
 JB = 128
-UNIT = 256
-UNITS = S // UNIT
+ROWS = 16
+QUAD = 32
+V_SC, V2_SC, W2_SC, W3_SC = 0, S, 2 * S, 2 * S + K_PASS
+STAGED = W3_SC + N
+FIRST = 256
 
 
 def tile_list_islanding_separation_kernel(
@@ -34,146 +36,123 @@ def tile_list_islanding_separation_kernel(
     nc = tc.nc
     with ExitStack() as ctx:
         keep = ctx.enter_context(tc.tile_pool(name="keep", bufs=1))
-        work = ctx.enter_context(tc.tile_pool(name="work", bufs=3))
-        psum_d = ctx.enter_context(tc.psum_pool(name="psum_d", bufs=5))
-        psum_y = ctx.enter_context(tc.psum_pool(name="psum_y", bufs=1))
+        work = ctx.enter_context(tc.tile_pool(name="work", bufs=5))
+        psum_d = ctx.enter_context(tc.psum_pool(name="psum_d", bufs=4))
+        psum_y = ctx.enter_context(tc.psum_pool(name="psum_y", bufs=2))
 
-        def kept(shape, dtype, name):
-            return keep.tile(shape, dtype, name=name, align_bytes=64)
+        def kept(shape, dtype, name, tag=None):
+            return keep.tile(shape, dtype, name=name, tag=tag or name, align_bytes=64)
 
         list8 = keep.tile([P, S // 16], U16, name="list8")
         list1 = keep.tile([P, S // 16], U16, name="list1")
         tab_sc = kept([P, T], U8, "tab_sc")
         tab2_sc = kept([P, T], U8, "tab2_sc")
-        w2_sc_raw = kept([P, H], U8, "w2_sc_raw")
-        planes = kept([P, 2 * S + H + BLOCKS * N], U8, "planes")
-        spread = kept([P, 2 * S + H + BLOCKS * N], U8, "spread")
-        v2_sc = planes[:, S : 2 * S]
-        w2_sc = planes[:, 2 * S : 2 * S + H]
-        w3_sc0 = 2 * S + H
+        w2_sc_raw = kept([P, K_PASS], U8, "w2_sc_raw")
+        staged = kept([P, STAGED], U8, "staged")
+        planes = kept([P, 2, STAGED], U8, "planes")
         tab_w = [kept([P, T], I32, "tab_w%d" % a) for a in range(PASSES)]
-        tab2_w = kept([P, T], I32, "tab2_w")
-        w1_raw = [[kept([P, PACK, K_PASS], F32, "w1_raw0%d" % a)[:] for a in range(PASSES)]]
+        w1_raw = {(0, a): kept([P, PACK, K_PASS], F32, "w1_raw0%d" % a)[:] for a in range(PASSES)}
         w2_raw = kept([P, 2 * H], U8, "w2_raw")
-        gain_rows = kept([P, K_PASS], F32, "gain_rows")
-        identity = kept([P, P], F32, "identity")
-        gain = psum_y.tile([P, PACK, P], F32, name="gain")
-        warm = kept([P, 2], F32, "warm")
+        gain_s = kept([P, BLOCKS, PACK], F32, "gain_s")
+        gc_raw = kept([P, BLOCKS, PACK], F32, "gc_raw")
+        gain_c = kept([P, BLOCKS, PACK], F32, "gain_c")
 
-        nc.vector.memset(tab_sc[:].bitcast(I32), 0)
-        nc.gpsimd.memset(tab2_sc[:].bitcast(I32), 0)
-        nc.vector.memset(w2_sc_raw[:].bitcast(I32), 0)
-        nc.vector.memset(planes[:].bitcast(I32), 0)
-        nc.vector.memset(warm[:, 0:1], 0.0)
-        nc.gpsimd.memset(gain_rows[:], 0.0)
-        make_identity(nc, identity[:])
+        nc.gpsimd.memset(tab_sc[:].bitcast(I32), 0)
+        nc.gpsimd.memset(planes[:].rearrange("p a c -> p (a c)").bitcast(I32), 0)
 
-        def load_w1(b, a, pieces=1):
+        def load_w1(b, a, i0=0, i1=PACK):
             rows = w1[a * K_PASS : (a + 1) * K_PASS, b * K_PASS : (b + 1) * K_PASS]
             rows = rows.rearrange("(p i) c -> p i c", i=PACK)
-            step = PACK // pieces
-            for i in range(0, PACK, step):
-                nc.sync.dma_start(out=w1_raw[b][a][:, i : i + step, :], in_=rows[:, i : i + step, :])
+            nc.sync.dma_start(out=w1_raw[b, a][:, i0:i1, :], in_=rows[:, i0:i1, :])
 
-        def load_words(tile, words, pieces):
-            words = words.rearrange("p t i -> p (t i)").bitcast(I32)
-            for c0 in range(0, T, T // pieces):
-                cols = slice(c0, c0 + T // pieces)
-                nc.sync.dma_start(out=tile[:, cols], in_=words[:, cols])
+        def load_words(tile, words):
+            nc.sync.dma_start(out=tile[:], in_=words.rearrange("p t i -> p (t i)").bitcast(I32))
 
-        nc.sync.dma_start(out=tab_sc[0:P:4, :].bitcast(I32), in_=tab_scales.rearrange("a q t -> q a t").bitcast(I32))
-        nc.sync.dma_start(out=tab2_sc[0:P:8, :].bitcast(I32), in_=tab2_scales[0].bitcast(I32))
-        nc.sync.dma_start(out=w2_sc_raw[0:P:8, :].bitcast(I32), in_=w2_scales[0].bitcast(I32))
-        nc.sync.dma_start(list8[:], offs)
         nc.sync.dma_start(list1[:], offs2)
-        load_words(tab_w[0], tab_words[0], 8)
-        nc.sync.dma_start(out=spread[0:P:8, w3_sc0:].bitcast(I32).rearrange("q (b n) -> q b n", b=BLOCKS),
+        nc.sync.dma_start(out=tab2_sc[:].bitcast(I32),
+                          in_=tab2_scales[0].bitcast(I32).unsqueeze(1).to_broadcast([ROWS, P // ROWS, T // 4]))
+        nc.sync.dma_start(list8[:], offs)
+        w2_halves = w2_scales[0].rearrange("q (b c) -> (q b) c", b=BLOCKS).bitcast(I32)
+        nc.sync.dma_start(out=w2_sc_raw[:].bitcast(I32),
+                          in_=w2_halves.unsqueeze(1).to_broadcast([ROWS * BLOCKS, 4, K_PASS // 4]))
+        nc.sync.dma_start(out=staged[0:P:4, W3_SC:].bitcast(I32),
                           in_=w3_scales.rearrange("b q n -> q b n").bitcast(I32))
-        for b in range(BLOCKS):
-            cols = slice(b * H, (b + 1) * H)
-            nc.sync.dma_start(out=w2_raw[:, cols].bitcast(I32), in_=w2_words[0][:, cols].bitcast(I32))
-        load_w1(0, 0, 4)
+        for i in range(PACK - 1):
+            load_w1(0, 0, i, i + 1)
+        nc.sync.dma_start(out=tab_sc[0:P:4, :].bitcast(I32), in_=tab_scales.rearrange("a q t -> q a t").bitcast(I32))
+        load_w1(0, 0, PACK - 1, PACK)
+        nc.sync.dma_start(out=w2_raw[:].bitcast(I32), in_=w2_words[0].bitcast(I32))
+        load_words(tab_w[0], tab_words[0])
         load_w1(0, 1)
-        load_words(tab_w[1], tab_words[1], 1)
-        load_words(tab2_w, tab2_words[0], 1)
-        nc.scalar.dma_start(out=gain_rows[0:BLOCKS, :], in_=gs.rearrange("(b c) -> b c", b=BLOCKS))
-        nc.scalar.dma_start(out=gain_rows[32 : 32 + BLOCKS, :], in_=gc.rearrange("(b c) -> b c", b=BLOCKS))
-        nc.gpsimd.tensor_scalar(out=gain_rows[32:64, :], in0=gain_rows[32:64, :], scalar1=-2.0, scalar2=0.0,
-                                op0=ALU.mult, op1=ALU.add)
-        for t in range(PACK):
-            nc.tensor.transpose(gain[:, t, :], gain_rows[:, t:K_PASS:PACK], identity[:])
-
-        nc.scalar.activation(out=warm[:, 1:2], in_=warm[:, 0:1], func=ACT.Sin)
-        v_sc_picked = kept([P, S], U8, "v_sc_picked")
-        v2_sc_picked = kept([P, S], U8, "v2_sc_picked")
-        v_w = [kept([P, PASSES * S // 2], U32, "v_first")]
-        v2_w = kept([P, S], U32, "v2_w")
+        load_words(tab_w[1], tab_words[1])
+        nc.gpsimd.dma_start(out=gain_s[:], in_=gs.rearrange("(b p t) -> p b t", p=P, t=PACK))
+        nc.gpsimd.dma_start(out=gc_raw[:], in_=gc.rearrange("(b p t) -> p b t", p=P, t=PACK))
+        nc.gpsimd.tensor_scalar(out=gain_c[:], in0=gc_raw[:], scalar1=-2.0, scalar2=0.0, op0=ALU.mult, op1=ALU.add)
 
         def pick(dst, window, offsets, j0, j1):
             nc.vector.tensor_copy(out=dst, in_=window.indirect(offsets[:, j0 // 16 : j1 // 16]))
 
-        def v_cols(a, j0, j1):
-            h, c0 = divmod(j0, S // 2)
-            return v_w[h][:, a * S // 2 + c0 : a * S // 2 + c0 + j1 - j0]
-
-        def pick_tab(a, j0, j1):
-            pick(v_cols(a, j0, j1), tab_w[a][:].bitcast(U32), list8, j0, j1)
-
-        def pick_tab2(j0, j1):
-            pick(v2_w[:, j0:j1], tab2_w[:].bitcast(U32), list1, j0, j1)
-
-        pick(v_sc_picked[:], tab_sc[:], list8, 0, S)
-        for q in range(0, P, 32):
-            nc.gpsimd.dma_start(out=planes[q + 4 : q + 8, 0:S].bitcast(I32),
-                              in_=v_sc_picked[q + 4 : q + 32 : 8, :].bitcast(I32))
+        v_sc_picked = kept([P, S], U8, "v_sc_picked")
+        v2_sc_picked = kept([P, S], U8, "v2_sc_picked")
         pick(v2_sc_picked[:], tab2_sc[:], list1, 0, S)
-        nc.vector.tensor_copy(out=spread[:, 0:S].bitcast(I32), in_=v_sc_picked[:].bitcast(I32))
-        nc.vector.tensor_copy(out=spread[:, 2 * S : 2 * S + H].rearrange("p (b t m) -> p b m t", b=BLOCKS, t=PACK),
-                              in_=w2_sc_raw[:].rearrange("p (b m t) -> p b m t", b=BLOCKS, t=PACK))
-        nc.vector.tensor_copy(out=spread[:, S : 2 * S].bitcast(I32), in_=v2_sc_picked[:].bitcast(I32))
-        for q in range(0, P, 32):
-            nc.sync.dma_start(out=planes[q : q + 4, :].bitcast(I32), in_=spread[q : q + 32 : 8, :].bitcast(I32))
+        nc.vector.tensor_copy(out=staged[:, V2_SC : V2_SC + S].bitcast(I32), in_=v2_sc_picked[:].bitcast(I32))
+        nc.vector.tensor_copy(out=staged[:, W2_SC : W2_SC + K_PASS].rearrange("p (t m) -> p m t", t=PACK),
+                              in_=w2_sc_raw[:].rearrange("p (m t) -> p m t", t=PACK))
+        pick(v_sc_picked[:], tab_sc[:], list8, 0, S)
+        nc.vector.tensor_copy(out=staged[:, V_SC : V_SC + S].bitcast(I32), in_=v_sc_picked[:].bitcast(I32))
+        for q in range(0, P, QUAD):
+            nc.scalar.dma_start(out=planes[q : q + 4, :, :].bitcast(I32), in_=staged[q : q + QUAD : 4, :].bitcast(I32))
 
-        w1_codes = [[kept([P, K_PASS], U32, "w1_codes%d%d" % (b, a)) for a in range(PASSES)] for b in range(BLOCKS)]
-        w1_sc = [[kept([P, K_PASS], U8, "w1_sc%d%d" % (b, a)) for a in range(PASSES)] for b in range(BLOCKS)]
-        w1_bf = [[kept([P, PACK * K_PASS], BF16, "w1_bf%d%d" % (b, a)) for a in range(PASSES)] for b in range(BLOCKS)]
+        w1_codes = {(b, a): kept([P, K_PASS], U32, "w1_codes%d%d" % (b, a)) for a in range(PASSES) for b in range(BLOCKS)}
+        w1_sc = {(b, a): kept([P, K_PASS], U8, "w1_sc%d%d" % (b, a)) for a in range(PASSES) for b in range(BLOCKS)}
+        w1_bf = {(0, a): kept([P, PACK * K_PASS], BF16, "w1_bf0%d" % a)[:] for a in range(PASSES)}
 
         def round_w1(b, a):
-            dst = w1_bf[b][a][:].rearrange("p (t m i) -> p m i t", t=PACK, i=PACK)
-            src = w1_raw[b][a].rearrange("p i (m t) -> p m i t", t=PACK)
+            dst = w1_bf[b, a].rearrange("p (t m i) -> p m i t", t=PACK, i=PACK)
+            src = w1_raw[b, a].rearrange("p i (m t) -> p m i t", t=PACK)
             if b == 0:
                 nc.scalar.activation(out=dst, in_=src, func=ACT.Copy, scale=-1.0)
             else:
                 nc.vector.tensor_scalar(out=dst, in0=src, scalar1=-1.0, scalar2=None, op0=ALU.mult)
 
         def quantize_w1(b, a):
-            nc.vector.quantize_mx(out=w1_codes[b][a][:].bitcast(FP8X4), scales=w1_sc[b][a][:], in_=w1_bf[b][a][:])
+            nc.vector.quantize_mx(out=w1_codes[b, a][:].bitcast(FP8X4), scales=w1_sc[b, a][:], in_=w1_bf[b, a])
 
         w2_w = kept([P, 2 * H], U8, "w2_w")
-
-        pick_tab(0, 0, S // 2)
-        round_w1(0, 0)
-        quantize_w1(0, 0)
-        pick_tab(1, 0, S // 2)
         nc.vector.tensor_copy(out=w2_w[:].bitcast(U16).rearrange("p (b t m) -> p b m t", b=BLOCKS, t=PACK),
                               in_=w2_raw[:].bitcast(U16).rearrange("p (b m t) -> p b m t", b=BLOCKS, t=PACK))
+        tab2_w = kept([P, T], I32, "tab2_w", tag="w2_raw")
+        load_words(tab2_w, tab2_words[0])
+        v_w = [kept([P, S], U32, "v_w0")]
+        pick(v_w[0][:], tab_w[0][:].bitcast(U32), list8, 0, S)
+        round_w1(0, 0)
+        quantize_w1(0, 0)
+        v_w.append(kept([P, S], U32, "v_w1", tag="w1_bf00"))
+        pick(v_w[1][:], tab_w[1][:].bitcast(U32), list8, 0, S)
         round_w1(0, 1)
         quantize_w1(0, 1)
-        w1_late = keep.tile([P, PASSES * PACK * K_PASS], F32, name="w1_late", tag="w1_bf01", align_bytes=64)
-        w1_raw.append([w1_late[:, a * PACK * K_PASS : (a + 1) * PACK * K_PASS].rearrange("p (i c) -> p i c", i=PACK)
-                       for a in range(PASSES)])
-        load_w1(1, 0)
-        load_w1(1, 1)
-        pick_tab2(0, UNIT)
-        pick_tab2(UNIT, 2 * UNIT)
+        v2_w = kept([P, S], U32, "v2_w", tag="w1_bf01")
+        pick(v2_w[:, 0:FIRST], tab2_w[:].bitcast(U32), list1, 0, FIRST)
+        pick(v2_w[:, FIRST:S], tab2_w[:].bitcast(U32), list1, FIRST, S)
+
+        w1_late = kept([P, PASSES * PACK * K_PASS], F32, "w1_late", tag="tab_w0")
+        w1_bf_late = kept([P, PASSES * PACK * K_PASS], BF16, "w1_bf_late", tag="w2_raw")
+        for a in range(PASSES):
+            w1_bf[1, a] = w1_bf_late[:, a * PACK * K_PASS : (a + 1) * PACK * K_PASS]
+            w1_raw[1, a] = w1_late[:, a * PACK * K_PASS : (a + 1) * PACK * K_PASS].rearrange("p (i c) -> p i c", i=PACK)
+            load_w1(1, a)
+        w4_raw = kept([P, BLOCKS, PACK, N], F32, "w4_raw", tag="w1_raw01")
+        nc.sync.dma_start(out=w4_raw[:], in_=w4.rearrange("(b p i) n -> p b i n", p=P, i=PACK))
+        w3_w = kept([P, BLOCKS, 2 * N], U8, "w3_w", tag="staged")
+        nc.sync.dma_start(out=w3_w[:].bitcast(I32), in_=w3_words.rearrange("b p c -> p b c").bitcast(I32))
 
         w4_bf = kept([P, BLOCKS * N * PACK], BF16, "w4_bf")
         w4_codes = kept([P, BLOCKS, N], U32, "w4_codes")
         w4_sc = kept([P, BLOCKS, N], U8, "w4_sc")
 
-        def angles(b, j0, width, last):
+        def angles(b, j0, width):
             sin_d = work.tile([P, width * PACK], F32, name="sin_d")
-            sin_h = work.tile([P, width * PACK], F32, name="sin_h")
+            sin_h = work.tile([P, width * PACK], F32, name="sin_h", bufs=2)
             sq = work.tile([P, width * PACK], F32, name="sq")
             for jj in range(width // JB):
                 j = j0 + jj * JB
@@ -184,42 +163,39 @@ def tile_list_islanding_separation_kernel(
                         m = slice(t * P, (t + 1) * P)
                         nc.tensor.matmul_mx(
                             out=bank[:, t, :],
-                            lhsT=w1_codes[b][a][:, m].bitcast(FP8X4), lhsT_scale=w1_sc[b][a][:, m],
-                            rhs=v_cols(a, j, j + JB).bitcast(FP8X4),
-                            rhs_scale=planes[4 * a : P, c],
+                            lhsT=w1_codes[b, a][:, m].bitcast(FP8X4), lhsT_scale=w1_sc[b, a][:, m],
+                            rhs=v_w[a][:, c].bitcast(FP8X4), rhs_scale=planes[:, a, V_SC + j : V_SC + j + JB],
                             start=(a == 0 and t == 0), stop=False)
                 for t in range(PACK):
                     r0 = b * K_PASS + t * P
                     nc.tensor.matmul_mx(
                         out=bank[:, t, :],
-                        lhsT=w2_w[:, 2 * r0 : 2 * (r0 + P)].bitcast(FP4X4), lhsT_scale=w2_sc[:, r0 : r0 + P],
-                        rhs=v2_w[:, c].bitcast(FP8X4), rhs_scale=v2_sc[:, c],
+                        lhsT=w2_w[:, 2 * r0 : 2 * (r0 + P)].bitcast(FP4X4),
+                        lhsT_scale=planes[:, b, W2_SC + t * P : W2_SC + (t + 1) * P],
+                        rhs=v2_w[:, c].bitcast(FP8X4), rhs_scale=planes[:, 0, V2_SC + j : V2_SC + j + JB],
                         start=False, stop=(t == PACK - 1))
                 cols = slice(jj * JB * PACK, (jj + 1) * JB * PACK)
                 minus_d = bank[:].rearrange("p t j -> p j t")
                 nc.scalar.activation(out=sin_h[:, cols].rearrange("p (j t) -> p j t", t=PACK), in_=minus_d,
                                      func=ACT.Sin, scale=0.5)
-                if not last:
-                    nc.gpsimd.tensor_tensor(out=sq[:, cols], in0=sin_h[:, cols], in1=sin_h[:, cols], op=ALU.mult)
                 nc.scalar.activation(out=sin_d[:, cols].rearrange("p (j t) -> p j t", t=PACK), in_=minus_d,
                                      func=ACT.Sin, scale=-1.0)
-            if last:
-                nc.scalar.activation(out=sq[:], in_=sin_h[:], func=ACT.Square)
+            nc.scalar.activation(out=sq[:], in_=sin_h[:], func=ACT.Square)
             return sin_d, sq
 
         def gains(b, width, sin_d, sq):
-            z = work.tile([P, 2, width * PACK], BF16, name="z", align_bytes=64)
+            z = work.tile([P, 2, width * PACK], BF16, name="z", align_bytes=64, bufs=3)
             nc.vector.tensor_tensor(
                 out=z[:, 0, :].rearrange("p (j t) -> p j t", t=PACK),
                 in0=sin_d[:].rearrange("p (j t) -> p j t", t=PACK),
-                in1=gain[:, :, b : b + 1].rearrange("p t o -> p o t").to_broadcast([P, width, PACK]), op=ALU.mult)
+                in1=gain_s[:, b : b + 1, :].to_broadcast([P, width, PACK]), op=ALU.mult)
             nc.vector.scalar_tensor_tensor(
                 out=z[:, 1, :].rearrange("p (j t) -> p j t", t=PACK),
                 in0=sq[:].rearrange("p (j t) -> p j t", t=PACK), scalar=0.5,
-                in1=gain[:, :, 32 + b : 33 + b].rearrange("p t o -> p o t").to_broadcast([P, width, PACK]), op0=ALU.subtract, op1=ALU.mult)
+                in1=gain_c[:, b : b + 1, :].to_broadcast([P, width, PACK]), op0=ALU.subtract, op1=ALU.mult)
             return z
 
-        z_codes, z_sc, late = {}, {}, {}
+        z_codes, z_sc = {}, {}
 
         def quantize_z(b, j0, width, z):
             codes = kept([P, 2, width], U32, "z_codes%d_%d" % (b, j0))
@@ -241,8 +217,8 @@ def tile_list_islanding_separation_kernel(
                     for b in range(BLOCKS):
                         nc.tensor.matmul_mx(
                             out=ys[:, n, jj * JB : (jj + 1) * JB],
-                            lhsT=late["w3"][:, b, 2 * n * P : 2 * (n + 1) * P].bitcast(FP4X4),
-                            lhsT_scale=planes[:, w3_sc0 + b * N + n * P : w3_sc0 + b * N + (n + 1) * P],
+                            lhsT=w3_w[:, b, 2 * n * P : 2 * (n + 1) * P].bitcast(FP4X4),
+                            lhsT_scale=planes[:, b, W3_SC + n * P : W3_SC + (n + 1) * P],
                             rhs=z_codes[b, j][0].bitcast(FP8X4), rhs_scale=z_sc[b, j][0],
                             start=(b == 0), stop=(b == BLOCKS - 1))
             for n in range(N // P):
@@ -255,42 +231,29 @@ def tile_list_islanding_separation_kernel(
                             lhsT_scale=w4_sc[:, b, n * P : (n + 1) * P],
                             rhs=z_codes[b, j][1].bitcast(FP8X4), rhs_scale=z_sc[b, j][1],
                             start=(b == 0), stop=(b == BLOCKS - 1))
-            ys_sb = work.tile([P, N // P, width], F32, name="ys_sb")
+            ys_sb = work.tile([P, N // P, width], F32, name="ys_sb", bufs=2)
             nc.scalar.copy(out=ys_sb[:], in_=ys[:])
-            res = work.tile([P, N // P, width], F32, name="res")
+            res = work.tile([P, N // P, width], F32, name="res", bufs=3)
             nc.vector.tensor_tensor(out=res[:], in0=yc[:], in1=ys_sb[:], op=ALU.mult)
             nc.sync.dma_start(out=out[:, j0 : j0 + width].rearrange("(n p) j -> p n j", p=P), in_=res[:])
 
         def side_work(step):
-            if step in (1, 2):
-                round_w1(1, step - 1)
-            if step in (2, 3):
-                quantize_w1(1, step - 2)
+            if step in (0, 2):
+                round_w1(1, step // 2)
+            if step in (1, 3):
+                quantize_w1(1, step // 2)
             if step == 3:
-                for b, copy in enumerate((nc.vector.tensor_copy, nc.scalar.copy)):
-                    copy(
-                        out=w4_bf[:, b * N * PACK : (b + 1) * N * PACK].rearrange("p (c e i) -> p c i e", e=4, i=PACK),
-                        in_=late["w4"][:, b, :, :].rearrange("p i (c e) -> p c i e", e=4))
+                nc.scalar.copy(out=w4_bf[:].rearrange("p (b c e i) -> p b c i e", b=BLOCKS, e=4, i=PACK),
+                               in_=w4_raw[:].rearrange("p b i (c e) -> p b c i e", e=4))
             if step == 4:
                 nc.vector.quantize_mx(out=w4_codes[:].rearrange("p b n -> p (b n)").bitcast(FP8X4),
                                       scales=w4_sc[:].rearrange("p b n -> p (b n)"), in_=w4_bf[:])
-            if step == 0:
-                v_w.append(keep.tile([P, PASSES * S // 2], U32, name="v_second", tag="spread", align_bytes=64))
-                pick_tab(0, S // 2, S)
-                pick_tab(1, S // 2, S)
-                pick_tab2(S // 2, S)
-                late["w4"] = keep.tile([P, BLOCKS, PACK, N], F32, name="w4_raw", tag="tab_w1", align_bytes=64)
-                late["w3"] = keep.tile([P, BLOCKS, 2 * N], U8, name="w3_w", tag="tab2_w", align_bytes=64)
-                nc.sync.dma_start(out=late["w3"][:].bitcast(I32),
-                                  in_=w3_words.rearrange("b p c -> p b c").bitcast(I32))
-                nc.sync.dma_start(out=late["w4"][:], in_=w4.rearrange("(b p i) n -> p b i n", p=P, i=PACK))
 
-
-        steps = [(0, 0, 256), (0, 256, 256), (0, 512, 256), (0, 768, 256),
+        steps = [(0, 0, 128), (0, 128, 128), (0, 256, 256), (0, 512, 256), (0, 768, 256),
                  (1, 0, 256), (1, 256, 256), (1, 512, 256), (1, 768, 128), (1, 896, 128)]
         pending = None
         for step, (b, j0, width) in enumerate(steps):
-            sin_d, sq = angles(b, j0, width, True)
+            sin_d, sq = angles(b, j0, width)
             side_work(step)
             z = gains(b, width, sin_d, sq)
             if pending is not None:

@@ -1,6 +1,7 @@
 from contextlib import ExitStack
 
 import concourse.mybir as mybir
+from concourse.masks import make_identity
 
 K, K2, T, S, H, N = 1024, 512, 2048, 1024, 1024, 256
 FLOPS = 2 * S * (K * H + K2 * H + 2 * H * N)
@@ -37,7 +38,7 @@ def tile_list_islanding_separation_kernel(
     with ExitStack() as ctx:
         keep = ctx.enter_context(tc.tile_pool(name="keep", bufs=1))
         work = ctx.enter_context(tc.tile_pool(name="work", bufs=5))
-        psum_d = ctx.enter_context(tc.psum_pool(name="psum_d", bufs=4))
+        psum_d = ctx.enter_context(tc.psum_pool(name="psum_d", bufs=3))
         psum_y = ctx.enter_context(tc.psum_pool(name="psum_y", bufs=2))
 
         def kept(shape, dtype, name, tag=None):
@@ -53,10 +54,15 @@ def tile_list_islanding_separation_kernel(
         tab_w = [kept([P, T], I32, "tab_w%d" % a) for a in range(PASSES)]
         w1_raw = {(0, a): kept([P, PACK, K_PASS], F32, "w1_raw0%d" % a)[:] for a in range(PASSES)}
         w2_raw = kept([P, 2 * H], U8, "w2_raw")
-        gain_s = kept([P, BLOCKS, PACK], F32, "gain_s")
-        gc_raw = kept([P, BLOCKS, PACK], F32, "gc_raw")
-        gain_c = kept([P, BLOCKS, PACK], F32, "gain_c")
+        gain_in = kept([P, P], F32, "gain_in")
+        gain_turned = kept([P, P], F32, "gain_turned")
+        gc_raw = kept([P, BLOCKS * PACK], F32, "gc_raw")
+        gs_raw = kept([P, BLOCKS * PACK], F32, "gs_raw")
+        identity = kept([P, P], F32, "identity")
 
+        warm = kept([P, 2], F32, "warm")
+        nc.vector.memset(warm[:, 0:1], 0.0)
+        nc.scalar.activation(out=warm[:, 1:2], in_=warm[:, 0:1], func=ACT.Sin)
         nc.gpsimd.memset(tab_sc[:].bitcast(I32), 0)
         nc.gpsimd.memset(planes[:].rearrange("p a c -> p (a c)").bitcast(I32), 0)
 
@@ -77,17 +83,29 @@ def tile_list_islanding_separation_kernel(
                           in_=w2_halves.unsqueeze(1).to_broadcast([ROWS * BLOCKS, 4, K_PASS // 4]))
         nc.sync.dma_start(out=staged[0:P:4, W3_SC:].bitcast(I32),
                           in_=w3_scales.rearrange("b q n -> q b n").bitcast(I32))
-        for i in range(PACK - 1):
-            load_w1(0, 0, i, i + 1)
+        for raw, vec in ((gs_raw, gs), (gc_raw, gc)):
+            nc.sync.dma_start(out=raw[:].rearrange("p (b t) -> p b t", t=PACK),
+                              in_=vec.rearrange("(b p t) -> p b t", p=P, t=PACK))
+        load_w1(0, 0, 0, PACK // 2)
         nc.sync.dma_start(out=tab_sc[0:P:4, :].bitcast(I32), in_=tab_scales.rearrange("a q t -> q a t").bitcast(I32))
-        load_w1(0, 0, PACK - 1, PACK)
+        load_w1(0, 0, PACK // 2, PACK)
         nc.sync.dma_start(out=w2_raw[:].bitcast(I32), in_=w2_words[0].bitcast(I32))
         load_words(tab_w[0], tab_words[0])
         load_w1(0, 1)
         load_words(tab_w[1], tab_words[1])
-        nc.gpsimd.dma_start(out=gain_s[:], in_=gs.rearrange("(b p t) -> p b t", p=P, t=PACK))
-        nc.gpsimd.dma_start(out=gc_raw[:], in_=gc.rearrange("(b p t) -> p b t", p=P, t=PACK))
-        nc.gpsimd.tensor_scalar(out=gain_c[:], in0=gc_raw[:], scalar1=-2.0, scalar2=0.0, op0=ALU.mult, op1=ALU.add)
+        nc.gpsimd.memset(gain_in[:], 0.0)
+        make_identity(nc, identity[:])
+        per_side = BLOCKS * PACK
+        nc.gpsimd.tensor_copy(out=gain_in[:, 0:per_side], in_=gs_raw[:])
+        nc.gpsimd.tensor_scalar(out=gain_in[:, per_side : 2 * per_side], in0=gc_raw[:], scalar1=-2.0, scalar2=0.0,
+                                op0=ALU.mult, op1=ALU.add)
+        gain_rows = psum_y.tile([P, P], F32, name="gain_rows", tag="ys")
+        nc.tensor.transpose(gain_rows[:], gain_in[:], identity[:])
+        nc.scalar.copy(out=gain_turned[:], in_=gain_rows[:])
+        gain = psum_y.tile([P, P], F32, name="gain", bufs=1)
+        nc.tensor.transpose(gain[:], gain_turned[:], identity[:])
+        gain_s = gain[:, 0:per_side].rearrange("p (b t) -> p b t", t=PACK)
+        gain_c = gain[:, per_side : 2 * per_side].rearrange("p (b t) -> p b t", t=PACK)
 
         def pick(dst, window, offsets, j0, j1):
             nc.vector.tensor_copy(out=dst, in_=window.indirect(offsets[:, j0 // 16 : j1 // 16]))
@@ -101,7 +119,7 @@ def tile_list_islanding_separation_kernel(
         pick(v_sc_picked[:], tab_sc[:], list8, 0, S)
         nc.vector.tensor_copy(out=staged[:, V_SC : V_SC + S].bitcast(I32), in_=v_sc_picked[:].bitcast(I32))
         for q in range(0, P, QUAD):
-            nc.scalar.dma_start(out=planes[q : q + 4, :, :].bitcast(I32), in_=staged[q : q + QUAD : 4, :].bitcast(I32))
+            nc.sync.dma_start(out=planes[q : q + 4, :, :].bitcast(I32), in_=staged[q : q + QUAD : 4, :].bitcast(I32))
 
         w1_codes = {(b, a): kept([P, K_PASS], U32, "w1_codes%d%d" % (b, a)) for a in range(PASSES) for b in range(BLOCKS)}
         w1_sc = {(b, a): kept([P, K_PASS], U8, "w1_sc%d%d" % (b, a)) for a in range(PASSES) for b in range(BLOCKS)}
@@ -127,11 +145,12 @@ def tile_list_islanding_separation_kernel(
         pick(v_w[0][:], tab_w[0][:].bitcast(U32), list8, 0, S)
         round_w1(0, 0)
         quantize_w1(0, 0)
-        v_w.append(kept([P, S], U32, "v_w1", tag="w1_bf00"))
-        pick(v_w[1][:], tab_w[1][:].bitcast(U32), list8, 0, S)
         round_w1(0, 1)
         quantize_w1(0, 1)
-        v2_w = kept([P, S], U32, "v2_w", tag="w1_bf01")
+        v_w.append(kept([P, S], U32, "v_w1", tag="w1_bf01"))
+        pick(v_w[1][:, 0:FIRST], tab_w[1][:].bitcast(U32), list8, 0, FIRST)
+        pick(v_w[1][:, FIRST:S], tab_w[1][:].bitcast(U32), list8, FIRST, S)
+        v2_w = kept([P, S], U32, "v2_w", tag="tab_w1")
         pick(v2_w[:, 0:FIRST], tab2_w[:].bitcast(U32), list1, 0, FIRST)
         pick(v2_w[:, FIRST:S], tab2_w[:].bitcast(U32), list1, FIRST, S)
 

@@ -25,8 +25,8 @@ BLOCKS = H // K_PASS
 JB = 128
 ROWS = 16
 QUAD = 32
-V_SC, V2_SC, W2_SC, W3_SC = 0, S, 2 * S, 2 * S + K_PASS
-STAGED = W3_SC + N
+V_SC, W2_SC = 0, S
+STAGED = W2_SC + K_PASS
 FIRST = 256
 
 
@@ -60,9 +60,6 @@ def tile_list_islanding_separation_kernel(
         gs_raw = kept([P, BLOCKS * PACK], F32, "gs_raw")
         identity = kept([P, P], F32, "identity")
 
-        warm = kept([P, 2], F32, "warm")
-        nc.vector.memset(warm[:, 0:1], 0.0)
-        nc.scalar.activation(out=warm[:, 1:2], in_=warm[:, 0:1], func=ACT.Sin)
         nc.gpsimd.memset(tab_sc[:].bitcast(I32), 0)
         nc.gpsimd.memset(planes[:].rearrange("p a c -> p (a c)").bitcast(I32), 0)
 
@@ -75,20 +72,20 @@ def tile_list_islanding_separation_kernel(
             nc.sync.dma_start(out=tile[:], in_=words.rearrange("p t i -> p (t i)").bitcast(I32))
 
         nc.sync.dma_start(list1[:], offs2)
-        nc.sync.dma_start(out=tab2_sc[:].bitcast(I32),
-                          in_=tab2_scales[0].bitcast(I32).unsqueeze(1).to_broadcast([ROWS, P // ROWS, T // 4]))
+        for d in (0, 2, 1, 3):
+            rows = tab2_scales[0, 4 * d : 4 * d + 4].bitcast(I32)
+            nc.sync.dma_start(out=tab2_sc[QUAD * d : QUAD * (d + 1), :].bitcast(I32),
+                              in_=rows.unsqueeze(0).to_broadcast([QUAD // 4, 4, T // 4]))
         nc.sync.dma_start(list8[:], offs)
+        load_w1(0, 0, 0, PACK // 2)
+        load_w1(0, 0, PACK // 2, PACK)
+        nc.sync.dma_start(out=tab_sc[0:P:4, :].bitcast(I32), in_=tab_scales.rearrange("a q t -> q a t").bitcast(I32))
         w2_halves = w2_scales[0].rearrange("q (b c) -> (q b) c", b=BLOCKS).bitcast(I32)
         nc.sync.dma_start(out=w2_sc_raw[:].bitcast(I32),
                           in_=w2_halves.unsqueeze(1).to_broadcast([ROWS * BLOCKS, 4, K_PASS // 4]))
-        nc.sync.dma_start(out=staged[0:P:4, W3_SC:].bitcast(I32),
-                          in_=w3_scales.rearrange("b q n -> q b n").bitcast(I32))
         for raw, vec in ((gs_raw, gs), (gc_raw, gc)):
             nc.sync.dma_start(out=raw[:].rearrange("p (b t) -> p b t", t=PACK),
                               in_=vec.rearrange("(b p t) -> p b t", p=P, t=PACK))
-        load_w1(0, 0, 0, PACK // 2)
-        nc.sync.dma_start(out=tab_sc[0:P:4, :].bitcast(I32), in_=tab_scales.rearrange("a q t -> q a t").bitcast(I32))
-        load_w1(0, 0, PACK // 2, PACK)
         nc.sync.dma_start(out=w2_raw[:].bitcast(I32), in_=w2_words[0].bitcast(I32))
         load_words(tab_w[0], tab_words[0])
         load_w1(0, 1)
@@ -113,9 +110,8 @@ def tile_list_islanding_separation_kernel(
         v_sc_picked = kept([P, S], U8, "v_sc_picked")
         v2_sc_picked = kept([P, S], U8, "v2_sc_picked")
         pick(v2_sc_picked[:], tab2_sc[:], list1, 0, S)
-        nc.vector.tensor_copy(out=staged[:, V2_SC : V2_SC + S].bitcast(I32), in_=v2_sc_picked[:].bitcast(I32))
-        nc.vector.tensor_copy(out=staged[:, W2_SC : W2_SC + K_PASS].rearrange("p (t m) -> p m t", t=PACK),
-                              in_=w2_sc_raw[:].rearrange("p (m t) -> p m t", t=PACK))
+        nc.vector.tensor_copy(out=staged[:, W2_SC : W2_SC + K_PASS].rearrange("p (t m) -> p t m", t=PACK),
+                              in_=w2_sc_raw[:].rearrange("p (m t) -> p t m", t=PACK))
         pick(v_sc_picked[:], tab_sc[:], list8, 0, S)
         nc.vector.tensor_copy(out=staged[:, V_SC : V_SC + S].bitcast(I32), in_=v_sc_picked[:].bitcast(I32))
         for q in range(0, P, QUAD):
@@ -137,8 +133,8 @@ def tile_list_islanding_separation_kernel(
             nc.vector.quantize_mx(out=w1_codes[b, a][:].bitcast(FP8X4), scales=w1_sc[b, a][:], in_=w1_bf[b, a])
 
         w2_w = kept([P, 2 * H], U8, "w2_w")
-        nc.vector.tensor_copy(out=w2_w[:].bitcast(U16).rearrange("p (b t m) -> p b m t", b=BLOCKS, t=PACK),
-                              in_=w2_raw[:].bitcast(U16).rearrange("p (b m t) -> p b m t", b=BLOCKS, t=PACK))
+        nc.vector.tensor_copy(out=w2_w[:].bitcast(U16).rearrange("p (b t m) -> p b t m", b=BLOCKS, t=PACK),
+                              in_=w2_raw[:].bitcast(U16).rearrange("p (b m t) -> p b t m", b=BLOCKS, t=PACK))
         tab2_w = kept([P, T], I32, "tab2_w", tag="w2_raw")
         load_words(tab2_w, tab2_words[0])
         v_w = [kept([P, S], U32, "v_w0")]
@@ -162,8 +158,14 @@ def tile_list_islanding_separation_kernel(
             load_w1(1, a)
         w4_raw = kept([P, BLOCKS, PACK, N], F32, "w4_raw", tag="w1_raw01")
         nc.sync.dma_start(out=w4_raw[:], in_=w4.rearrange("(b p i) n -> p b i n", p=P, i=PACK))
-        w3_w = kept([P, BLOCKS, 2 * N], U8, "w3_w", tag="staged")
+        w3_w = kept([P, BLOCKS, 2 * N], U8, "w3_w", tag="w1_bf00")
         nc.sync.dma_start(out=w3_w[:].bitcast(I32), in_=w3_words.rearrange("b p c -> p b c").bitcast(I32))
+
+        w3_sc = kept([P, BLOCKS, N], U8, "w3_sc", tag="staged")
+        nc.gpsimd.memset(w3_sc[:].rearrange("p b n -> p (b n)").bitcast(I32), 0)
+        for r in range(4):
+            nc.sync.dma_start(out=w3_sc[r:P:QUAD, :, :].bitcast(I32),
+                              in_=w3_scales[:, r:ROWS:4, :].rearrange("b d n -> d b n").bitcast(I32))
 
         w4_bf = kept([P, BLOCKS * N * PACK], BF16, "w4_bf")
         w4_codes = kept([P, BLOCKS, N], U32, "w4_codes")
@@ -191,7 +193,7 @@ def tile_list_islanding_separation_kernel(
                         out=bank[:, t, :],
                         lhsT=w2_w[:, 2 * r0 : 2 * (r0 + P)].bitcast(FP4X4),
                         lhsT_scale=planes[:, b, W2_SC + t * P : W2_SC + (t + 1) * P],
-                        rhs=v2_w[:, c].bitcast(FP8X4), rhs_scale=planes[:, 0, V2_SC + j : V2_SC + j + JB],
+                        rhs=v2_w[:, c].bitcast(FP8X4), rhs_scale=v2_sc_picked[:, c],
                         start=False, stop=(t == PACK - 1))
                 cols = slice(jj * JB * PACK, (jj + 1) * JB * PACK)
                 minus_d = bank[:].rearrange("p t j -> p j t")
@@ -202,56 +204,57 @@ def tile_list_islanding_separation_kernel(
             nc.scalar.activation(out=sq[:], in_=sin_h[:], func=ACT.Square)
             return sin_d, sq
 
-        def gains(b, width, sin_d, sq):
-            z = work.tile([P, 2, width * PACK], BF16, name="z", align_bytes=64, bufs=3)
+        def gain_sine(b, width, sin_d, z):
             nc.vector.tensor_tensor(
                 out=z[:, 0, :].rearrange("p (j t) -> p j t", t=PACK),
                 in0=sin_d[:].rearrange("p (j t) -> p j t", t=PACK),
                 in1=gain_s[:, b : b + 1, :].to_broadcast([P, width, PACK]), op=ALU.mult)
+
+        def gain_cosine(b, width, sq, z):
             nc.vector.scalar_tensor_tensor(
                 out=z[:, 1, :].rearrange("p (j t) -> p j t", t=PACK),
                 in0=sq[:].rearrange("p (j t) -> p j t", t=PACK), scalar=0.5,
                 in1=gain_c[:, b : b + 1, :].to_broadcast([P, width, PACK]), op0=ALU.subtract, op1=ALU.mult)
-            return z
 
         z_codes, z_sc = {}, {}
 
-        def quantize_z(b, j0, width, z):
-            codes = kept([P, 2, width], U32, "z_codes%d_%d" % (b, j0))
-            scales = kept([P, 2, width], U8, "z_sc%d_%d" % (b, j0))
+        def quantize_z(b, j0, width, z, s0=0, s1=2):
+            codes = kept([P, s1 - s0, width], U32, "z_codes%d_%d_%d" % (b, j0, s0))
+            scales = kept([P, s1 - s0, width], U8, "z_sc%d_%d_%d" % (b, j0, s0))
             nc.vector.quantize_mx(out=codes[:].rearrange("p s j -> p (s j)").bitcast(FP8X4),
                                   scales=scales[:].rearrange("p s j -> p (s j)"),
-                                  in_=z[:].rearrange("p s c -> p (s c)"))
-            for jj in range(width // JB):
-                c = slice(jj * JB, (jj + 1) * JB)
-                z_codes[b, j0 + jj * JB] = [codes[:, s, c] for s in range(2)]
-                z_sc[b, j0 + jj * JB] = [scales[:, s, c] for s in range(2)]
+                                  in_=z[:, s0:s1, :].rearrange("p s c -> p (s c)"))
+            for s in range(s0, s1):
+                for jj in range(width // JB):
+                    c = slice(jj * JB, (jj + 1) * JB)
+                    z_codes[s, b, j0 + jj * JB] = codes[:, s - s0, c]
+                    z_sc[s, b, j0 + jj * JB] = scales[:, s - s0, c]
 
-        def second_stage(j0, width):
+        def product(side, y, j0, width):
+            for n in range(N // P):
+                cols = slice(n * P, (n + 1) * P)
+                for jj in range(width // JB):
+                    j = j0 + jj * JB
+                    for b in range(BLOCKS):
+                        if side == 0:
+                            w, w_sc = w3_w[:, b, 2 * n * P : 2 * (n + 1) * P].bitcast(FP4X4), w3_sc[:, b, cols]
+                        else:
+                            w, w_sc = w4_codes[:, b, cols].bitcast(FP8X4), w4_sc[:, b, cols]
+                        nc.tensor.matmul_mx(
+                            out=y[:, n, jj * JB : (jj + 1) * JB], lhsT=w, lhsT_scale=w_sc,
+                            rhs=z_codes[side, b, j].bitcast(FP8X4), rhs_scale=z_sc[side, b, j],
+                            start=(b == 0), stop=(b == BLOCKS - 1))
+
+        def sine_side(j0, width):
             ys = psum_y.tile([P, N // P, width], F32, name="ys")
-            yc = psum_y.tile([P, N // P, width], F32, name="yc")
-            for n in range(N // P):
-                for jj in range(width // JB):
-                    j = j0 + jj * JB
-                    for b in range(BLOCKS):
-                        nc.tensor.matmul_mx(
-                            out=ys[:, n, jj * JB : (jj + 1) * JB],
-                            lhsT=w3_w[:, b, 2 * n * P : 2 * (n + 1) * P].bitcast(FP4X4),
-                            lhsT_scale=planes[:, b, W3_SC + n * P : W3_SC + (n + 1) * P],
-                            rhs=z_codes[b, j][0].bitcast(FP8X4), rhs_scale=z_sc[b, j][0],
-                            start=(b == 0), stop=(b == BLOCKS - 1))
-            for n in range(N // P):
-                for jj in range(width // JB):
-                    j = j0 + jj * JB
-                    for b in range(BLOCKS):
-                        nc.tensor.matmul_mx(
-                            out=yc[:, n, jj * JB : (jj + 1) * JB],
-                            lhsT=w4_codes[:, b, n * P : (n + 1) * P].bitcast(FP8X4),
-                            lhsT_scale=w4_sc[:, b, n * P : (n + 1) * P],
-                            rhs=z_codes[b, j][1].bitcast(FP8X4), rhs_scale=z_sc[b, j][1],
-                            start=(b == 0), stop=(b == BLOCKS - 1))
+            product(0, ys, j0, width)
             ys_sb = work.tile([P, N // P, width], F32, name="ys_sb", bufs=2)
             nc.scalar.copy(out=ys_sb[:], in_=ys[:])
+            return ys_sb
+
+        def cosine_side(j0, width, ys_sb):
+            yc = psum_y.tile([P, N // P, width], F32, name="yc")
+            product(1, yc, j0, width)
             res = work.tile([P, N // P, width], F32, name="res", bufs=3)
             nc.vector.tensor_tensor(out=res[:], in0=yc[:], in1=ys_sb[:], op=ALU.mult)
             nc.sync.dma_start(out=out[:, j0 : j0 + width].rearrange("(n p) j -> p n j", p=P), in_=res[:])
@@ -274,11 +277,17 @@ def tile_list_islanding_separation_kernel(
         for step, (b, j0, width) in enumerate(steps):
             sin_d, sq = angles(b, j0, width)
             side_work(step)
-            z = gains(b, width, sin_d, sq)
+            z = work.tile([P, 2, width * PACK], BF16, name="z", align_bytes=64, bufs=3)
+            gain_sine(b, width, sin_d, z)
+            if step < len(steps) - 1:
+                gain_cosine(b, width, sq, z)
             if pending is not None:
                 quantize_z(*pending)
                 if pending[0] == BLOCKS - 1:
-                    second_stage(pending[1], pending[2])
+                    cosine_side(pending[1], pending[2], sine_side(pending[1], pending[2]))
             pending = (b, j0, width, z)
-        quantize_z(*pending)
-        second_stage(pending[1], pending[2])
+        quantize_z(b, j0, width, z, 0, 1)
+        gain_cosine(b, width, sq, z)
+        ys_sb = sine_side(j0, width)
+        quantize_z(b, j0, width, z, 1, 2)
+        cosine_side(j0, width, ys_sb)

@@ -28,6 +28,8 @@ QUAD = 32
 V_SC, W2_SC = 0, S
 STAGED = W2_SC + K_PASS
 FIRST = 256
+TABLE_BYTES = 4 * T
+PICKED_BYTES = 4 * S
 
 
 def tile_list_islanding_separation_kernel(
@@ -37,12 +39,16 @@ def tile_list_islanding_separation_kernel(
     nc = tc.nc
     with ExitStack() as ctx:
         keep = ctx.enter_context(tc.tile_pool(name="keep", bufs=1))
+        shared = ctx.enter_context(tc.tile_pool(name="shared", bufs=1))
         work = ctx.enter_context(tc.tile_pool(name="work", bufs=5))
         psum_d = ctx.enter_context(tc.psum_pool(name="psum_d", bufs=3))
         psum_y = ctx.enter_context(tc.psum_pool(name="psum_y", bufs=2))
 
         def kept(shape, dtype, name, tag=None):
             return keep.tile(shape, dtype, name=name, tag=tag or name, align_bytes=64)
+
+        def placed(shape, dtype, name, offset):
+            return shared.tile(shape, dtype, name=name, align_bytes=64, offset=offset)
 
         list8 = keep.tile([P, S // 16], U16, name="list8")
         list1 = keep.tile([P, S // 16], U16, name="list1")
@@ -51,9 +57,9 @@ def tile_list_islanding_separation_kernel(
         w2_sc_raw = kept([P, K_PASS], U8, "w2_sc_raw")
         staged = kept([P, STAGED], U8, "staged")
         planes = kept([P, 2, STAGED], U8, "planes")
-        tab_w = [kept([P, T], I32, "tab_w%d" % a) for a in range(PASSES)]
+        tab_w = [kept([P, T], I32, "tab_w0")]
         w1_raw = {(0, a): kept([P, PACK, K_PASS], F32, "w1_raw0%d" % a)[:] for a in range(PASSES)}
-        w2_raw = kept([P, 2 * H], U8, "w2_raw")
+        w2_raw = placed([P, 2 * H], U8, "w2_raw", TABLE_BYTES - H)
         gain_in = kept([P, P], F32, "gain_in")
         gain_turned = kept([P, P], F32, "gain_turned")
         gc_raw = kept([P, BLOCKS * PACK], F32, "gc_raw")
@@ -63,33 +69,34 @@ def tile_list_islanding_separation_kernel(
         nc.gpsimd.memset(tab_sc[:].bitcast(I32), 0)
         nc.gpsimd.memset(planes[:].rearrange("p a c -> p (a c)").bitcast(I32), 0)
 
-        def load_w1(b, a, i0=0, i1=PACK):
+        def load_w1(b, a, i0=0, i1=PACK, c0=0, c1=K_PASS, queue=nc.sync):
             rows = w1[a * K_PASS : (a + 1) * K_PASS, b * K_PASS : (b + 1) * K_PASS]
             rows = rows.rearrange("(p i) c -> p i c", i=PACK)
-            nc.sync.dma_start(out=w1_raw[b, a][:, i0:i1, :], in_=rows[:, i0:i1, :])
+            queue.dma_start(out=w1_raw[b, a][:, i0:i1, c0:c1], in_=rows[:, i0:i1, c0:c1])
 
         def load_words(tile, words):
             nc.sync.dma_start(out=tile[:], in_=words.rearrange("p t i -> p (t i)").bitcast(I32))
 
+        w2_halves = w2_scales[0].rearrange("q (b c) -> (q b) c", b=BLOCKS).bitcast(I32)
+        nc.scalar.dma_start(out=w2_sc_raw[:].bitcast(I32),
+                          in_=w2_halves.unsqueeze(1).to_broadcast([ROWS * BLOCKS, 4, K_PASS // 4]))
         nc.sync.dma_start(list1[:], offs2)
         for d in (0, 2, 1, 3):
             rows = tab2_scales[0, 4 * d : 4 * d + 4].bitcast(I32)
-            nc.sync.dma_start(out=tab2_sc[QUAD * d : QUAD * (d + 1), :].bitcast(I32),
+            queue = nc.sync if d < 2 else nc.scalar
+            queue.dma_start(out=tab2_sc[QUAD * d : QUAD * (d + 1), :].bitcast(I32),
                               in_=rows.unsqueeze(0).to_broadcast([QUAD // 4, 4, T // 4]))
         nc.sync.dma_start(list8[:], offs)
-        load_w1(0, 0, 0, PACK // 2)
-        load_w1(0, 0, PACK // 2, PACK)
+        load_w1(0, 0, 0, PACK - 1, queue=nc.scalar)
         nc.sync.dma_start(out=tab_sc[0:P:4, :].bitcast(I32), in_=tab_scales.rearrange("a q t -> q a t").bitcast(I32))
-        w2_halves = w2_scales[0].rearrange("q (b c) -> (q b) c", b=BLOCKS).bitcast(I32)
-        nc.sync.dma_start(out=w2_sc_raw[:].bitcast(I32),
-                          in_=w2_halves.unsqueeze(1).to_broadcast([ROWS * BLOCKS, 4, K_PASS // 4]))
+        load_w1(0, 0, PACK - 1, PACK)
         for raw, vec in ((gs_raw, gs), (gc_raw, gc)):
             nc.sync.dma_start(out=raw[:].rearrange("p (b t) -> p b t", t=PACK),
                               in_=vec.rearrange("(b p t) -> p b t", p=P, t=PACK))
         nc.sync.dma_start(out=w2_raw[:].bitcast(I32), in_=w2_words[0].bitcast(I32))
         load_words(tab_w[0], tab_words[0])
-        load_w1(0, 1)
-        load_words(tab_w[1], tab_words[1])
+        for h in range(2):
+            load_w1(0, 1, 0, PACK, h * K_PASS // 2, (h + 1) * K_PASS // 2)
         nc.gpsimd.memset(gain_in[:], 0.0)
         make_identity(nc, identity[:])
         per_side = BLOCKS * PACK
@@ -109,9 +116,9 @@ def tile_list_islanding_separation_kernel(
 
         v_sc_picked = kept([P, S], U8, "v_sc_picked")
         v2_sc_picked = kept([P, S], U8, "v2_sc_picked")
-        pick(v2_sc_picked[:], tab2_sc[:], list1, 0, S)
         nc.vector.tensor_copy(out=staged[:, W2_SC : W2_SC + K_PASS].rearrange("p (t m) -> p t m", t=PACK),
                               in_=w2_sc_raw[:].rearrange("p (m t) -> p t m", t=PACK))
+        pick(v2_sc_picked[:], tab2_sc[:], list1, 0, S)
         pick(v_sc_picked[:], tab_sc[:], list8, 0, S)
         nc.vector.tensor_copy(out=staged[:, V_SC : V_SC + S].bitcast(I32), in_=v_sc_picked[:].bitcast(I32))
         for q in range(0, P, QUAD):
@@ -119,11 +126,12 @@ def tile_list_islanding_separation_kernel(
 
         w1_codes = {(b, a): kept([P, K_PASS], U32, "w1_codes%d%d" % (b, a)) for a in range(PASSES) for b in range(BLOCKS)}
         w1_sc = {(b, a): kept([P, K_PASS], U8, "w1_sc%d%d" % (b, a)) for a in range(PASSES) for b in range(BLOCKS)}
-        w1_bf = {(0, a): kept([P, PACK * K_PASS], BF16, "w1_bf0%d" % a)[:] for a in range(PASSES)}
+        w1_bf = {(0, 0): kept([P, PACK * K_PASS], BF16, "w1_bf00")[:],
+                 (0, 1): placed([P, PACK * K_PASS], BF16, "w1_bf01", 2 * TABLE_BYTES + PICKED_BYTES // 2)[:]}
 
-        def round_w1(b, a):
-            dst = w1_bf[b, a].rearrange("p (t m i) -> p m i t", t=PACK, i=PACK)
-            src = w1_raw[b, a].rearrange("p i (m t) -> p m i t", t=PACK)
+        def round_w1(b, a, m0=0, m1=P):
+            dst = w1_bf[b, a].rearrange("p (t m i) -> p m i t", t=PACK, i=PACK)[:, m0:m1]
+            src = w1_raw[b, a].rearrange("p i (m t) -> p m i t", t=PACK)[:, m0:m1]
             if b == 0:
                 nc.scalar.activation(out=dst, in_=src, func=ACT.Copy, scale=-1.0)
             else:
@@ -135,23 +143,27 @@ def tile_list_islanding_separation_kernel(
         w2_w = kept([P, 2 * H], U8, "w2_w")
         nc.vector.tensor_copy(out=w2_w[:].bitcast(U16).rearrange("p (b t m) -> p b t m", b=BLOCKS, t=PACK),
                               in_=w2_raw[:].bitcast(U16).rearrange("p (b m t) -> p b t m", b=BLOCKS, t=PACK))
-        tab2_w = kept([P, T], I32, "tab2_w", tag="w2_raw")
+        tab_w.append(placed([P, T], I32, "tab_w1", 0))
+        load_words(tab_w[1], tab_words[1])
+        tab2_w = placed([P, T], I32, "tab2_w", TABLE_BYTES)
         load_words(tab2_w, tab2_words[0])
         v_w = [kept([P, S], U32, "v_w0")]
         pick(v_w[0][:], tab_w[0][:].bitcast(U32), list8, 0, S)
         round_w1(0, 0)
         quantize_w1(0, 0)
-        round_w1(0, 1)
+        for h in range(2):
+            round_w1(0, 1, h * P // 2, (h + 1) * P // 2)
         quantize_w1(0, 1)
-        v_w.append(kept([P, S], U32, "v_w1", tag="w1_bf01"))
+        v_w.append(placed([P, S], U32, "v_w1", 2 * TABLE_BYTES))
+        v2_w = placed([P, S], U32, "v2_w", 2 * TABLE_BYTES + PICKED_BYTES)
         pick(v_w[1][:, 0:FIRST], tab_w[1][:].bitcast(U32), list8, 0, FIRST)
-        pick(v_w[1][:, FIRST:S], tab_w[1][:].bitcast(U32), list8, FIRST, S)
-        v2_w = kept([P, S], U32, "v2_w", tag="tab_w1")
+        pick(v_w[1][:, FIRST : S - FIRST], tab_w[1][:].bitcast(U32), list8, FIRST, S - FIRST)
         pick(v2_w[:, 0:FIRST], tab2_w[:].bitcast(U32), list1, 0, FIRST)
         pick(v2_w[:, FIRST:S], tab2_w[:].bitcast(U32), list1, FIRST, S)
+        pick(v_w[1][:, S - FIRST : S], tab_w[1][:].bitcast(U32), list8, S - FIRST, S)
 
-        w1_late = kept([P, PASSES * PACK * K_PASS], F32, "w1_late", tag="tab_w0")
-        w1_bf_late = kept([P, PASSES * PACK * K_PASS], BF16, "w1_bf_late", tag="w2_raw")
+        w1_late = kept([P, PASSES * PACK * K_PASS], F32, "w1_late", tag="w1_raw00")
+        w1_bf_late = placed([P, PASSES * PACK * K_PASS], BF16, "w1_bf_late", TABLE_BYTES)
         for a in range(PASSES):
             w1_bf[1, a] = w1_bf_late[:, a * PACK * K_PASS : (a + 1) * PACK * K_PASS]
             w1_raw[1, a] = w1_late[:, a * PACK * K_PASS : (a + 1) * PACK * K_PASS].rearrange("p (i c) -> p i c", i=PACK)
@@ -265,8 +277,9 @@ def tile_list_islanding_separation_kernel(
             if step in (1, 3):
                 quantize_w1(1, step // 2)
             if step == 3:
-                nc.scalar.copy(out=w4_bf[:].rearrange("p (b c e i) -> p b c i e", b=BLOCKS, e=4, i=PACK),
-                               in_=w4_raw[:].rearrange("p b i (c e) -> p b c i e", e=4))
+                for b, copy in enumerate((nc.vector.tensor_copy, nc.scalar.copy)):
+                    copy(out=w4_bf[:, b * N * PACK : (b + 1) * N * PACK].rearrange("p (c e i) -> p c i e", e=4, i=PACK),
+                         in_=w4_raw[:, b, :, :].rearrange("p i (c e) -> p c i e", e=4))
             if step == 4:
                 nc.vector.quantize_mx(out=w4_codes[:].rearrange("p b n -> p (b n)").bitcast(FP8X4),
                                       scales=w4_sc[:].rearrange("p b n -> p (b n)"), in_=w4_bf[:])

@@ -1,3 +1,4 @@
+import math
 from contextlib import ExitStack
 
 import concourse.mybir as mybir
@@ -60,19 +61,16 @@ def tile_list_islanding_separation_kernel(
         tab_w = [kept([P, T], I32, "tab_w0")]
         w1_raw = {(0, a): kept([P, PACK, K_PASS], F32, "w1_raw0%d" % a)[:] for a in range(PASSES)}
         w2_raw = placed([P, 2 * H], U8, "w2_raw", TABLE_BYTES - H)
-        gain_in = kept([P, P], F32, "gain_in")
-        gain_turned = kept([P, P], F32, "gain_turned")
-        gc_raw = kept([P, BLOCKS * PACK], F32, "gc_raw")
-        gs_raw = kept([P, BLOCKS * PACK], F32, "gs_raw")
+        gain_rows = kept([P, K_PASS], F32, "gain_rows")
         identity = kept([P, P], F32, "identity")
 
         nc.gpsimd.memset(tab_sc[:].bitcast(I32), 0)
         nc.gpsimd.memset(planes[:].rearrange("p a c -> p (a c)").bitcast(I32), 0)
 
-        def load_w1(b, a, i0=0, i1=PACK, c0=0, c1=K_PASS, queue=nc.sync):
+        def load_w1(b, a, i0=0, i1=PACK, queue=nc.sync):
             rows = w1[a * K_PASS : (a + 1) * K_PASS, b * K_PASS : (b + 1) * K_PASS]
             rows = rows.rearrange("(p i) c -> p i c", i=PACK)
-            queue.dma_start(out=w1_raw[b, a][:, i0:i1, c0:c1], in_=rows[:, i0:i1, c0:c1])
+            queue.dma_start(out=w1_raw[b, a][:, i0:i1, :], in_=rows[:, i0:i1, :])
 
         def load_words(tile, words):
             nc.sync.dma_start(out=tile[:], in_=words.rearrange("p t i -> p (t i)").bitcast(I32))
@@ -90,26 +88,19 @@ def tile_list_islanding_separation_kernel(
         load_w1(0, 0, 0, PACK - 1, queue=nc.scalar)
         nc.sync.dma_start(out=tab_sc[0:P:4, :].bitcast(I32), in_=tab_scales.rearrange("a q t -> q a t").bitcast(I32))
         load_w1(0, 0, PACK - 1, PACK)
-        for raw, vec in ((gs_raw, gs), (gc_raw, gc)):
-            nc.sync.dma_start(out=raw[:].rearrange("p (b t) -> p b t", t=PACK),
-                              in_=vec.rearrange("(b p t) -> p b t", p=P, t=PACK))
         nc.sync.dma_start(out=w2_raw[:].bitcast(I32), in_=w2_words[0].bitcast(I32))
         load_words(tab_w[0], tab_words[0])
-        for h in range(2):
-            load_w1(0, 1, 0, PACK, h * K_PASS // 2, (h + 1) * K_PASS // 2)
-        nc.gpsimd.memset(gain_in[:], 0.0)
+        load_w1(0, 1)
+        nc.gpsimd.memset(gain_rows[:], 0.0)
+        nc.gpsimd.dma_start(out=gain_rows[0:BLOCKS, :], in_=gs.rearrange("(b c) -> b c", b=BLOCKS))
+        nc.gpsimd.dma_start(out=gain_rows[BLOCKS : 2 * BLOCKS, :], in_=gc.rearrange("(b c) -> b c", b=BLOCKS))
         make_identity(nc, identity[:])
-        per_side = BLOCKS * PACK
-        nc.gpsimd.tensor_copy(out=gain_in[:, 0:per_side], in_=gs_raw[:])
-        nc.gpsimd.tensor_scalar(out=gain_in[:, per_side : 2 * per_side], in0=gc_raw[:], scalar1=-2.0, scalar2=0.0,
-                                op0=ALU.mult, op1=ALU.add)
-        gain_rows = psum_y.tile([P, P], F32, name="gain_rows", tag="ys")
-        nc.tensor.transpose(gain_rows[:], gain_in[:], identity[:])
-        nc.scalar.copy(out=gain_turned[:], in_=gain_rows[:])
-        gain = psum_y.tile([P, P], F32, name="gain", bufs=1)
-        nc.tensor.transpose(gain[:], gain_turned[:], identity[:])
-        gain_s = gain[:, 0:per_side].rearrange("p (b t) -> p b t", t=PACK)
-        gain_c = gain[:, per_side : 2 * per_side].rearrange("p (b t) -> p b t", t=PACK)
+        gain = psum_y.tile([P, PACK, P], F32, name="gain", bufs=1)
+        for t in range(PACK):
+            nc.tensor.transpose(gain[:, t, :], gain_rows[:, t:K_PASS:PACK], identity[:])
+
+        def gain_of(row, width):
+            return gain[:, :, row : row + 1].rearrange("p t o -> p o t").to_broadcast([P, width, PACK])
 
         def pick(dst, window, offsets, j0, j1):
             nc.vector.tensor_copy(out=dst, in_=window.indirect(offsets[:, j0 // 16 : j1 // 16]))
@@ -129,9 +120,9 @@ def tile_list_islanding_separation_kernel(
         w1_bf = {(0, 0): kept([P, PACK * K_PASS], BF16, "w1_bf00")[:],
                  (0, 1): placed([P, PACK * K_PASS], BF16, "w1_bf01", 2 * TABLE_BYTES + PICKED_BYTES // 2)[:]}
 
-        def round_w1(b, a, m0=0, m1=P):
-            dst = w1_bf[b, a].rearrange("p (t m i) -> p m i t", t=PACK, i=PACK)[:, m0:m1]
-            src = w1_raw[b, a].rearrange("p i (m t) -> p m i t", t=PACK)[:, m0:m1]
+        def round_w1(b, a):
+            dst = w1_bf[b, a].rearrange("p (t m i) -> p m i t", t=PACK, i=PACK)
+            src = w1_raw[b, a].rearrange("p i (m t) -> p m i t", t=PACK)
             if b == 0:
                 nc.scalar.activation(out=dst, in_=src, func=ACT.Copy, scale=-1.0)
             else:
@@ -151,8 +142,7 @@ def tile_list_islanding_separation_kernel(
         pick(v_w[0][:], tab_w[0][:].bitcast(U32), list8, 0, S)
         round_w1(0, 0)
         quantize_w1(0, 0)
-        for h in range(2):
-            round_w1(0, 1, h * P // 2, (h + 1) * P // 2)
+        round_w1(0, 1)
         quantize_w1(0, 1)
         v_w.append(placed([P, S], U32, "v_w1", 2 * TABLE_BYTES))
         v2_w = placed([P, S], U32, "v2_w", 2 * TABLE_BYTES + PICKED_BYTES)
@@ -212,21 +202,21 @@ def tile_list_islanding_separation_kernel(
                 nc.scalar.activation(out=sin_h[:, cols].rearrange("p (j t) -> p j t", t=PACK), in_=minus_d,
                                      func=ACT.Sin, scale=0.5)
                 nc.scalar.activation(out=sin_d[:, cols].rearrange("p (j t) -> p j t", t=PACK), in_=minus_d,
-                                     func=ACT.Sin, scale=-1.0)
-            nc.scalar.activation(out=sq[:], in_=sin_h[:], func=ACT.Square)
+                                     func=ACT.Sin)
+            nc.scalar.activation(out=sq[:], in_=sin_h[:], func=ACT.Square, scale=math.sqrt(2.0))
             return sin_d, sq
 
         def gain_sine(b, width, sin_d, z):
             nc.vector.tensor_tensor(
                 out=z[:, 0, :].rearrange("p (j t) -> p j t", t=PACK),
                 in0=sin_d[:].rearrange("p (j t) -> p j t", t=PACK),
-                in1=gain_s[:, b : b + 1, :].to_broadcast([P, width, PACK]), op=ALU.mult)
+                in1=gain_of(b, width), op=ALU.mult)
 
         def gain_cosine(b, width, sq, z):
             nc.vector.scalar_tensor_tensor(
                 out=z[:, 1, :].rearrange("p (j t) -> p j t", t=PACK),
-                in0=sq[:].rearrange("p (j t) -> p j t", t=PACK), scalar=0.5,
-                in1=gain_c[:, b : b + 1, :].to_broadcast([P, width, PACK]), op0=ALU.subtract, op1=ALU.mult)
+                in0=sq[:].rearrange("p (j t) -> p j t", t=PACK), scalar=1.0,
+                in1=gain_of(BLOCKS + b, width), op0=ALU.subtract, op1=ALU.mult)
 
         z_codes, z_sc = {}, {}
 

@@ -113,7 +113,7 @@ def tile_list_islanding_separation_kernel(
         pick(v_sc_picked[:], tab_sc[:], list8, 0, S)
         nc.vector.tensor_copy(out=staged[:, V_SC : V_SC + S].bitcast(I32), in_=v_sc_picked[:].bitcast(I32))
         for q in range(0, P, QUAD):
-            nc.sync.dma_start(out=planes[q : q + 4, :, :].bitcast(I32), in_=staged[q : q + QUAD : 4, :].bitcast(I32))
+            nc.scalar.dma_start(out=planes[q : q + 4, :, :].bitcast(I32), in_=staged[q : q + QUAD : 4, :].bitcast(I32))
 
         w1_codes = {(b, a): kept([P, K_PASS], U32, "w1_codes%d%d" % (b, a)) for a in range(PASSES) for b in range(BLOCKS)}
         w1_sc = {(b, a): kept([P, K_PASS], U8, "w1_sc%d%d" % (b, a)) for a in range(PASSES) for b in range(BLOCKS)}

@@ -29,6 +29,7 @@ QUAD = 32
 V_SC, W2_SC = 0, S
 STAGED = W2_SC + K_PASS
 FIRST = 256
+RUN = 64
 TABLE_BYTES = 4 * T
 PICKED_BYTES = 4 * S
 
@@ -99,9 +100,6 @@ def tile_list_islanding_separation_kernel(
         for t in range(PACK):
             nc.tensor.transpose(gain[:, t, :], gain_rows[:, t:K_PASS:PACK], identity[:])
 
-        def gain_of(row, width):
-            return gain[:, :, row : row + 1].rearrange("p t o -> p o t").to_broadcast([P, width, PACK])
-
         def pick(dst, window, offsets, j0, j1):
             nc.vector.tensor_copy(out=dst, in_=window.indirect(offsets[:, j0 // 16 : j1 // 16]))
 
@@ -143,6 +141,14 @@ def tile_list_islanding_separation_kernel(
         round_w1(0, 0)
         quantize_w1(0, 0)
         round_w1(0, 1)
+        gain_run = kept([P, 2 * BLOCKS, RUN, PACK], F32, "gain_run", tag="v_sc_picked")
+        nc.scalar.copy(out=gain_run[:], in_=gain[:, :, 0 : 2 * BLOCKS].rearrange("p t r -> p r t").unsqueeze(2)
+                       .to_broadcast([P, 2 * BLOCKS, RUN, PACK]))
+
+        def gain_of(row, width):
+            run = gain_run[:, row].rearrange("p j t -> p (j t)")
+            return run.unsqueeze(1).to_broadcast([P, width // RUN, RUN * PACK])
+
         quantize_w1(0, 1)
         v_w.append(placed([P, S], U32, "v_w1", 2 * TABLE_BYTES))
         v2_w = placed([P, S], U32, "v2_w", 2 * TABLE_BYTES + PICKED_BYTES)
@@ -208,14 +214,14 @@ def tile_list_islanding_separation_kernel(
 
         def gain_sine(b, width, sin_d, z):
             nc.vector.tensor_tensor(
-                out=z[:, 0, :].rearrange("p (j t) -> p j t", t=PACK),
-                in0=sin_d[:].rearrange("p (j t) -> p j t", t=PACK),
+                out=z[:, 0, :].rearrange("p (u c) -> p u c", c=RUN * PACK),
+                in0=sin_d[:].rearrange("p (u c) -> p u c", c=RUN * PACK),
                 in1=gain_of(b, width), op=ALU.mult)
 
         def gain_cosine(b, width, sq, z):
             nc.vector.scalar_tensor_tensor(
-                out=z[:, 1, :].rearrange("p (j t) -> p j t", t=PACK),
-                in0=sq[:].rearrange("p (j t) -> p j t", t=PACK), scalar=1.0,
+                out=z[:, 1, :].rearrange("p (u c) -> p u c", c=RUN * PACK),
+                in0=sq[:].rearrange("p (u c) -> p u c", c=RUN * PACK), scalar=1.0,
                 in1=gain_of(BLOCKS + b, width), op0=ALU.subtract, op1=ALU.mult)
 
         z_codes, z_sc = {}, {}

@@ -29,7 +29,7 @@ QUAD = 32
 V_SC, W2_SC = 0, S
 STAGED = W2_SC + K_PASS
 FIRST = 256
-RUN = 64
+PIECES = 4
 TABLE_BYTES = 4 * T
 PICKED_BYTES = 4 * S
 
@@ -113,8 +113,8 @@ def tile_list_islanding_separation_kernel(
         for q in range(0, P, QUAD):
             nc.scalar.dma_start(out=planes[q : q + 4, :, :].bitcast(I32), in_=staged[q : q + QUAD : 4, :].bitcast(I32))
 
-        w1_codes = {(b, a): kept([P, K_PASS], U32, "w1_codes%d%d" % (b, a)) for a in range(PASSES) for b in range(BLOCKS)}
-        w1_sc = {(b, a): kept([P, K_PASS], U8, "w1_sc%d%d" % (b, a)) for a in range(PASSES) for b in range(BLOCKS)}
+        w1_codes = {(0, a): kept([P, K_PASS], U32, "w1_codes0%d" % a)[:] for a in range(PASSES)}
+        w1_sc = {(0, a): kept([P, K_PASS], U8, "w1_sc0%d" % a)[:] for a in range(PASSES)}
         w1_bf = {(0, 0): kept([P, PACK * K_PASS], BF16, "w1_bf00")[:],
                  (0, 1): placed([P, PACK * K_PASS], BF16, "w1_bf01", 2 * TABLE_BYTES + PICKED_BYTES // 2)[:]}
 
@@ -124,10 +124,14 @@ def tile_list_islanding_separation_kernel(
             if b == 0:
                 nc.scalar.activation(out=dst, in_=src, func=ACT.Copy, scale=-1.0)
             else:
-                nc.vector.tensor_scalar(out=dst, in0=src, scalar1=-1.0, scalar2=None, op0=ALU.mult)
+                dst, src = dst.rearrange("p m i t -> p m t i"), src.rearrange("p m i t -> p m t i")
+                for m0 in range(0, P, P // PIECES):
+                    m = slice(m0, m0 + P // PIECES)
+                    nc.gpsimd.tensor_scalar(out=dst[:, m], in0=src[:, m], scalar1=-1.0, scalar2=0.0,
+                                            op0=ALU.mult, op1=ALU.add)
 
         def quantize_w1(b, a):
-            nc.vector.quantize_mx(out=w1_codes[b, a][:].bitcast(FP8X4), scales=w1_sc[b, a][:], in_=w1_bf[b, a])
+            nc.vector.quantize_mx(out=w1_codes[b, a].bitcast(FP8X4), scales=w1_sc[b, a], in_=w1_bf[b, a])
 
         w2_w = kept([P, 2 * H], U8, "w2_w")
         nc.vector.tensor_copy(out=w2_w[:].bitcast(U16).rearrange("p (b t m) -> p b t m", b=BLOCKS, t=PACK),
@@ -141,13 +145,9 @@ def tile_list_islanding_separation_kernel(
         round_w1(0, 0)
         quantize_w1(0, 0)
         round_w1(0, 1)
-        gain_run = kept([P, 2 * BLOCKS, RUN, PACK], F32, "gain_run", tag="v_sc_picked")
-        nc.scalar.copy(out=gain_run[:], in_=gain[:, :, 0 : 2 * BLOCKS].rearrange("p t r -> p r t").unsqueeze(2)
-                       .to_broadcast([P, 2 * BLOCKS, RUN, PACK]))
 
         def gain_of(row, width):
-            run = gain_run[:, row].rearrange("p j t -> p (j t)")
-            return run.unsqueeze(1).to_broadcast([P, width // RUN, RUN * PACK])
+            return gain[:, :, row].unsqueeze(1).to_broadcast([P, width, PACK])
 
         quantize_w1(0, 1)
         v_w.append(placed([P, S], U32, "v_w1", 2 * TABLE_BYTES))
@@ -176,13 +176,25 @@ def tile_list_islanding_separation_kernel(
                               in_=w3_scales[:, r:ROWS:4, :].rearrange("b d n -> d b n").bitcast(I32))
 
         w4_bf = kept([P, BLOCKS * N * PACK], BF16, "w4_bf")
-        w4_codes = kept([P, BLOCKS, N], U32, "w4_codes")
         w4_sc = kept([P, BLOCKS, N], U8, "w4_sc")
+        late = {}
+        for a in range(PASSES):
+            round_w1(1, a)
+        for b in range(BLOCKS):
+            dst = w4_bf[:, b * N * PACK : (b + 1) * N * PACK].rearrange("p (c i) -> p c i", i=PACK)
+            src = w4_raw[:, b, :, :].rearrange("p i c -> p c i")
+            for c0 in range(0, N, N // 2):
+                c = slice(c0, c0 + N // 2)
+                nc.gpsimd.tensor_scalar(out=dst[:, c], in0=src[:, c], scalar1=1.0, scalar2=0.0,
+                                        op0=ALU.mult, op1=ALU.add)
 
-        def angles(b, j0, width):
+        def angles(step, b, j0, width):
             sin_d = work.tile([P, width * PACK], F32, name="sin_d")
             sin_h = work.tile([P, width * PACK], F32, name="sin_h", bufs=2)
-            sq = work.tile([P, width * PACK], F32, name="sq")
+            if step in (2, 4):
+                sq = kept([P, width * PACK], F32, "sq%d" % step)
+            else:
+                sq = work.tile([P, width * PACK], F32, name="sq")
             for jj in range(width // JB):
                 j = j0 + jj * JB
                 c = slice(j, j + JB)
@@ -214,14 +226,14 @@ def tile_list_islanding_separation_kernel(
 
         def gain_sine(b, width, sin_d, z):
             nc.vector.tensor_tensor(
-                out=z[:, 0, :].rearrange("p (u c) -> p u c", c=RUN * PACK),
-                in0=sin_d[:].rearrange("p (u c) -> p u c", c=RUN * PACK),
+                out=z[:, 0, :].rearrange("p (u c) -> p u c", c=PACK),
+                in0=sin_d[:].rearrange("p (u c) -> p u c", c=PACK),
                 in1=gain_of(b, width), op=ALU.mult)
 
         def gain_cosine(b, width, sq, z):
             nc.vector.scalar_tensor_tensor(
-                out=z[:, 1, :].rearrange("p (u c) -> p u c", c=RUN * PACK),
-                in0=sq[:].rearrange("p (u c) -> p u c", c=RUN * PACK), scalar=1.0,
+                out=z[:, 1, :].rearrange("p (u c) -> p u c", c=PACK),
+                in0=sq[:].rearrange("p (u c) -> p u c", c=PACK), scalar=1.0,
                 in1=gain_of(BLOCKS + b, width), op0=ALU.subtract, op1=ALU.mult)
 
         z_codes, z_sc = {}, {}
@@ -247,7 +259,7 @@ def tile_list_islanding_separation_kernel(
                         if side == 0:
                             w, w_sc = w3_w[:, b, 2 * n * P : 2 * (n + 1) * P].bitcast(FP4X4), w3_sc[:, b, cols]
                         else:
-                            w, w_sc = w4_codes[:, b, cols].bitcast(FP8X4), w4_sc[:, b, cols]
+                            w, w_sc = late["w4"][:, b, cols].bitcast(FP8X4), w4_sc[:, b, cols]
                         nc.tensor.matmul_mx(
                             out=y[:, n, jj * JB : (jj + 1) * JB], lhsT=w, lhsT_scale=w_sc,
                             rhs=z_codes[side, b, j].bitcast(FP8X4), rhs_scale=z_sc[side, b, j],
@@ -268,23 +280,23 @@ def tile_list_islanding_separation_kernel(
             nc.sync.dma_start(out=out[:, j0 : j0 + width].rearrange("(n p) j -> p n j", p=P), in_=res[:])
 
         def side_work(step):
-            if step in (0, 2):
-                round_w1(1, step // 2)
-            if step in (1, 3):
-                quantize_w1(1, step // 2)
             if step == 3:
-                for b, copy in enumerate((nc.vector.tensor_copy, nc.scalar.copy)):
-                    copy(out=w4_bf[:, b * N * PACK : (b + 1) * N * PACK].rearrange("p (c e i) -> p c i e", e=4, i=PACK),
-                         in_=w4_raw[:, b, :, :].rearrange("p i (c e) -> p c i e", e=4))
-            if step == 4:
-                nc.vector.quantize_mx(out=w4_codes[:].rearrange("p b n -> p (b n)").bitcast(FP8X4),
+                codes = kept([P, PASSES * K_PASS], U32, "w1_codes_late", tag="sq2")
+                scales = kept([P, PASSES * K_PASS], U8, "w1_sc_late")
+                nc.vector.quantize_mx(out=codes[:].bitcast(FP8X4), scales=scales[:], in_=w1_bf_late[:])
+                for a in range(PASSES):
+                    w1_codes[1, a] = codes[:, a * K_PASS : (a + 1) * K_PASS]
+                    w1_sc[1, a] = scales[:, a * K_PASS : (a + 1) * K_PASS]
+            if step == 5:
+                late["w4"] = kept([P, BLOCKS, N], U32, "w4_codes", tag="sq4")
+                nc.vector.quantize_mx(out=late["w4"][:].rearrange("p b n -> p (b n)").bitcast(FP8X4),
                                       scales=w4_sc[:].rearrange("p b n -> p (b n)"), in_=w4_bf[:])
 
         steps = [(0, 0, 128), (0, 128, 128), (0, 256, 256), (0, 512, 256), (0, 768, 256),
                  (1, 0, 256), (1, 256, 256), (1, 512, 256), (1, 768, 128), (1, 896, 128)]
         pending = None
         for step, (b, j0, width) in enumerate(steps):
-            sin_d, sq = angles(b, j0, width)
+            sin_d, sq = angles(step, b, j0, width)
             side_work(step)
             z = work.tile([P, 2, width * PACK], BF16, name="z", align_bytes=64, bufs=3)
             gain_sine(b, width, sin_d, z)

@@ -60,8 +60,8 @@ def tile_list_islanding_separation_kernel(
         staged = kept([P, STAGED], U8, "staged")
         planes = kept([P, 2, STAGED], U8, "planes")
         tab_w = [kept([P, T], I32, "tab_w0")]
-        w1_raw = {(0, a): kept([P, PACK, K_PASS], F32, "w1_raw0%d" % a)[:] for a in range(PASSES)}
-        w2_raw = placed([P, 2 * H], U8, "w2_raw", TABLE_BYTES - H)
+        w1_raw = {(0, 0): kept([P, PACK, K_PASS], F32, "w1_raw00")[:]}
+        w2_raw = placed([P, 2 * H], U8, "w2_raw", TABLE_BYTES)
         gain_rows = kept([P, K_PASS], F32, "gain_rows")
         identity = kept([P, P], F32, "identity")
 
@@ -91,7 +91,12 @@ def tile_list_islanding_separation_kernel(
         load_w1(0, 0, PACK - 1, PACK)
         nc.sync.dma_start(out=w2_raw[:].bitcast(I32), in_=w2_words[0].bitcast(I32))
         load_words(tab_w[0], tab_words[0])
-        load_w1(0, 1)
+        w1_halves = [kept([P, PACK, K_PASS // 2], F32, "w1_half%d" % h) for h in range(2)]
+        for h in range(2):
+            rows = w1[K_PASS : 2 * K_PASS, h * K_PASS // 2 : (h + 1) * K_PASS // 2]
+            nc.sync.dma_start(out=w1_halves[h][:], in_=rows.rearrange("(p i) c -> p i c", i=PACK))
+        tab_w.append(placed([P, T], I32, "tab_w1", 0))
+        load_words(tab_w[1], tab_words[1])
         nc.gpsimd.memset(gain_rows[:], 0.0)
         nc.gpsimd.dma_start(out=gain_rows[0:BLOCKS, :], in_=gs.rearrange("(b c) -> b c", b=BLOCKS))
         nc.gpsimd.dma_start(out=gain_rows[BLOCKS : 2 * BLOCKS, :], in_=gc.rearrange("(b c) -> b c", b=BLOCKS))
@@ -136,15 +141,16 @@ def tile_list_islanding_separation_kernel(
         w2_w = kept([P, 2 * H], U8, "w2_w")
         nc.vector.tensor_copy(out=w2_w[:].bitcast(U16).rearrange("p (b t m) -> p b t m", b=BLOCKS, t=PACK),
                               in_=w2_raw[:].bitcast(U16).rearrange("p (b m t) -> p b t m", b=BLOCKS, t=PACK))
-        tab_w.append(placed([P, T], I32, "tab_w1", 0))
-        load_words(tab_w[1], tab_words[1])
         tab2_w = placed([P, T], I32, "tab2_w", TABLE_BYTES)
         load_words(tab2_w, tab2_words[0])
         v_w = [kept([P, S], U32, "v_w0")]
         pick(v_w[0][:], tab_w[0][:].bitcast(U32), list8, 0, S)
         round_w1(0, 0)
         quantize_w1(0, 0)
-        round_w1(0, 1)
+        for h in range(2):
+            dst = w1_bf[0, 1].rearrange("p (t m i) -> p m i t", t=PACK, i=PACK)[:, h * P // 2 : (h + 1) * P // 2]
+            nc.scalar.activation(out=dst, in_=w1_halves[h][:].rearrange("p i (m t) -> p m i t", t=PACK),
+                                 func=ACT.Copy, scale=-1.0)
 
         def gain_of(row, width):
             return gain[:, :, row].unsqueeze(1).to_broadcast([P, width, PACK])
@@ -153,20 +159,19 @@ def tile_list_islanding_separation_kernel(
         v_w.append(placed([P, S], U32, "v_w1", 2 * TABLE_BYTES))
         v2_w = placed([P, S], U32, "v2_w", 2 * TABLE_BYTES + PICKED_BYTES)
         pick(v_w[1][:, 0:FIRST], tab_w[1][:].bitcast(U32), list8, 0, FIRST)
-        pick(v_w[1][:, FIRST : S - FIRST], tab_w[1][:].bitcast(U32), list8, FIRST, S - FIRST)
+        pick(v_w[1][:, FIRST:S], tab_w[1][:].bitcast(U32), list8, FIRST, S)
         pick(v2_w[:, 0:FIRST], tab2_w[:].bitcast(U32), list1, 0, FIRST)
         pick(v2_w[:, FIRST:S], tab2_w[:].bitcast(U32), list1, FIRST, S)
-        pick(v_w[1][:, S - FIRST : S], tab_w[1][:].bitcast(U32), list8, S - FIRST, S)
 
-        w1_late = kept([P, PASSES * PACK * K_PASS], F32, "w1_late", tag="w1_raw00")
+        w1_late = kept([P, PASSES * PACK * K_PASS], F32, "w1_late", tag="tab_w0")
         w1_bf_late = placed([P, PASSES * PACK * K_PASS], BF16, "w1_bf_late", TABLE_BYTES)
         for a in range(PASSES):
             w1_bf[1, a] = w1_bf_late[:, a * PACK * K_PASS : (a + 1) * PACK * K_PASS]
             w1_raw[1, a] = w1_late[:, a * PACK * K_PASS : (a + 1) * PACK * K_PASS].rearrange("p (i c) -> p i c", i=PACK)
             load_w1(1, a)
-        w4_raw = kept([P, BLOCKS, PACK, N], F32, "w4_raw", tag="w1_raw01")
+        w4_raw = placed([P, BLOCKS, PACK, N], F32, "w4_raw", 0)
         nc.sync.dma_start(out=w4_raw[:], in_=w4.rearrange("(b p i) n -> p b i n", p=P, i=PACK))
-        w3_w = kept([P, BLOCKS, 2 * N], U8, "w3_w", tag="w1_bf00")
+        w3_w = kept([P, BLOCKS, 2 * N], U8, "w3_w", tag="w1_half1")
         nc.sync.dma_start(out=w3_w[:].bitcast(I32), in_=w3_words.rearrange("b p c -> p b c").bitcast(I32))
 
         w3_sc = kept([P, BLOCKS, N], U8, "w3_sc", tag="staged")
@@ -221,7 +226,11 @@ def tile_list_islanding_separation_kernel(
                                      func=ACT.Sin, scale=0.5)
                 nc.scalar.activation(out=sin_d[:, cols].rearrange("p (j t) -> p j t", t=PACK), in_=minus_d,
                                      func=ACT.Sin)
-            nc.scalar.activation(out=sq[:], in_=sin_h[:], func=ACT.Square, scale=math.sqrt(2.0))
+            if step in (0, 1):
+                nc.vector.scalar_tensor_tensor(out=sq[:], in0=sin_h[:], scalar=2.0, in1=sin_h[:],
+                                               op0=ALU.mult, op1=ALU.mult)
+            else:
+                nc.scalar.activation(out=sq[:], in_=sin_h[:], func=ACT.Square, scale=math.sqrt(2.0))
             return sin_d, sq
 
         def gain_sine(b, width, sin_d, z):
@@ -293,7 +302,7 @@ def tile_list_islanding_separation_kernel(
                                       scales=w4_sc[:].rearrange("p b n -> p (b n)"), in_=w4_bf[:])
 
         steps = [(0, 0, 128), (0, 128, 128), (0, 256, 256), (0, 512, 256), (0, 768, 256),
-                 (1, 0, 256), (1, 256, 256), (1, 512, 256), (1, 768, 128), (1, 896, 128)]
+                 (1, 0, 256), (1, 256, 256), (1, 512, 128), (1, 640, 128), (1, 768, 128), (1, 896, 128)]
         pending = None
         for step, (b, j0, width) in enumerate(steps):
             sin_d, sq = angles(step, b, j0, width)

@@ -28,8 +28,8 @@ ROWS = 16
 QUAD = 32
 V_SC, W2_SC = 0, S
 STAGED = W2_SC + K_PASS
+HALF = 8
 FIRST = 256
-PIECES = 4
 TABLE_BYTES = 4 * T
 PICKED_BYTES = 4 * S
 
@@ -57,8 +57,8 @@ def tile_list_islanding_separation_kernel(
         tab_sc = kept([P, T], U8, "tab_sc")
         tab2_sc = kept([P, T], U8, "tab2_sc")
         w2_sc_raw = kept([P, K_PASS], U8, "w2_sc_raw")
-        staged = kept([P, STAGED], U8, "staged")
-        planes = kept([P, 2, STAGED], U8, "planes")
+        planes = kept([P, STAGED], U8, "planes")
+        w2_sc_late = kept([P, K_PASS], U8, "w2_sc_late")
         tab_w = [kept([P, T], I32, "tab_w0")]
         w1_raw = {(0, 0): kept([P, PACK, K_PASS], F32, "w1_raw00")[:]}
         w2_raw = placed([P, 2 * H], U8, "w2_raw", TABLE_BYTES)
@@ -66,7 +66,7 @@ def tile_list_islanding_separation_kernel(
         identity = kept([P, P], F32, "identity")
 
         nc.gpsimd.memset(tab_sc[:].bitcast(I32), 0)
-        nc.gpsimd.memset(planes[:].rearrange("p a c -> p (a c)").bitcast(I32), 0)
+        nc.gpsimd.memset(w2_sc_raw[:].bitcast(I32), 0)
 
         def load_w1(b, a, i0=0, i1=PACK, queue=nc.sync):
             rows = w1[a * K_PASS : (a + 1) * K_PASS, b * K_PASS : (b + 1) * K_PASS]
@@ -76,9 +76,6 @@ def tile_list_islanding_separation_kernel(
         def load_words(tile, words):
             nc.sync.dma_start(out=tile[:], in_=words.rearrange("p t i -> p (t i)").bitcast(I32))
 
-        w2_halves = w2_scales[0].rearrange("q (b c) -> (q b) c", b=BLOCKS).bitcast(I32)
-        nc.scalar.dma_start(out=w2_sc_raw[:].bitcast(I32),
-                          in_=w2_halves.unsqueeze(1).to_broadcast([ROWS * BLOCKS, 4, K_PASS // 4]))
         nc.sync.dma_start(list1[:], offs2)
         for d in (0, 2, 1, 3):
             rows = tab2_scales[0, 4 * d : 4 * d + 4].bitcast(I32)
@@ -87,8 +84,13 @@ def tile_list_islanding_separation_kernel(
                               in_=rows.unsqueeze(0).to_broadcast([QUAD // 4, 4, T // 4]))
         nc.sync.dma_start(list8[:], offs)
         load_w1(0, 0, 0, PACK - 1, queue=nc.scalar)
-        nc.sync.dma_start(out=tab_sc[0:P:4, :].bitcast(I32), in_=tab_scales.rearrange("a q t -> q a t").bitcast(I32))
         load_w1(0, 0, PACK - 1, PACK)
+        for e in range(2):
+            nc.sync.dma_start(out=tab_sc[e:P:HALF, :].bitcast(I32),
+                              in_=tab_scales[:, e:ROWS:2, :].rearrange("a g t -> g a t").bitcast(I32))
+        for e in range(2):
+            nc.sync.dma_start(out=w2_sc_raw[e:P:HALF, :].bitcast(I32),
+                              in_=w2_scales[0, e:ROWS:2, :].rearrange("g (b c) -> g b c", b=BLOCKS).bitcast(I32))
         nc.sync.dma_start(out=w2_raw[:].bitcast(I32), in_=w2_words[0].bitcast(I32))
         load_words(tab_w[0], tab_words[0])
         w1_halves = [kept([P, PACK, K_PASS // 2], F32, "w1_half%d" % h) for h in range(2)]
@@ -110,13 +112,14 @@ def tile_list_islanding_separation_kernel(
 
         v_sc_picked = kept([P, S], U8, "v_sc_picked")
         v2_sc_picked = kept([P, S], U8, "v2_sc_picked")
-        nc.vector.tensor_copy(out=staged[:, W2_SC : W2_SC + K_PASS].rearrange("p (t m) -> p t m", t=PACK),
-                              in_=w2_sc_raw[:].rearrange("p (m t) -> p t m", t=PACK))
         pick(v2_sc_picked[:], tab2_sc[:], list1, 0, S)
         pick(v_sc_picked[:], tab_sc[:], list8, 0, S)
-        nc.vector.tensor_copy(out=staged[:, V_SC : V_SC + S].bitcast(I32), in_=v_sc_picked[:].bitcast(I32))
-        for q in range(0, P, QUAD):
-            nc.scalar.dma_start(out=planes[q : q + 4, :, :].bitcast(I32), in_=staged[q : q + QUAD : 4, :].bitcast(I32))
+        nc.vector.tensor_copy(out=planes[:, W2_SC : W2_SC + K_PASS].rearrange("p (t m) -> p t m", t=PACK),
+                              in_=w2_sc_raw[:].rearrange("p (m t) -> p t m", t=PACK))
+        nc.vector.tensor_copy(out=planes[:, V_SC : V_SC + S].bitcast(I32), in_=v_sc_picked[:].bitcast(I32))
+        for row in (0, HALF, 1, HALF + 1):
+            nc.scalar.dma_start(out=planes[row + 2 : P : QUAD, :].bitcast(I32),
+                                in_=planes[row + 16 : P : QUAD, :].bitcast(I32))
 
         w1_codes = {(0, a): kept([P, K_PASS], U32, "w1_codes0%d" % a)[:] for a in range(PASSES)}
         w1_sc = {(0, a): kept([P, K_PASS], U8, "w1_sc0%d" % a)[:] for a in range(PASSES)}
@@ -129,11 +132,7 @@ def tile_list_islanding_separation_kernel(
             if b == 0:
                 nc.scalar.activation(out=dst, in_=src, func=ACT.Copy, scale=-1.0)
             else:
-                dst, src = dst.rearrange("p m i t -> p m t i"), src.rearrange("p m i t -> p m t i")
-                for m0 in range(0, P, P // PIECES):
-                    m = slice(m0, m0 + P // PIECES)
-                    nc.gpsimd.tensor_scalar(out=dst[:, m], in0=src[:, m], scalar1=-1.0, scalar2=0.0,
-                                            op0=ALU.mult, op1=ALU.add)
+                nc.vector.tensor_scalar(out=dst, in0=src, scalar1=-1.0, scalar2=None, op0=ALU.mult)
 
         def quantize_w1(b, a):
             nc.vector.quantize_mx(out=w1_codes[b, a].bitcast(FP8X4), scales=w1_sc[b, a], in_=w1_bf[b, a])
@@ -174,24 +173,20 @@ def tile_list_islanding_separation_kernel(
         w3_w = kept([P, BLOCKS, 2 * N], U8, "w3_w", tag="w1_half1")
         nc.sync.dma_start(out=w3_w[:].bitcast(I32), in_=w3_words.rearrange("b p c -> p b c").bitcast(I32))
 
-        w3_sc = kept([P, BLOCKS, N], U8, "w3_sc", tag="staged")
+        w3_sc = kept([P, BLOCKS, N], U8, "w3_sc", tag="w2_sc_raw")
         nc.gpsimd.memset(w3_sc[:].rearrange("p b n -> p (b n)").bitcast(I32), 0)
         for r in range(4):
             nc.sync.dma_start(out=w3_sc[r:P:QUAD, :, :].bitcast(I32),
                               in_=w3_scales[:, r:ROWS:4, :].rearrange("b d n -> d b n").bitcast(I32))
 
+        nc.gpsimd.memset(w2_sc_late[:].bitcast(I32), 0)
+        for q in range(0, P, QUAD):
+            nc.sync.dma_start(out=w2_sc_late[q : q + 4, :].bitcast(I32),
+                              in_=planes[q + HALF : q + HALF + 4, W2_SC:STAGED].bitcast(I32))
+        w2_sc = [planes[:, W2_SC:STAGED], w2_sc_late[:]]
         w4_bf = kept([P, BLOCKS * N * PACK], BF16, "w4_bf")
         w4_sc = kept([P, BLOCKS, N], U8, "w4_sc")
         late = {}
-        for a in range(PASSES):
-            round_w1(1, a)
-        for b in range(BLOCKS):
-            dst = w4_bf[:, b * N * PACK : (b + 1) * N * PACK].rearrange("p (c i) -> p c i", i=PACK)
-            src = w4_raw[:, b, :, :].rearrange("p i c -> p c i")
-            for c0 in range(0, N, N // 2):
-                c = slice(c0, c0 + N // 2)
-                nc.gpsimd.tensor_scalar(out=dst[:, c], in0=src[:, c], scalar1=1.0, scalar2=0.0,
-                                        op0=ALU.mult, op1=ALU.add)
 
         def angles(step, b, j0, width):
             sin_d = work.tile([P, width * PACK], F32, name="sin_d")
@@ -210,14 +205,14 @@ def tile_list_islanding_separation_kernel(
                         nc.tensor.matmul_mx(
                             out=bank[:, t, :],
                             lhsT=w1_codes[b, a][:, m].bitcast(FP8X4), lhsT_scale=w1_sc[b, a][:, m],
-                            rhs=v_w[a][:, c].bitcast(FP8X4), rhs_scale=planes[:, a, V_SC + j : V_SC + j + JB],
+                            rhs=v_w[a][:, c].bitcast(FP8X4), rhs_scale=planes[HALF * a : P, V_SC + j : V_SC + j + JB],
                             start=(a == 0 and t == 0), stop=False)
                 for t in range(PACK):
                     r0 = b * K_PASS + t * P
                     nc.tensor.matmul_mx(
                         out=bank[:, t, :],
                         lhsT=w2_w[:, 2 * r0 : 2 * (r0 + P)].bitcast(FP4X4),
-                        lhsT_scale=planes[:, b, W2_SC + t * P : W2_SC + (t + 1) * P],
+                        lhsT_scale=w2_sc[b][:, t * P : (t + 1) * P],
                         rhs=v2_w[:, c].bitcast(FP8X4), rhs_scale=v2_sc_picked[:, c],
                         start=False, stop=(t == PACK - 1))
                 cols = slice(jj * JB * PACK, (jj + 1) * JB * PACK)
@@ -226,11 +221,7 @@ def tile_list_islanding_separation_kernel(
                                      func=ACT.Sin, scale=0.5)
                 nc.scalar.activation(out=sin_d[:, cols].rearrange("p (j t) -> p j t", t=PACK), in_=minus_d,
                                      func=ACT.Sin)
-            if step in (0, 1):
-                nc.vector.scalar_tensor_tensor(out=sq[:], in0=sin_h[:], scalar=2.0, in1=sin_h[:],
-                                               op0=ALU.mult, op1=ALU.mult)
-            else:
-                nc.scalar.activation(out=sq[:], in_=sin_h[:], func=ACT.Square, scale=math.sqrt(2.0))
+            nc.scalar.activation(out=sq[:], in_=sin_h[:], func=ACT.Square, scale=math.sqrt(2.0))
             return sin_d, sq
 
         def gain_sine(b, width, sin_d, z):
@@ -289,6 +280,11 @@ def tile_list_islanding_separation_kernel(
             nc.sync.dma_start(out=out[:, j0 : j0 + width].rearrange("(n p) j -> p n j", p=P), in_=res[:])
 
         def side_work(step):
+            if step in (0, 2):
+                round_w1(1, step // 2)
+            if step == 4:
+                nc.vector.tensor_copy(out=w4_bf[:].rearrange("p (b c e i) -> p b c i e", b=BLOCKS, e=4, i=PACK),
+                                      in_=w4_raw[:].rearrange("p b i (c e) -> p b c i e", e=4))
             if step == 3:
                 codes = kept([P, PASSES * K_PASS], U32, "w1_codes_late", tag="sq2")
                 scales = kept([P, PASSES * K_PASS], U8, "w1_sc_late")

@@ -79,11 +79,11 @@ def tile_list_islanding_separation_kernel(
         nc.sync.dma_start(list1[:], offs2)
         for d in (0, 2, 1, 3):
             rows = tab2_scales[0, 4 * d : 4 * d + 4].bitcast(I32)
-            queue = nc.sync if d < 2 else nc.scalar
+            queue = nc.sync if d == 0 else nc.scalar
             queue.dma_start(out=tab2_sc[QUAD * d : QUAD * (d + 1), :].bitcast(I32),
                               in_=rows.unsqueeze(0).to_broadcast([QUAD // 4, 4, T // 4]))
         nc.sync.dma_start(list8[:], offs)
-        load_w1(0, 0, 0, PACK - 1, queue=nc.scalar)
+        load_w1(0, 0, 0, PACK - 1)
         load_w1(0, 0, PACK - 1, PACK)
         for e in range(2):
             nc.sync.dma_start(out=tab_sc[e:P:HALF, :].bitcast(I32),
@@ -155,15 +155,22 @@ def tile_list_islanding_separation_kernel(
             return gain[:, :, row].unsqueeze(1).to_broadcast([P, width, PACK])
 
         quantize_w1(0, 1)
-        v_w.append(placed([P, S], U32, "v_w1", 2 * TABLE_BYTES))
+        v_w.append(placed([P, S - FIRST], U32, "v_w1", 2 * TABLE_BYTES + 4 * FIRST))
         v2_w = placed([P, S], U32, "v2_w", 2 * TABLE_BYTES + PICKED_BYTES)
         pick(v_w[1][:, 0:FIRST], tab_w[1][:].bitcast(U32), list8, 0, FIRST)
-        pick(v_w[1][:, FIRST:S], tab_w[1][:].bitcast(U32), list8, FIRST, S)
+        pick(v_w[1][:, FIRST : S - FIRST], tab_w[1][:].bitcast(U32), list8, FIRST, S - FIRST)
         pick(v2_w[:, 0:FIRST], tab2_w[:].bitcast(U32), list1, 0, FIRST)
         pick(v2_w[:, FIRST:S], tab2_w[:].bitcast(U32), list1, FIRST, S)
+        v_w1_last = placed([P, FIRST], U32, "v_w1_last", TABLE_BYTES)
+        pick(v_w1_last[:], tab_w[1][:].bitcast(U32), list8, S - FIRST, S)
+
+        def v_words(a, j):
+            if a == 1 and j >= S - FIRST:
+                return v_w1_last[:, j - (S - FIRST) : j - (S - FIRST) + JB]
+            return v_w[a][:, j : j + JB]
 
         w1_late = kept([P, PASSES * PACK * K_PASS], F32, "w1_late", tag="tab_w0")
-        w1_bf_late = placed([P, PASSES * PACK * K_PASS], BF16, "w1_bf_late", TABLE_BYTES)
+        w1_bf_late = placed([P, PASSES * PACK * K_PASS], BF16, "w1_bf_late", TABLE_BYTES + 4 * FIRST)
         for a in range(PASSES):
             w1_bf[1, a] = w1_bf_late[:, a * PACK * K_PASS : (a + 1) * PACK * K_PASS]
             w1_raw[1, a] = w1_late[:, a * PACK * K_PASS : (a + 1) * PACK * K_PASS].rearrange("p (i c) -> p i c", i=PACK)
@@ -205,7 +212,7 @@ def tile_list_islanding_separation_kernel(
                         nc.tensor.matmul_mx(
                             out=bank[:, t, :],
                             lhsT=w1_codes[b, a][:, m].bitcast(FP8X4), lhsT_scale=w1_sc[b, a][:, m],
-                            rhs=v_w[a][:, c].bitcast(FP8X4), rhs_scale=planes[HALF * a : P, V_SC + j : V_SC + j + JB],
+                            rhs=v_words(a, j).bitcast(FP8X4), rhs_scale=planes[HALF * a : P, V_SC + j : V_SC + j + JB],
                             start=(a == 0 and t == 0), stop=False)
                 for t in range(PACK):
                     r0 = b * K_PASS + t * P
@@ -283,8 +290,9 @@ def tile_list_islanding_separation_kernel(
             if step in (0, 2):
                 round_w1(1, step // 2)
             if step == 4:
-                nc.vector.tensor_copy(out=w4_bf[:].rearrange("p (b c e i) -> p b c i e", b=BLOCKS, e=4, i=PACK),
-                                      in_=w4_raw[:].rearrange("p b i (c e) -> p b c i e", e=4))
+                for b, copy in enumerate((nc.vector.tensor_copy, nc.scalar.copy)):
+                    copy(out=w4_bf[:, b * N * PACK : (b + 1) * N * PACK].rearrange("p (c e i) -> p c i e", e=4, i=PACK),
+                         in_=w4_raw[:, b, :, :].rearrange("p i (c e) -> p c i e", e=4))
             if step == 3:
                 codes = kept([P, PASSES * K_PASS], U32, "w1_codes_late", tag="sq2")
                 scales = kept([P, PASSES * K_PASS], U8, "w1_sc_late")

@@ -99,7 +99,7 @@ def tile_list_islanding_separation_kernel(
             nc.sync.dma_start(out=w1_halves[h][:], in_=rows.rearrange("(p i) c -> p i c", i=PACK))
         tab_w.append(placed([P, T], I32, "tab_w1", 0))
         load_words(tab_w[1], tab_words[1])
-        nc.gpsimd.memset(gain_rows[:], 0.0)
+        nc.vector.memset(gain_rows[:], 0.0)
         nc.gpsimd.dma_start(out=gain_rows[0:BLOCKS, :], in_=gs.rearrange("(b c) -> b c", b=BLOCKS))
         nc.gpsimd.dma_start(out=gain_rows[BLOCKS : 2 * BLOCKS, :], in_=gc.rearrange("(b c) -> b c", b=BLOCKS))
         make_identity(nc, identity[:])
@@ -180,13 +180,12 @@ def tile_list_islanding_separation_kernel(
         w3_w = kept([P, BLOCKS, 2 * N], U8, "w3_w", tag="w1_half1")
         nc.sync.dma_start(out=w3_w[:].bitcast(I32), in_=w3_words.rearrange("b p c -> p b c").bitcast(I32))
 
-        w3_sc = kept([P, BLOCKS, N], U8, "w3_sc", tag="w2_sc_raw")
-        nc.gpsimd.memset(w3_sc[:].rearrange("p b n -> p (b n)").bitcast(I32), 0)
+        w3_sc = w2_sc_raw[:].rearrange("p (b n) -> p b n", b=BLOCKS)
         for r in range(4):
             nc.sync.dma_start(out=w3_sc[r:P:QUAD, :, :].bitcast(I32),
                               in_=w3_scales[:, r:ROWS:4, :].rearrange("b d n -> d b n").bitcast(I32))
 
-        nc.gpsimd.memset(w2_sc_late[:].bitcast(I32), 0)
+        nc.vector.memset(w2_sc_late[:].bitcast(I32), 0)
         for q in range(0, P, QUAD):
             nc.sync.dma_start(out=w2_sc_late[q : q + 4, :].bitcast(I32),
                               in_=planes[q + HALF : q + HALF + 4, W2_SC:STAGED].bitcast(I32))

@@ -2,7 +2,6 @@ import math
 from contextlib import ExitStack
 
 import concourse.mybir as mybir
-from concourse.masks import make_identity
 
 K, K2, T, S, H, N = 1024, 512, 2048, 1024, 1024, 256
 FLOPS = 2 * S * (K * H + K2 * H + 2 * H * N)
@@ -24,14 +23,23 @@ K_PASS = P * PACK
 PASSES = K // K_PASS
 BLOCKS = H // K_PASS
 JB = 128
+WIDE = 256
 ROWS = 16
 QUAD = 32
-V_SC, W2_SC = 0, S
-STAGED = W2_SC + K_PASS
 HALF = 8
-FIRST = 256
-TABLE_BYTES = 4 * T
-PICKED_BYTES = 4 * S
+W2_SC = S
+STAGED = W2_SC + K_PASS
+BIG = 4 * T
+SLOT = 16 * WIDE
+STEPS = [(0, 0, JB), (0, JB, JB), (0, 256, WIDE), (0, 512, WIDE), (0, 768, WIDE),
+         (1, 256, WIDE), (1, 512, WIDE), (1, 768, WIDE), (1, 0, JB), (1, JB, JB)]
+LAST = len(STEPS) - 1
+W1_STEP, W4_STEP = 2, 3
+HELD = 5
+W2_RAW = BIG
+W4_RAW = 2 * BIG + BIG // 8
+HALVES = W4_RAW + BIG
+SLOTS = HALVES + 2 * BIG + BIG // 4
 
 
 def tile_list_islanding_separation_kernel(
@@ -42,15 +50,18 @@ def tile_list_islanding_separation_kernel(
     with ExitStack() as ctx:
         keep = ctx.enter_context(tc.tile_pool(name="keep", bufs=1))
         shared = ctx.enter_context(tc.tile_pool(name="shared", bufs=1))
-        work = ctx.enter_context(tc.tile_pool(name="work", bufs=5))
+        work = ctx.enter_context(tc.tile_pool(name="work", bufs=4))
         psum_d = ctx.enter_context(tc.psum_pool(name="psum_d", bufs=3))
         psum_y = ctx.enter_context(tc.psum_pool(name="psum_y", bufs=2))
 
-        def kept(shape, dtype, name, tag=None):
-            return keep.tile(shape, dtype, name=name, tag=tag or name, align_bytes=64)
+        def kept(shape, dtype, name):
+            return keep.tile(shape, dtype, name=name, align_bytes=64)
 
         def placed(shape, dtype, name, offset):
             return shared.tile(shape, dtype, name=name, align_bytes=64, offset=offset)
+
+        def slot(step):
+            return SLOTS + step * SLOT + (3 * SLOT // 4 if step > 1 else 0) + (SLOT // 2 if step > 2 else 0)
 
         list8 = keep.tile([P, S // 16], U16, name="list8")
         list1 = keep.tile([P, S // 16], U16, name="list1")
@@ -58,20 +69,12 @@ def tile_list_islanding_separation_kernel(
         tab2_sc = kept([P, T], U8, "tab2_sc")
         w2_sc_raw = kept([P, K_PASS], U8, "w2_sc_raw")
         planes = kept([P, STAGED], U8, "planes")
-        w2_sc_late = kept([P, K_PASS], U8, "w2_sc_late")
-        tab_w = [kept([P, T], I32, "tab_w0")]
-        w1_raw = {(0, 0): kept([P, PACK, K_PASS], F32, "w1_raw00")[:]}
-        w2_raw = placed([P, 2 * H], U8, "w2_raw", TABLE_BYTES)
-        gain_rows = kept([P, K_PASS], F32, "gain_rows")
-        identity = kept([P, P], F32, "identity")
+        for tile in (tab_sc, w2_sc_raw):
+            nc.vector.memset(tile[:].bitcast(I32), 0)
 
-        nc.gpsimd.memset(tab_sc[:].bitcast(I32), 0)
-        nc.gpsimd.memset(w2_sc_raw[:].bitcast(I32), 0)
-
-        def load_w1(b, a, i0=0, i1=PACK, queue=nc.sync):
-            rows = w1[a * K_PASS : (a + 1) * K_PASS, b * K_PASS : (b + 1) * K_PASS]
-            rows = rows.rearrange("(p i) c -> p i c", i=PACK)
-            queue.dma_start(out=w1_raw[b, a][:, i0:i1, :], in_=rows[:, i0:i1, :])
+        def load_w1(tile, b, a, c0=0, c1=K_PASS):
+            rows = w1[a * K_PASS : (a + 1) * K_PASS, b * K_PASS + c0 : b * K_PASS + c1]
+            nc.sync.dma_start(out=tile[:], in_=rows.rearrange("(p i) c -> p i c", i=PACK))
 
         def load_words(tile, words):
             nc.sync.dma_start(out=tile[:], in_=words.rearrange("p t i -> p (t i)").bitcast(I32))
@@ -81,146 +84,123 @@ def tile_list_islanding_separation_kernel(
             rows = tab2_scales[0, 4 * d : 4 * d + 4].bitcast(I32)
             queue = nc.sync if d == 0 else nc.scalar
             queue.dma_start(out=tab2_sc[QUAD * d : QUAD * (d + 1), :].bitcast(I32),
-                              in_=rows.unsqueeze(0).to_broadcast([QUAD // 4, 4, T // 4]))
+                            in_=rows.unsqueeze(0).to_broadcast([QUAD // 4, 4, T // 4]))
         nc.sync.dma_start(list8[:], offs)
-        load_w1(0, 0, 0, PACK - 1)
-        load_w1(0, 0, PACK - 1, PACK)
+        w1_first = kept([P, PACK, K_PASS], F32, "w1_first")
+        load_w1(w1_first, 0, 0)
         for e in range(2):
             nc.sync.dma_start(out=tab_sc[e:P:HALF, :].bitcast(I32),
                               in_=tab_scales[:, e:ROWS:2, :].rearrange("a g t -> g a t").bitcast(I32))
         for e in range(2):
             nc.sync.dma_start(out=w2_sc_raw[e:P:HALF, :].bitcast(I32),
                               in_=w2_scales[0, e:ROWS:2, :].rearrange("g (b c) -> g b c", b=BLOCKS).bitcast(I32))
-        nc.sync.dma_start(out=w2_raw[:].bitcast(I32), in_=w2_words[0].bitcast(I32))
+        tab_w = [placed([P, T], I32, "tab_w0", 0), kept([P, T], I32, "tab_w1")]
+        w2_raw = placed([P, 2 * H], U8, "w2_raw", W2_RAW)
         load_words(tab_w[0], tab_words[0])
-        w1_halves = [kept([P, PACK, K_PASS // 2], F32, "w1_half%d" % h) for h in range(2)]
-        for h in range(2):
-            rows = w1[K_PASS : 2 * K_PASS, h * K_PASS // 2 : (h + 1) * K_PASS // 2]
-            nc.sync.dma_start(out=w1_halves[h][:], in_=rows.rearrange("(p i) c -> p i c", i=PACK))
-        tab_w.append(placed([P, T], I32, "tab_w1", 0))
+        nc.sync.dma_start(out=w2_raw[:].bitcast(I32), in_=w2_words[0].bitcast(I32))
         load_words(tab_w[1], tab_words[1])
-        nc.vector.memset(gain_rows[:], 0.0)
-        nc.gpsimd.dma_start(out=gain_rows[0:BLOCKS, :], in_=gs.rearrange("(b c) -> b c", b=BLOCKS))
-        nc.gpsimd.dma_start(out=gain_rows[BLOCKS : 2 * BLOCKS, :], in_=gc.rearrange("(b c) -> b c", b=BLOCKS))
-        make_identity(nc, identity[:])
-        gain = psum_y.tile([P, PACK, P], F32, name="gain", bufs=1)
-        for t in range(PACK):
-            nc.tensor.transpose(gain[:, t, :], gain_rows[:, t:K_PASS:PACK], identity[:])
+        w1_halves = [placed([P, PACK, K_PASS // 2], F32, "w1_half%d" % h, HALVES + h * (BIG + BIG // 4)) for h in range(2)]
+        for h in range(2):
+            load_w1(w1_halves[h], 0, 1, h * K_PASS // 2, (h + 1) * K_PASS // 2)
 
         def pick(dst, window, offsets, j0, j1):
             nc.vector.tensor_copy(out=dst, in_=window.indirect(offsets[:, j0 // 16 : j1 // 16]))
 
+        def dealt(bf):
+            return bf.rearrange("p (t m i) -> p m i t", t=PACK, i=PACK)
+
+        def by_column(raw):
+            return raw.rearrange("p i (m t) -> p m i t", t=PACK)
+
+        w1_bf = [kept([P, PACK * K_PASS], BF16, "w1_bf0"), placed([P, PACK * K_PASS], BF16, "w1_bf1", W4_RAW)]
+        nc.scalar.activation(out=dealt(w1_bf[0][:]), in_=by_column(w1_first[:]), func=ACT.Copy, scale=-1.0)
+
         v_sc_picked = kept([P, S], U8, "v_sc_picked")
-        v2_sc_picked = kept([P, S], U8, "v2_sc_picked")
-        pick(v2_sc_picked[:], tab2_sc[:], list1, 0, S)
+        v2_sc = kept([P, S], U8, "v2_sc")
+        pick(v2_sc[:], tab2_sc[:], list1, 0, S)
         pick(v_sc_picked[:], tab_sc[:], list8, 0, S)
-        nc.vector.tensor_copy(out=planes[:, W2_SC : W2_SC + K_PASS].rearrange("p (t m) -> p t m", t=PACK),
+        nc.vector.tensor_copy(out=planes[:, W2_SC:STAGED].rearrange("p (t m) -> p t m", t=PACK),
                               in_=w2_sc_raw[:].rearrange("p (m t) -> p t m", t=PACK))
-        nc.vector.tensor_copy(out=planes[:, V_SC : V_SC + S].bitcast(I32), in_=v_sc_picked[:].bitcast(I32))
+        nc.vector.tensor_copy(out=planes[:, 0:S].bitcast(I32), in_=v_sc_picked[:].bitcast(I32))
         for row in (0, HALF, 1, HALF + 1):
             nc.scalar.dma_start(out=planes[row + 2 : P : QUAD, :].bitcast(I32),
                                 in_=planes[row + 16 : P : QUAD, :].bitcast(I32))
 
-        w1_codes = {(0, a): kept([P, K_PASS], U32, "w1_codes0%d" % a)[:] for a in range(PASSES)}
-        w1_sc = {(0, a): kept([P, K_PASS], U8, "w1_sc0%d" % a)[:] for a in range(PASSES)}
-        w1_bf = {(0, 0): kept([P, PACK * K_PASS], BF16, "w1_bf00")[:],
-                 (0, 1): placed([P, PACK * K_PASS], BF16, "w1_bf01", 2 * TABLE_BYTES + PICKED_BYTES // 2)[:]}
+        w1_codes, w1_sc = {}, {}
 
-        def round_w1(b, a):
-            dst = w1_bf[b, a].rearrange("p (t m i) -> p m i t", t=PACK, i=PACK)
-            src = w1_raw[b, a].rearrange("p i (m t) -> p m i t", t=PACK)
-            if b == 0:
-                nc.scalar.activation(out=dst, in_=src, func=ACT.Copy, scale=-1.0)
-            else:
-                nc.vector.tensor_scalar(out=dst, in0=src, scalar1=-1.0, scalar2=None, op0=ALU.mult)
+        def quantize_w1(a):
+            w1_codes[0, a] = kept([P, K_PASS], U32, "w1_codes%d" % a)[:]
+            w1_sc[0, a] = kept([P, K_PASS], U8, "w1_sc%d" % a)[:]
+            nc.vector.quantize_mx(out=w1_codes[0, a].bitcast(FP8X4), scales=w1_sc[0, a], in_=w1_bf[a][:])
 
-        def quantize_w1(b, a):
-            nc.vector.quantize_mx(out=w1_codes[b, a].bitcast(FP8X4), scales=w1_sc[b, a], in_=w1_bf[b, a])
+        quantize_w1(0)
 
         w2_w = kept([P, 2 * H], U8, "w2_w")
-        nc.vector.tensor_copy(out=w2_w[:].bitcast(U16).rearrange("p (b t m) -> p b t m", b=BLOCKS, t=PACK),
-                              in_=w2_raw[:].bitcast(U16).rearrange("p (b m t) -> p b t m", b=BLOCKS, t=PACK))
-        tab2_w = placed([P, T], I32, "tab2_w", TABLE_BYTES)
+        nc.scalar.copy(out=w2_w[:].bitcast(U16).rearrange("p (b t m) -> p b t m", b=BLOCKS, t=PACK),
+                       in_=w2_raw[:].bitcast(U16).rearrange("p (b m t) -> p b t m", b=BLOCKS, t=PACK))
+        tab2_w = placed([P, T], I32, "tab2_w", W2_RAW + BIG // 8)
         load_words(tab2_w, tab2_words[0])
-        v_w = [kept([P, S], U32, "v_w0")]
-        pick(v_w[0][:], tab_w[0][:].bitcast(U32), list8, 0, S)
-        round_w1(0, 0)
-        quantize_w1(0, 0)
         for h in range(2):
-            dst = w1_bf[0, 1].rearrange("p (t m i) -> p m i t", t=PACK, i=PACK)[:, h * P // 2 : (h + 1) * P // 2]
-            nc.scalar.activation(out=dst, in_=w1_halves[h][:].rearrange("p i (m t) -> p m i t", t=PACK),
-                                 func=ACT.Copy, scale=-1.0)
+            nc.scalar.activation(out=dealt(w1_bf[1][:])[:, h * P // 2 : (h + 1) * P // 2],
+                                 in_=by_column(w1_halves[h][:]), func=ACT.Copy, scale=-1.0)
 
-        def gain_of(row, width):
-            return gain[:, :, row].unsqueeze(1).to_broadcast([P, width, PACK])
+        gains = []
+        for side, g in enumerate((gs, gc)):
+            gains.append(placed([P, BLOCKS, PACK], F32, "gain%d" % side, HALVES + 64 * side))
+            nc.sync.dma_start(out=gains[side][:], in_=g.rearrange("(b p t) -> p b t", p=P, t=PACK))
 
-        quantize_w1(0, 1)
-        v_w.append(placed([P, S - FIRST], U32, "v_w1", 2 * TABLE_BYTES + 4 * FIRST))
-        v2_w = placed([P, S], U32, "v2_w", 2 * TABLE_BYTES + PICKED_BYTES)
-        pick(v_w[1][:, 0:FIRST], tab_w[1][:].bitcast(U32), list8, 0, FIRST)
-        pick(v_w[1][:, FIRST : S - FIRST], tab_w[1][:].bitcast(U32), list8, FIRST, S - FIRST)
-        pick(v2_w[:, 0:FIRST], tab2_w[:].bitcast(U32), list1, 0, FIRST)
-        pick(v2_w[:, FIRST:S], tab2_w[:].bitcast(U32), list1, FIRST, S)
-        v_w1_last = placed([P, FIRST], U32, "v_w1_last", TABLE_BYTES)
-        pick(v_w1_last[:], tab_w[1][:].bitcast(U32), list8, S - FIRST, S)
-
-        def v_words(a, j):
-            if a == 1 and j >= S - FIRST:
-                return v_w1_last[:, j - (S - FIRST) : j - (S - FIRST) + JB]
-            return v_w[a][:, j : j + JB]
-
-        w1_late = kept([P, PASSES * PACK * K_PASS], F32, "w1_late", tag="tab_w0")
-        w1_bf_late = placed([P, PASSES * PACK * K_PASS], BF16, "w1_bf_late", TABLE_BYTES + 4 * FIRST)
+        v_w = []
         for a in range(PASSES):
-            w1_bf[1, a] = w1_bf_late[:, a * PACK * K_PASS : (a + 1) * PACK * K_PASS]
-            w1_raw[1, a] = w1_late[:, a * PACK * K_PASS : (a + 1) * PACK * K_PASS].rearrange("p (i c) -> p i c", i=PACK)
-            load_w1(1, a)
-        w4_raw = placed([P, BLOCKS, PACK, N], F32, "w4_raw", 0)
+            v_w.append(kept([P, S], U32, "v_w%d" % a))
+            pick(v_w[a][:], tab_w[a][:].bitcast(U32), list8, 0, S)
+        quantize_w1(1)
+        v2_w = kept([P, S], U32, "v2_w")
+        pick(v2_w[:, 0:WIDE], tab2_w[:].bitcast(U32), list1, 0, WIDE)
+        pick(v2_w[:, WIDE:S], tab2_w[:].bitcast(U32), list1, WIDE, S)
+
+        w1_late = [placed([P, PACK, K_PASS], F32, "w1_late%d" % a, (BIG // 8, HALVES + BIG // 4 + BIG)[a]) for a in range(PASSES)]
+        for a in range(PASSES):
+            load_w1(w1_late[a], 1, a)
+        w4_raw = placed([P, BLOCKS, PACK, N], F32, "w4_raw", W4_RAW)
         nc.sync.dma_start(out=w4_raw[:], in_=w4.rearrange("(b p i) n -> p b i n", p=P, i=PACK))
-        w3_w = kept([P, BLOCKS, 2 * N], U8, "w3_w", tag="w1_half1")
+        w2_sc = [planes[:, W2_SC:STAGED]]
+        w3_w = placed([P, BLOCKS, 2 * N], U8, "w3_w", HALVES + BIG // 8)
         nc.sync.dma_start(out=w3_w[:].bitcast(I32), in_=w3_words.rearrange("b p c -> p b c").bitcast(I32))
 
-        w3_sc = w2_sc_raw[:].rearrange("p (b n) -> p b n", b=BLOCKS)
-        for r in range(4):
-            nc.sync.dma_start(out=w3_sc[r:P:QUAD, :, :].bitcast(I32),
-                              in_=w3_scales[:, r:ROWS:4, :].rearrange("b d n -> d b n").bitcast(I32))
-
-        nc.vector.memset(w2_sc_late[:].bitcast(I32), 0)
-        for q in range(0, P, QUAD):
-            nc.sync.dma_start(out=w2_sc_late[q : q + 4, :].bitcast(I32),
-                              in_=planes[q + HALF : q + HALF + 4, W2_SC:STAGED].bitcast(I32))
-        w2_sc = [planes[:, W2_SC:STAGED], w2_sc_late[:]]
-        w4_bf = kept([P, BLOCKS * N * PACK], BF16, "w4_bf")
         w4_sc = kept([P, BLOCKS, N], U8, "w4_sc")
         late = {}
 
-        def angles(step, b, j0, width):
-            sin_d = work.tile([P, width * PACK], F32, name="sin_d")
-            sin_h = work.tile([P, width * PACK], F32, name="sin_h", bufs=2)
-            if step in (2, 4):
-                sq = kept([P, width * PACK], F32, "sq%d" % step)
-            else:
-                sq = work.tile([P, width * PACK], F32, name="sq")
-            for jj in range(width // JB):
-                j = j0 + jj * JB
-                c = slice(j, j + JB)
-                bank = psum_d.tile([P, PACK, JB], F32, name="bank")
-                for a in range(PASSES):
-                    for t in range(PACK):
-                        m = slice(t * P, (t + 1) * P)
-                        nc.tensor.matmul_mx(
-                            out=bank[:, t, :],
-                            lhsT=w1_codes[b, a][:, m].bitcast(FP8X4), lhsT_scale=w1_sc[b, a][:, m],
-                            rhs=v_words(a, j).bitcast(FP8X4), rhs_scale=planes[HALF * a : P, V_SC + j : V_SC + j + JB],
-                            start=(a == 0 and t == 0), stop=False)
-                for t in range(PACK):
+        def round_late(a, bf):
+            late["w1_bf", a] = bf
+            nc.vector.tensor_scalar(out=dealt(bf[:]), in0=by_column(w1_late[a][:]),
+                                    scalar1=-1.0, scalar2=None, op0=ALU.mult)
+
+        round_late(0, kept([P, PACK * K_PASS], BF16, "w1_bf_late0"))
+
+        def first_pass(bank, kind, b, j, start, stop):
+            c = slice(j, j + JB)
+            for t in range(PACK):
+                m = slice(t * P, (t + 1) * P)
+                if kind < PASSES:
+                    operands = dict(lhsT=w1_codes[b, kind][:, m].bitcast(FP8X4), lhsT_scale=w1_sc[b, kind][:, m],
+                                    rhs=v_w[kind][:, c].bitcast(FP8X4), rhs_scale=planes[HALF * kind : P, c])
+                else:
                     r0 = b * K_PASS + t * P
-                    nc.tensor.matmul_mx(
-                        out=bank[:, t, :],
-                        lhsT=w2_w[:, 2 * r0 : 2 * (r0 + P)].bitcast(FP4X4),
-                        lhsT_scale=w2_sc[b][:, t * P : (t + 1) * P],
-                        rhs=v2_w[:, c].bitcast(FP8X4), rhs_scale=v2_sc_picked[:, c],
-                        start=False, stop=(t == PACK - 1))
+                    operands = dict(lhsT=w2_w[:, 2 * r0 : 2 * (r0 + P)].bitcast(FP4X4), lhsT_scale=w2_sc[b][:, m],
+                                    rhs=v2_w[:, c].bitcast(FP8X4), rhs_scale=v2_sc[:, c])
+                nc.tensor.matmul_mx(out=bank[:, t, :], start=(start and t == 0), stop=(stop and t == PACK - 1),
+                                    **operands)
+
+        def angles(step):
+            b, j0, width = STEPS[step]
+            sin_d = kept([P, width * PACK], F32, "sin_d%d" % step)
+            sq = kept([P, width * PACK], F32, "sq%d" % step)
+            sin_h = placed([P, width * PACK], F32, "sin_h%d" % step, slot(step) + SLOT // 2 - 8 * width)
+            for jj in range(width // JB):
+                bank = psum_d.tile([P, PACK, JB], F32, name="bank")
+                order = ((0, 1, 2), (0, 2, 1), (2, 0, 1))[min(step, 2)]
+                for kind in order:
+                    first_pass(bank, kind, b, j0 + jj * JB, kind == order[0], kind == order[-1])
                 cols = slice(jj * JB * PACK, (jj + 1) * JB * PACK)
                 minus_d = bank[:].rearrange("p t j -> p j t")
                 nc.scalar.activation(out=sin_h[:, cols].rearrange("p (j t) -> p j t", t=PACK), in_=minus_d,
@@ -230,97 +210,118 @@ def tile_list_islanding_separation_kernel(
             nc.scalar.activation(out=sq[:], in_=sin_h[:], func=ACT.Square, scale=math.sqrt(2.0))
             return sin_d, sq
 
-        def gain_sine(b, width, sin_d, z):
+        def gain_of(side, b, width):
+            return gains[side][:, b, :].unsqueeze(1).to_broadcast([P, width, PACK])
+
+        def gain_sine(step, sin_d, z):
+            b, j0, width = STEPS[step]
             nc.vector.tensor_tensor(
                 out=z[:, 0, :].rearrange("p (u c) -> p u c", c=PACK),
                 in0=sin_d[:].rearrange("p (u c) -> p u c", c=PACK),
-                in1=gain_of(b, width), op=ALU.mult)
+                in1=gain_of(0, b, width), op=ALU.mult)
 
-        def gain_cosine(b, width, sq, z):
+        def gain_cosine(step, sq, z):
+            b, j0, width = STEPS[step]
             nc.vector.scalar_tensor_tensor(
                 out=z[:, 1, :].rearrange("p (u c) -> p u c", c=PACK),
                 in0=sq[:].rearrange("p (u c) -> p u c", c=PACK), scalar=1.0,
-                in1=gain_of(BLOCKS + b, width), op0=ALU.subtract, op1=ALU.mult)
+                in1=gain_of(1, b, width), op0=ALU.subtract, op1=ALU.mult)
 
         z_codes, z_sc = {}, {}
 
-        def quantize_z(b, j0, width, z, s0=0, s1=2):
-            codes = kept([P, s1 - s0, width], U32, "z_codes%d_%d_%d" % (b, j0, s0))
-            scales = kept([P, s1 - s0, width], U8, "z_sc%d_%d_%d" % (b, j0, s0))
+        def quantize_z(step, z, s0=0, s1=2):
+            b, j0, width = STEPS[step]
+            name = "z_codes%d_%d" % (step, s0)
+            if step < HELD:
+                codes = placed([P, 2, width], U32, name, slot(step + 1) + SLOT // 2 - 8 * width)
+            else:
+                codes = placed([P, s1 - s0, width], U32, name, HALVES + BIG // 4 + BIG + 8 * j0 + 4 * width * s0)
+            scales = kept([P, s1 - s0, width], U8, "z_sc%d_%d" % (step, s0))
             nc.vector.quantize_mx(out=codes[:].rearrange("p s j -> p (s j)").bitcast(FP8X4),
                                   scales=scales[:].rearrange("p s j -> p (s j)"),
                                   in_=z[:, s0:s1, :].rearrange("p s c -> p (s c)"))
             for s in range(s0, s1):
-                for jj in range(width // JB):
-                    c = slice(jj * JB, (jj + 1) * JB)
-                    z_codes[s, b, j0 + jj * JB] = codes[:, s - s0, c]
-                    z_sc[s, b, j0 + jj * JB] = scales[:, s - s0, c]
+                z_codes[s, b, j0] = codes[:, s - s0, :]
+                z_sc[s, b, j0] = scales[:, s - s0, :]
 
-        def product(side, y, j0, width):
+        def product(side, step):
+            j0, width = STEPS[step][1:]
+            y = psum_y.tile([P, N // P, width], F32, name=("ys", "yc")[side], bufs=2 + side)
             for n in range(N // P):
                 cols = slice(n * P, (n + 1) * P)
-                for jj in range(width // JB):
-                    j = j0 + jj * JB
-                    for b in range(BLOCKS):
-                        if side == 0:
-                            w, w_sc = w3_w[:, b, 2 * n * P : 2 * (n + 1) * P].bitcast(FP4X4), w3_sc[:, b, cols]
-                        else:
-                            w, w_sc = late["w4"][:, b, cols].bitcast(FP8X4), w4_sc[:, b, cols]
-                        nc.tensor.matmul_mx(
-                            out=y[:, n, jj * JB : (jj + 1) * JB], lhsT=w, lhsT_scale=w_sc,
-                            rhs=z_codes[side, b, j].bitcast(FP8X4), rhs_scale=z_sc[side, b, j],
-                            start=(b == 0), stop=(b == BLOCKS - 1))
+                for b in range(BLOCKS):
+                    if side == 0:
+                        w, w_sc = w3_w[:, b, 2 * n * P : 2 * (n + 1) * P].bitcast(FP4X4), late["w3_sc"][:, b, cols]
+                    else:
+                        w, w_sc = late["w4"][:, b, cols].bitcast(FP8X4), w4_sc[:, b, cols]
+                    nc.tensor.matmul_mx(
+                        out=y[:, n, :], lhsT=w, lhsT_scale=w_sc,
+                        rhs=z_codes[side, b, j0].bitcast(FP8X4), rhs_scale=z_sc[side, b, j0],
+                        start=(b == 0), stop=(b == BLOCKS - 1))
+            return y
 
-        def sine_side(j0, width):
-            ys = psum_y.tile([P, N // P, width], F32, name="ys")
-            product(0, ys, j0, width)
-            ys_sb = work.tile([P, N // P, width], F32, name="ys_sb", bufs=2)
+        def copy_out(step, ys):
+            width = STEPS[step][2]
+            name = "ys_sb%d" % step
+            ys_sb = placed([P, N // P, width], F32, name, HALVES + BIG // 4 + 8 * STEPS[step][1])
             nc.scalar.copy(out=ys_sb[:], in_=ys[:])
             return ys_sb
 
-        def cosine_side(j0, width, ys_sb):
-            yc = psum_y.tile([P, N // P, width], F32, name="yc")
-            product(1, yc, j0, width)
-            res = work.tile([P, N // P, width], F32, name="res", bufs=3)
+        def finish(step, ys_sb, yc):
+            j0, width = STEPS[step][1:]
+            res = placed([P, N // P, width], F32, "res%d" % step, 8 * j0)
             nc.vector.tensor_tensor(out=res[:], in0=yc[:], in1=ys_sb[:], op=ALU.mult)
             nc.sync.dma_start(out=out[:, j0 : j0 + width].rearrange("(n p) j -> p n j", p=P), in_=res[:])
 
         def side_work(step):
-            if step in (0, 2):
-                round_w1(1, step // 2)
-            if step == 4:
+            if step == 0:
+                rows = placed([P, 2, K_PASS], U8, "late_sc", slot(0) + SLOT // 4)
+                nc.vector.memset(rows[:].bitcast(I32), 0)
+                for q in range(0, P, QUAD):
+                    nc.sync.dma_start(out=rows[q : q + 4, 0, :].bitcast(I32),
+                                      in_=planes[q + HALF : q + HALF + 4, W2_SC:STAGED].bitcast(I32))
+                w2_sc.append(rows[:, 0, :])
+                late["w3_sc"] = rows[:, 1, :].rearrange("p (b n) -> p b n", b=BLOCKS)
+                for r in range(4):
+                    nc.sync.dma_start(out=late["w3_sc"][r:P:QUAD, :, :].bitcast(I32),
+                                      in_=w3_scales[:, r:ROWS:4, :].rearrange("b d n -> d b n").bitcast(I32))
+            if step == 1:
+                round_late(1, placed([P, PACK * K_PASS], BF16, "w1_bf_late1", slot(step) + SLOT // 2))
+            if step == 2:
+                late["w4_bf"] = placed([P, BLOCKS, N * PACK], BF16, "w4_bf", slot(step) + SLOT // 2)
                 for b, copy in enumerate((nc.vector.tensor_copy, nc.scalar.copy)):
-                    copy(out=w4_bf[:, b * N * PACK : (b + 1) * N * PACK].rearrange("p (c e i) -> p c i e", e=4, i=PACK),
+                    copy(out=late["w4_bf"][:, b, :].rearrange("p (c e i) -> p c i e", e=4, i=PACK),
                          in_=w4_raw[:, b, :, :].rearrange("p i (c e) -> p c i e", e=4))
-            if step == 3:
-                codes = kept([P, PASSES * K_PASS], U32, "w1_codes_late", tag="sq2")
-                scales = kept([P, PASSES * K_PASS], U8, "w1_sc_late")
-                nc.vector.quantize_mx(out=codes[:].bitcast(FP8X4), scales=scales[:], in_=w1_bf_late[:])
-                for a in range(PASSES):
-                    w1_codes[1, a] = codes[:, a * K_PASS : (a + 1) * K_PASS]
-                    w1_sc[1, a] = scales[:, a * K_PASS : (a + 1) * K_PASS]
-            if step == 5:
-                late["w4"] = kept([P, BLOCKS, N], U32, "w4_codes", tag="sq4")
+            if step in (0, W1_STEP):
+                a = step // W1_STEP
+                w1_codes[1, a] = placed([P, K_PASS], U32, "w1_codes_late%d" % a, slot(step) + (SLOT // 2, -SLOT // 4)[a])[:]
+                w1_sc[1, a] = kept([P, K_PASS], U8, "w1_sc_late%d" % a)[:]
+                nc.vector.quantize_mx(out=w1_codes[1, a].bitcast(FP8X4), scales=w1_sc[1, a], in_=late["w1_bf", a][:])
+            if step == W4_STEP:
+                late["w4"] = placed([P, BLOCKS, N], U32, "w4_codes", slot(step) + SLOT // 2)
                 nc.vector.quantize_mx(out=late["w4"][:].rearrange("p b n -> p (b n)").bitcast(FP8X4),
-                                      scales=w4_sc[:].rearrange("p b n -> p (b n)"), in_=w4_bf[:])
+                                      scales=w4_sc[:].rearrange("p b n -> p (b n)"),
+                                      in_=late["w4_bf"][:].rearrange("p b c -> p (b c)"))
 
-        steps = [(0, 0, 128), (0, 128, 128), (0, 256, 256), (0, 512, 256), (0, 768, 256),
-                 (1, 0, 256), (1, 256, 256), (1, 512, 128), (1, 640, 128), (1, 768, 128), (1, 896, 128)]
-        pending = None
-        for step, (b, j0, width) in enumerate(steps):
-            sin_d, sq = angles(step, b, j0, width)
+        z, sums = {}, {}
+        for step in range(LAST + 1):
+            sin_d, sq = angles(step)
+            z[step] = work.tile([P, 2, STEPS[step][2] * PACK], BF16, name="z", align_bytes=64)
+            gain_sine(step, sin_d, z[step])
+            if step < LAST:
+                gain_cosine(step, sq, z[step])
+            if step > 0:
+                quantize_z(step - 1, z[step - 1])
+                if STEPS[step - 1][0] == BLOCKS - 1:
+                    yc = product(1, step - 1)
+                    sums[step - 1] = (product(0, step - 1), yc)
             side_work(step)
-            z = work.tile([P, 2, width * PACK], BF16, name="z", align_bytes=64, bufs=3)
-            gain_sine(b, width, sin_d, z)
-            if step < len(steps) - 1:
-                gain_cosine(b, width, sq, z)
-            if pending is not None:
-                quantize_z(*pending)
-                if pending[0] == BLOCKS - 1:
-                    cosine_side(pending[1], pending[2], sine_side(pending[1], pending[2]))
-            pending = (b, j0, width, z)
-        quantize_z(b, j0, width, z, 0, 1)
-        gain_cosine(b, width, sq, z)
-        ys_sb = sine_side(j0, width)
-        quantize_z(b, j0, width, z, 1, 2)
-        cosine_side(j0, width, ys_sb)
+            for done in sorted(sums):
+                if done <= step - 2 or step >= LAST - 1:
+                    ys, yc = sums.pop(done)
+                    finish(done, copy_out(done, ys), yc)
+        quantize_z(LAST, z[LAST], 0, 1)
+        gain_cosine(LAST, sq, z[LAST])
+        ys_sb = copy_out(LAST, product(0, LAST))
+        quantize_z(LAST, z[LAST], 1, 2)
+        finish(LAST, ys_sb, product(1, LAST))

@@ -35,7 +35,7 @@ STEPS = [(0, 0, JB), (0, JB, JB), (0, 256, WIDE), (0, 512, WIDE), (0, 768, WIDE)
          (1, 256, WIDE), (1, 512, WIDE), (1, 768, WIDE), (1, 0, JB), (1, JB, JB)]
 LAST = len(STEPS) - 1
 W1_STEP, W4_STEP = 2, 3
-HELD = 5
+HELD = 6
 W2_RAW = BIG
 W4_RAW = 2 * BIG + BIG // 8
 HALVES = W4_RAW + BIG
@@ -94,7 +94,7 @@ def tile_list_islanding_separation_kernel(
         for e in range(2):
             nc.sync.dma_start(out=w2_sc_raw[e:P:HALF, :].bitcast(I32),
                               in_=w2_scales[0, e:ROWS:2, :].rearrange("g (b c) -> g b c", b=BLOCKS).bitcast(I32))
-        tab_w = [placed([P, T], I32, "tab_w0", 0), kept([P, T], I32, "tab_w1")]
+        tab_w = [placed([P, T], I32, "tab_w0", 0), placed([P, T], I32, "tab_w1", slot(LAST + 1))]
         w2_raw = placed([P, 2 * H], U8, "w2_raw", W2_RAW)
         load_words(tab_w[0], tab_words[0])
         nc.sync.dma_start(out=w2_raw[:].bitcast(I32), in_=w2_words[0].bitcast(I32))
@@ -155,10 +155,10 @@ def tile_list_islanding_separation_kernel(
             pick(v_w[a][:], tab_w[a][:].bitcast(U32), list8, 0, S)
         quantize_w1(1)
         v2_w = kept([P, S], U32, "v2_w")
-        pick(v2_w[:, 0:WIDE], tab2_w[:].bitcast(U32), list1, 0, WIDE)
-        pick(v2_w[:, WIDE:S], tab2_w[:].bitcast(U32), list1, WIDE, S)
+        for j0, j1 in ((0, JB), (JB, WIDE), (WIDE, S)):
+            pick(v2_w[:, j0:j1], tab2_w[:].bitcast(U32), list1, j0, j1)
 
-        w1_late = [placed([P, PACK, K_PASS], F32, "w1_late%d" % a, (BIG // 8, HALVES + BIG // 4 + BIG)[a]) for a in range(PASSES)]
+        w1_late = [placed([P, PACK, K_PASS], F32, "w1_late%d" % a, (BIG // 8, slot(LAST + 1))[a]) for a in range(PASSES)]
         for a in range(PASSES):
             load_w1(w1_late[a], 1, a)
         w4_raw = placed([P, BLOCKS, PACK, N], F32, "w4_raw", W4_RAW)
@@ -198,7 +198,7 @@ def tile_list_islanding_separation_kernel(
             sin_h = placed([P, width * PACK], F32, "sin_h%d" % step, slot(step) + SLOT // 2 - 8 * width)
             for jj in range(width // JB):
                 bank = psum_d.tile([P, PACK, JB], F32, name="bank")
-                order = ((0, 1, 2), (0, 2, 1), (2, 0, 1))[min(step, 2)]
+                order = (0, 1, 2) if step < 2 else (0, 2, 1)
                 for kind in order:
                     first_pass(bank, kind, b, j0 + jj * JB, kind == order[0], kind == order[-1])
                 cols = slice(jj * JB * PACK, (jj + 1) * JB * PACK)
@@ -289,9 +289,8 @@ def tile_list_islanding_separation_kernel(
                 round_late(1, placed([P, PACK * K_PASS], BF16, "w1_bf_late1", slot(step) + SLOT // 2))
             if step == 2:
                 late["w4_bf"] = placed([P, BLOCKS, N * PACK], BF16, "w4_bf", slot(step) + SLOT // 2)
-                for b, copy in enumerate((nc.vector.tensor_copy, nc.scalar.copy)):
-                    copy(out=late["w4_bf"][:, b, :].rearrange("p (c e i) -> p c i e", e=4, i=PACK),
-                         in_=w4_raw[:, b, :, :].rearrange("p i (c e) -> p c i e", e=4))
+                nc.vector.tensor_copy(out=late["w4_bf"][:].rearrange("p b (c e i) -> p b c i e", e=4, i=PACK),
+                                      in_=w4_raw[:].rearrange("p b i (c e) -> p b c i e", e=4))
             if step in (0, W1_STEP):
                 a = step // W1_STEP
                 w1_codes[1, a] = placed([P, K_PASS], U32, "w1_codes_late%d" % a, slot(step) + (SLOT // 2, -SLOT // 4)[a])[:]
@@ -303,7 +302,7 @@ def tile_list_islanding_separation_kernel(
                                       scales=w4_sc[:].rearrange("p b n -> p (b n)"),
                                       in_=late["w4_bf"][:].rearrange("p b c -> p (b c)"))
 
-        z, sums = {}, {}
+        z, sums, copied = {}, {}, {}
         for step in range(LAST + 1):
             sin_d, sq = angles(step)
             z[step] = work.tile([P, 2, STEPS[step][2] * PACK], BF16, name="z", align_bytes=64)
@@ -316,12 +315,15 @@ def tile_list_islanding_separation_kernel(
                     yc = product(1, step - 1)
                     sums[step - 1] = (product(0, step - 1), yc)
             side_work(step)
-            for done in sorted(sums):
-                if done <= step - 2 or step >= LAST - 1:
-                    ys, yc = sums.pop(done)
-                    finish(done, copy_out(done, ys), yc)
+            if step - 2 in sums:
+                copied[step - 2] = copy_out(step - 2, sums[step - 2][0])
+                if step < LAST:
+                    finish(step - 2, copied[step - 2], sums[step - 2][1])
+        copied[LAST - 1] = copy_out(LAST - 1, sums[LAST - 1][0])
         quantize_z(LAST, z[LAST], 0, 1)
         gain_cosine(LAST, sq, z[LAST])
-        ys_sb = copy_out(LAST, product(0, LAST))
+        copied[LAST] = copy_out(LAST, product(0, LAST))
         quantize_z(LAST, z[LAST], 1, 2)
-        finish(LAST, ys_sb, product(1, LAST))
+        sums[LAST] = (None, product(1, LAST))
+        for step in range(LAST - 2, LAST + 1):
+            finish(step, copied[step], sums[step][1])

@@ -2,6 +2,7 @@ import math
 from contextlib import ExitStack
 
 import concourse.mybir as mybir
+from concourse.masks import make_identity
 
 K, K2, T, S, H, N = 1024, 512, 2048, 1024, 1024, 256
 FLOPS = 2 * S * (K * H + K2 * H + 2 * H * N)
@@ -35,7 +36,7 @@ STEPS = [(0, 0, JB), (0, JB, JB), (0, 256, WIDE), (0, 512, WIDE), (0, 768, WIDE)
          (1, 256, WIDE), (1, 512, WIDE), (1, 768, WIDE), (1, 0, JB), (1, JB, JB)]
 LAST = len(STEPS) - 1
 W1_STEP, W4_STEP = 2, 3
-HELD = 6
+HELD = 0
 W2_RAW = BIG
 W4_RAW = 2 * BIG + BIG // 8
 HALVES = W4_RAW + BIG
@@ -52,7 +53,7 @@ def tile_list_islanding_separation_kernel(
         shared = ctx.enter_context(tc.tile_pool(name="shared", bufs=1))
         work = ctx.enter_context(tc.tile_pool(name="work", bufs=4))
         psum_d = ctx.enter_context(tc.psum_pool(name="psum_d", bufs=3))
-        psum_y = ctx.enter_context(tc.psum_pool(name="psum_y", bufs=2))
+        psum_y = ctx.enter_context(tc.psum_pool(name="psum_y", bufs=4))
 
         def kept(shape, dtype, name):
             return keep.tile(shape, dtype, name=name, align_bytes=64)
@@ -71,6 +72,17 @@ def tile_list_islanding_separation_kernel(
         planes = kept([P, STAGED], U8, "planes")
         for tile in (tab_sc, w2_sc_raw):
             nc.vector.memset(tile[:].bitcast(I32), 0)
+
+        gain_rows = kept([P, K_PASS], F32, "gain_rows")
+        identity = kept([P, P], F32, "identity")
+        nc.vector.memset(gain_rows[:], 0.0)
+        for side, g in enumerate((gs, gc)):
+            nc.gpsimd.dma_start(out=gain_rows[side * BLOCKS : (side + 1) * BLOCKS, :],
+                                in_=g.rearrange("(b c) -> b c", b=BLOCKS))
+        make_identity(nc, identity[:])
+        gain = psum_y.tile([P, PACK, P], F32, name="gain", bufs=1)
+        for t in range(PACK):
+            nc.tensor.transpose(gain[:, t, :], gain_rows[:, t:K_PASS:PACK], identity[:])
 
         def load_w1(tile, b, a, c0=0, c1=K_PASS):
             rows = w1[a * K_PASS : (a + 1) * K_PASS, b * K_PASS + c0 : b * K_PASS + c1]
@@ -144,11 +156,6 @@ def tile_list_islanding_separation_kernel(
             nc.scalar.activation(out=dealt(w1_bf[1][:])[:, h * P // 2 : (h + 1) * P // 2],
                                  in_=by_column(w1_halves[h][:]), func=ACT.Copy, scale=-1.0)
 
-        gains = []
-        for side, g in enumerate((gs, gc)):
-            gains.append(placed([P, BLOCKS, PACK], F32, "gain%d" % side, HALVES + 64 * side))
-            nc.sync.dma_start(out=gains[side][:], in_=g.rearrange("(b p t) -> p b t", p=P, t=PACK))
-
         v_w = []
         for a in range(PASSES):
             v_w.append(kept([P, S], U32, "v_w%d" % a))
@@ -194,11 +201,11 @@ def tile_list_islanding_separation_kernel(
         def angles(step):
             b, j0, width = STEPS[step]
             sin_d = kept([P, width * PACK], F32, "sin_d%d" % step)
-            sq = kept([P, width * PACK], F32, "sq%d" % step)
+            sq = work.tile([P, width * PACK], F32, name="sq", bufs=5)
             sin_h = placed([P, width * PACK], F32, "sin_h%d" % step, slot(step) + SLOT // 2 - 8 * width)
             for jj in range(width // JB):
                 bank = psum_d.tile([P, PACK, JB], F32, name="bank")
-                order = (0, 1, 2) if step < 2 else (0, 2, 1)
+                order = (0, 1, 2) if step == 0 else (0, 2, 1)
                 for kind in order:
                     first_pass(bank, kind, b, j0 + jj * JB, kind == order[0], kind == order[-1])
                 cols = slice(jj * JB * PACK, (jj + 1) * JB * PACK)
@@ -211,7 +218,7 @@ def tile_list_islanding_separation_kernel(
             return sin_d, sq
 
         def gain_of(side, b, width):
-            return gains[side][:, b, :].unsqueeze(1).to_broadcast([P, width, PACK])
+            return gain[:, :, side * BLOCKS + b].unsqueeze(1).to_broadcast([P, width, PACK])
 
         def gain_sine(step, sin_d, z):
             b, j0, width = STEPS[step]
@@ -235,7 +242,7 @@ def tile_list_islanding_separation_kernel(
             if step < HELD:
                 codes = placed([P, 2, width], U32, name, slot(step + 1) + SLOT // 2 - 8 * width)
             else:
-                codes = placed([P, s1 - s0, width], U32, name, HALVES + BIG // 4 + BIG + 8 * j0 + 4 * width * s0)
+                codes = kept([P, s1 - s0, width], U32, name)
             scales = kept([P, s1 - s0, width], U8, "z_sc%d_%d" % (step, s0))
             nc.vector.quantize_mx(out=codes[:].rearrange("p s j -> p (s j)").bitcast(FP8X4),
                                   scales=scales[:].rearrange("p s j -> p (s j)"),
@@ -244,9 +251,10 @@ def tile_list_islanding_separation_kernel(
                 z_codes[s, b, j0] = codes[:, s - s0, :]
                 z_sc[s, b, j0] = scales[:, s - s0, :]
 
-        def product(side, step):
+        def product(side, step, y=None):
             j0, width = STEPS[step][1:]
-            y = psum_y.tile([P, N // P, width], F32, name=("ys", "yc")[side], bufs=2 + side)
+            if y is None:
+                y = psum_y.tile([P, N // P, width], F32, name="y")
             for n in range(N // P):
                 cols = slice(n * P, (n + 1) * P)
                 for b in range(BLOCKS):
@@ -276,7 +284,7 @@ def tile_list_islanding_separation_kernel(
         def side_work(step):
             if step == 0:
                 rows = placed([P, 2, K_PASS], U8, "late_sc", slot(0) + SLOT // 4)
-                nc.vector.memset(rows[:].bitcast(I32), 0)
+                nc.gpsimd.memset(rows[:].bitcast(I32), 0)
                 for q in range(0, P, QUAD):
                     nc.sync.dma_start(out=rows[q : q + 4, 0, :].bitcast(I32),
                                       in_=planes[q + HALF : q + HALF + 4, W2_SC:STAGED].bitcast(I32))
@@ -312,8 +320,13 @@ def tile_list_islanding_separation_kernel(
             if step > 0:
                 quantize_z(step - 1, z[step - 1])
                 if STEPS[step - 1][0] == BLOCKS - 1:
-                    yc = product(1, step - 1)
-                    sums[step - 1] = (product(0, step - 1), yc)
+                    if step == LAST:
+                        both = psum_y.tile([P, 2, N // P, JB], F32, name="y")
+                        yc = product(1, step - 1, both[:, 1])
+                        sums[step - 1] = (product(0, step - 1, both[:, 0]), yc)
+                    else:
+                        yc = product(1, step - 1)
+                        sums[step - 1] = (product(0, step - 1), yc)
             side_work(step)
             if step - 2 in sums:
                 copied[step - 2] = copy_out(step - 2, sums[step - 2][0])

@@ -184,9 +184,8 @@ def tile_list_islanding_separation_kernel(
 
         round_late(0, kept([P, PACK * K_PASS], BF16, "w1_bf_late0"))
 
-        def first_pass(bank, kind, b, j, start, stop):
-            c = slice(j, j + JB)
-            for t in range(PACK):
+        def first_pass(bank, kind, b, c, slices, start, stop):
+            for t in slices:
                 m = slice(t * P, (t + 1) * P)
                 if kind < PASSES:
                     operands = dict(lhsT=w1_codes[b, kind][:, m].bitcast(FP8X4), lhsT_scale=w1_sc[b, kind][:, m],
@@ -195,26 +194,36 @@ def tile_list_islanding_separation_kernel(
                     r0 = b * K_PASS + t * P
                     operands = dict(lhsT=w2_w[:, 2 * r0 : 2 * (r0 + P)].bitcast(FP4X4), lhsT_scale=w2_sc[b][:, m],
                                     rhs=v2_w[:, c].bitcast(FP8X4), rhs_scale=v2_sc[:, c])
-                nc.tensor.matmul_mx(out=bank[:, t, :], start=(start and t == 0), stop=(stop and t == PACK - 1),
-                                    **operands)
+                nc.tensor.matmul_mx(out=bank[:, t - slices[0], :], start=(start and t == slices[0]),
+                                    stop=(stop and t == slices[-1]), **operands)
+
+        def by_bank(values, banks):
+            return values.rearrange("p (h j e) -> p j h e", h=banks, e=PACK // banks)
+
+        def woven(values, banks):
+            return values.rearrange("p (j h e) -> p j h e", h=banks, e=PACK // banks)
 
         def angles(step):
             b, j0, width = STEPS[step]
             sin_d = kept([P, width * PACK], F32, "sin_d%d" % step)
             sq = work.tile([P, width * PACK], F32, name="sq", bufs=5)
             sin_h = placed([P, width * PACK], F32, "sin_h%d" % step, slot(step) + SLOT // 2 - 8 * width)
-            for jj in range(width // JB):
-                bank = psum_d.tile([P, PACK, JB], F32, name="bank")
+            banks = width // JB
+            share = PACK // banks
+            for h in range(banks):
+                bank = psum_d.tile([P, share, width], F32, name="bank")
                 order = (0, 1, 2) if step == 0 else (0, 2, 1)
                 for kind in order:
-                    first_pass(bank, kind, b, j0 + jj * JB, kind == order[0], kind == order[-1])
-                cols = slice(jj * JB * PACK, (jj + 1) * JB * PACK)
-                minus_d = bank[:].rearrange("p t j -> p j t")
-                nc.scalar.activation(out=sin_h[:, cols].rearrange("p (j t) -> p j t", t=PACK), in_=minus_d,
+                    first_pass(bank, kind, b, slice(j0, j0 + width), range(h * share, (h + 1) * share),
+                               kind == order[0], kind == order[-1])
+                cols = slice(h * K_PASS, (h + 1) * K_PASS)
+                minus_d = bank[:].rearrange("p e j -> p j e")
+                nc.scalar.activation(out=sin_h[:, cols].rearrange("p (j e) -> p j e", e=share), in_=minus_d,
                                      func=ACT.Sin, scale=0.5)
-                nc.scalar.activation(out=sin_d[:, cols].rearrange("p (j t) -> p j t", t=PACK), in_=minus_d,
+                nc.scalar.activation(out=sin_d[:, cols].rearrange("p (j e) -> p j e", e=share), in_=minus_d,
                                      func=ACT.Sin)
-            nc.scalar.activation(out=sq[:], in_=sin_h[:], func=ACT.Square, scale=math.sqrt(2.0))
+            nc.scalar.activation(out=woven(sq[:], banks), in_=by_bank(sin_h[:], banks), func=ACT.Square,
+                                 scale=math.sqrt(2.0))
             return sin_d, sq
 
         def gain_of(side, b, width):
@@ -223,9 +232,8 @@ def tile_list_islanding_separation_kernel(
         def gain_sine(step, sin_d, z):
             b, j0, width = STEPS[step]
             nc.vector.tensor_tensor(
-                out=z[:, 0, :].rearrange("p (u c) -> p u c", c=PACK),
-                in0=sin_d[:].rearrange("p (u c) -> p u c", c=PACK),
-                in1=gain_of(0, b, width), op=ALU.mult)
+                out=woven(z[:, 0, :], width // JB), in0=by_bank(sin_d[:], width // JB),
+                in1=gain_of(0, b, width).rearrange("p j (h e) -> p j h e", h=width // JB), op=ALU.mult)
 
         def gain_cosine(step, sq, z):
             b, j0, width = STEPS[step]

@@ -36,10 +36,10 @@ STEPS = [(0, 0, JB), (0, JB, JB), (0, 256, WIDE), (0, 512, WIDE), (0, 768, WIDE)
          (1, 256, WIDE), (1, 512, WIDE), (1, 768, WIDE), (1, 0, JB), (1, JB, JB)]
 LAST = len(STEPS) - 1
 W1_STEP, W4_STEP = 2, 3
-HELD = 0
 W2_RAW = BIG
 W4_RAW = 2 * BIG + BIG // 8
 HALVES = W4_RAW + BIG
+ASIDE = HALVES + BIG + BIG // 4 + BIG // 2
 SLOTS = HALVES + 2 * BIG + BIG // 4
 
 
@@ -84,6 +84,9 @@ def tile_list_islanding_separation_kernel(
         for t in range(PACK):
             nc.tensor.transpose(gain[:, t, :], gain_rows[:, t:K_PASS:PACK], identity[:])
 
+        gain_s = kept([P, BLOCKS, PACK], F32, "gain_s")
+        nc.scalar.copy(out=gain_s[:], in_=gain[:, :, 0:BLOCKS].rearrange("p t b -> p b t"))
+
         def load_w1(tile, b, a, c0=0, c1=K_PASS):
             rows = w1[a * K_PASS : (a + 1) * K_PASS, b * K_PASS + c0 : b * K_PASS + c1]
             nc.sync.dma_start(out=tile[:], in_=rows.rearrange("(p i) c -> p i c", i=PACK))
@@ -107,7 +110,7 @@ def tile_list_islanding_separation_kernel(
             nc.sync.dma_start(out=w2_sc_raw[e:P:HALF, :].bitcast(I32),
                               in_=w2_scales[0, e:ROWS:2, :].rearrange("g (b c) -> g b c", b=BLOCKS).bitcast(I32))
         tab_w = [placed([P, T], I32, "tab_w0", 0), placed([P, T], I32, "tab_w1", slot(LAST + 1))]
-        w2_raw = placed([P, 2 * H], U8, "w2_raw", W2_RAW)
+        w2_raw = kept([P, 2 * H], U8, "w2_raw")
         load_words(tab_w[0], tab_words[0])
         nc.sync.dma_start(out=w2_raw[:].bitcast(I32), in_=w2_words[0].bitcast(I32))
         load_words(tab_w[1], tab_words[1])
@@ -124,10 +127,10 @@ def tile_list_islanding_separation_kernel(
         def by_column(raw):
             return raw.rearrange("p i (m t) -> p m i t", t=PACK)
 
-        w1_bf = [kept([P, PACK * K_PASS], BF16, "w1_bf0"), placed([P, PACK * K_PASS], BF16, "w1_bf1", W4_RAW)]
+        w1_bf = [placed([P, PACK * K_PASS], BF16, "w1_bf0", W2_RAW), placed([P, PACK * K_PASS], BF16, "w1_bf1", W4_RAW)]
         nc.scalar.activation(out=dealt(w1_bf[0][:]), in_=by_column(w1_first[:]), func=ACT.Copy, scale=-1.0)
 
-        v_sc_picked = kept([P, S], U8, "v_sc_picked")
+        v_sc_picked = placed([P, S], U8, "v_sc_picked", slot(LAST + 1) + BIG)
         v2_sc = kept([P, S], U8, "v2_sc")
         pick(v2_sc[:], tab2_sc[:], list1, 0, S)
         pick(v_sc_picked[:], tab_sc[:], list8, 0, S)
@@ -141,7 +144,10 @@ def tile_list_islanding_separation_kernel(
         w1_codes, w1_sc = {}, {}
 
         def quantize_w1(a):
-            w1_codes[0, a] = kept([P, K_PASS], U32, "w1_codes%d" % a)[:]
+            if a == 0:
+                w1_codes[0, a] = placed([P, K_PASS], U32, "w1_codes0", slot(LAST + 1) + BIG)[:]
+            else:
+                w1_codes[0, a] = kept([P, K_PASS], U32, "w1_codes1")[:]
             w1_sc[0, a] = kept([P, K_PASS], U8, "w1_sc%d" % a)[:]
             nc.vector.quantize_mx(out=w1_codes[0, a].bitcast(FP8X4), scales=w1_sc[0, a], in_=w1_bf[a][:])
 
@@ -184,8 +190,9 @@ def tile_list_islanding_separation_kernel(
 
         round_late(0, kept([P, PACK * K_PASS], BF16, "w1_bf_late0"))
 
-        def first_pass(bank, kind, b, c, slices, start, stop):
-            for t in slices:
+        def first_pass(bank, kind, b, j, start, stop):
+            c = slice(j, j + JB)
+            for t in range(PACK):
                 m = slice(t * P, (t + 1) * P)
                 if kind < PASSES:
                     operands = dict(lhsT=w1_codes[b, kind][:, m].bitcast(FP8X4), lhsT_scale=w1_sc[b, kind][:, m],
@@ -194,70 +201,78 @@ def tile_list_islanding_separation_kernel(
                     r0 = b * K_PASS + t * P
                     operands = dict(lhsT=w2_w[:, 2 * r0 : 2 * (r0 + P)].bitcast(FP4X4), lhsT_scale=w2_sc[b][:, m],
                                     rhs=v2_w[:, c].bitcast(FP8X4), rhs_scale=v2_sc[:, c])
-                nc.tensor.matmul_mx(out=bank[:, t - slices[0], :], start=(start and t == slices[0]),
-                                    stop=(stop and t == slices[-1]), **operands)
-
-        def by_bank(values, banks):
-            return values.rearrange("p (h j e) -> p j h e", h=banks, e=PACK // banks)
-
-        def woven(values, banks):
-            return values.rearrange("p (j h e) -> p j h e", h=banks, e=PACK // banks)
+                nc.tensor.matmul_mx(out=bank[:, t, :], start=(start and t == 0), stop=(stop and t == PACK - 1),
+                                    **operands)
 
         def angles(step):
             b, j0, width = STEPS[step]
             sin_d = kept([P, width * PACK], F32, "sin_d%d" % step)
             sq = work.tile([P, width * PACK], F32, name="sq", bufs=5)
             sin_h = placed([P, width * PACK], F32, "sin_h%d" % step, slot(step) + SLOT // 2 - 8 * width)
-            banks = width // JB
-            share = PACK // banks
-            for h in range(banks):
-                bank = psum_d.tile([P, share, width], F32, name="bank")
+            for jj in range(width // JB):
+                bank = psum_d.tile([P, PACK, JB], F32, name="bank")
                 order = (0, 1, 2) if step == 0 else (0, 2, 1)
                 for kind in order:
-                    first_pass(bank, kind, b, slice(j0, j0 + width), range(h * share, (h + 1) * share),
-                               kind == order[0], kind == order[-1])
-                cols = slice(h * K_PASS, (h + 1) * K_PASS)
-                minus_d = bank[:].rearrange("p e j -> p j e")
-                nc.scalar.activation(out=sin_h[:, cols].rearrange("p (j e) -> p j e", e=share), in_=minus_d,
+                    first_pass(bank, kind, b, j0 + jj * JB, kind == order[0], kind == order[-1])
+                cols = slice(jj * JB * PACK, (jj + 1) * JB * PACK)
+                minus_d = bank[:].rearrange("p t j -> p j t")
+                nc.scalar.activation(out=sin_h[:, cols].rearrange("p (j t) -> p j t", t=PACK), in_=minus_d,
                                      func=ACT.Sin, scale=0.5)
-                nc.scalar.activation(out=sin_d[:, cols].rearrange("p (j e) -> p j e", e=share), in_=minus_d,
+                nc.scalar.activation(out=sin_d[:, cols].rearrange("p (j t) -> p j t", t=PACK), in_=minus_d,
                                      func=ACT.Sin)
-            nc.scalar.activation(out=woven(sq[:], banks), in_=by_bank(sin_h[:], banks), func=ACT.Square,
-                                 scale=math.sqrt(2.0))
+            nc.scalar.activation(out=sq[:], in_=sin_h[:], func=ACT.Square, scale=math.sqrt(2.0))
             return sin_d, sq
 
         def gain_of(side, b, width):
             return gain[:, :, side * BLOCKS + b].unsqueeze(1).to_broadcast([P, width, PACK])
 
-        def gain_sine(step, sin_d, z):
-            b, j0, width = STEPS[step]
-            nc.vector.tensor_tensor(
-                out=woven(z[:, 0, :], width // JB), in0=by_bank(sin_d[:], width // JB),
-                in1=gain_of(0, b, width).rearrange("p j (h e) -> p j h e", h=width // JB), op=ALU.mult)
+        def by_entry(values):
+            return values.rearrange("p (u c) -> p u c", c=PACK)
 
-        def gain_cosine(step, sq, z):
+        def aside(step):
+            return JB if STEPS[step][2] == WIDE or step == LAST - 1 else 0
+
+        def gain_sine(step, sin_d):
+            b, j0, width = STEPS[step]
+            cut = aside(step) * PACK
+            if step == 1:
+                z[step] = placed([P, 2 * width * PACK], BF16, "z1", ASIDE)
+            else:
+                z[step] = work.tile([P, 2 * width * PACK - cut], BF16, name="z", align_bytes=64)
+            if cut:
+                z_aside[step] = placed([P, cut], BF16, "z_aside%d" % step, ASIDE)
+                nc.gpsimd.tensor_tensor(
+                    out=by_entry(z_aside[step][:]), in0=by_entry(sin_d[:, 0:cut]),
+                    in1=gain_s[:, b, :].unsqueeze(1).to_broadcast([P, aside(step), PACK]), op=ALU.mult)
+            if cut < width * PACK:
+                nc.vector.tensor_tensor(
+                    out=by_entry(z[step][:, 0 : width * PACK - cut]), in0=by_entry(sin_d[:, cut:]),
+                    in1=gain_of(0, b, width - aside(step)), op=ALU.mult)
+
+        def gain_cosine(step, sq):
             b, j0, width = STEPS[step]
             nc.vector.scalar_tensor_tensor(
-                out=z[:, 1, :].rearrange("p (u c) -> p u c", c=PACK),
-                in0=sq[:].rearrange("p (u c) -> p u c", c=PACK), scalar=1.0,
+                out=by_entry(z[step][:, (width - aside(step)) * PACK :]), in0=by_entry(sq[:]), scalar=1.0,
                 in1=gain_of(1, b, width), op0=ALU.subtract, op1=ALU.mult)
 
-        z_codes, z_sc = {}, {}
+        z, z_aside, z_codes, z_sc = {}, {}, {}, {}
 
-        def quantize_z(step, z, s0=0, s1=2):
+        def quantize_z(step, c0, c1, values):
             b, j0, width = STEPS[step]
-            name = "z_codes%d_%d" % (step, s0)
-            if step < HELD:
-                codes = placed([P, 2, width], U32, name, slot(step + 1) + SLOT // 2 - 8 * width)
-            else:
-                codes = kept([P, s1 - s0, width], U32, name)
-            scales = kept([P, s1 - s0, width], U8, "z_sc%d_%d" % (step, s0))
-            nc.vector.quantize_mx(out=codes[:].rearrange("p s j -> p (s j)").bitcast(FP8X4),
-                                  scales=scales[:].rearrange("p s j -> p (s j)"),
-                                  in_=z[:, s0:s1, :].rearrange("p s c -> p (s c)"))
-            for s in range(s0, s1):
-                z_codes[s, b, j0] = codes[:, s - s0, :]
-                z_sc[s, b, j0] = scales[:, s - s0, :]
+            if (0, b, j0) not in z_codes:
+                codes = kept([P, 2 * width], U32, "z_codes%d" % step)
+                scales = kept([P, 2 * width], U8, "z_sc%d" % step)
+                z_codes["all", step], z_sc["all", step] = codes, scales
+                for side in range(2):
+                    z_codes[side, b, j0] = codes[:, side * width : (side + 1) * width]
+                    z_sc[side, b, j0] = scales[:, side * width : (side + 1) * width]
+            nc.vector.quantize_mx(out=z_codes["all", step][:, c0:c1].bitcast(FP8X4), scales=z_sc["all", step][:, c0:c1],
+                                  in_=values)
+
+        def quantize_step(step):
+            quantize_z(step, aside(step), 2 * STEPS[step][2], z[step][:])
+            if aside(step):
+                quantize_z(step, 0, aside(step), z_aside[step][:])
 
         def product(side, step, y=None):
             j0, width = STEPS[step][1:]
@@ -276,11 +291,11 @@ def tile_list_islanding_separation_kernel(
                         start=(b == 0), stop=(b == BLOCKS - 1))
             return y
 
-        def copy_out(step, ys):
+        def copy_out(step, ys, copy):
             width = STEPS[step][2]
             name = "ys_sb%d" % step
             ys_sb = placed([P, N // P, width], F32, name, HALVES + BIG // 4 + 8 * STEPS[step][1])
-            nc.scalar.copy(out=ys_sb[:], in_=ys[:])
+            copy(out=ys_sb[:], in_=ys[:])
             return ys_sb
 
         def finish(step, ys_sb, yc):
@@ -318,33 +333,35 @@ def tile_list_islanding_separation_kernel(
                                       scales=w4_sc[:].rearrange("p b n -> p (b n)"),
                                       in_=late["w4_bf"][:].rearrange("p b c -> p (b c)"))
 
-        z, sums, copied = {}, {}, {}
-        for step in range(LAST + 1):
+        sums, copied = {}, {}
+        for step in range(LAST):
+            b, j0, width = STEPS[step]
             sin_d, sq = angles(step)
-            z[step] = work.tile([P, 2, STEPS[step][2] * PACK], BF16, name="z", align_bytes=64)
-            gain_sine(step, sin_d, z[step])
-            if step < LAST:
-                gain_cosine(step, sq, z[step])
-            if step > 0:
-                quantize_z(step - 1, z[step - 1])
-                if STEPS[step - 1][0] == BLOCKS - 1:
-                    if step == LAST:
-                        both = psum_y.tile([P, 2, N // P, JB], F32, name="y")
-                        yc = product(1, step - 1, both[:, 1])
-                        sums[step - 1] = (product(0, step - 1, both[:, 0]), yc)
-                    else:
-                        yc = product(1, step - 1)
-                        sums[step - 1] = (product(0, step - 1), yc)
+            gain_sine(step, sin_d)
+            due = step - 1 in sums and width == WIDE
+            if due:
+                copied[step - 1] = copy_out(step - 1, sums[step - 1][0], nc.scalar.copy if step == LAST - 2 else nc.vector.tensor_copy)
+            gain_cosine(step, sq)
+            if due:
+                finish(step - 1, copied[step - 1], sums[step - 1][1])
             side_work(step)
-            if step - 2 in sums:
-                copied[step - 2] = copy_out(step - 2, sums[step - 2][0])
-                if step < LAST:
-                    finish(step - 2, copied[step - 2], sums[step - 2][1])
-        copied[LAST - 1] = copy_out(LAST - 1, sums[LAST - 1][0])
-        quantize_z(LAST, z[LAST], 0, 1)
-        gain_cosine(LAST, sq, z[LAST])
-        copied[LAST] = copy_out(LAST, product(0, LAST))
-        quantize_z(LAST, z[LAST], 1, 2)
+            if step < LAST - 1:
+                quantize_step(step)
+            if b == BLOCKS - 1 and step < LAST - 1:
+                yc = product(1, step)
+                sums[step] = (product(0, step), yc)
+        sin_d, sq = angles(LAST)
+        gain_sine(LAST, sin_d)
+        quantize_step(LAST - 1)
+        both = psum_y.tile([P, 2, N // P, JB], F32, name="y")
+        yc = product(1, LAST - 1, both[:, 1])
+        sums[LAST - 1] = (product(0, LAST - 1, both[:, 0]), yc)
+        for step in (LAST - 2, LAST - 1):
+            copied[step] = copy_out(step, sums[step][0], nc.scalar.copy)
+        quantize_z(LAST, 0, JB, z[LAST][:, 0 : JB * PACK])
+        gain_cosine(LAST, sq)
+        copied[LAST] = copy_out(LAST, product(0, LAST), nc.scalar.copy)
+        quantize_z(LAST, JB, 2 * JB, z[LAST][:, JB * PACK :])
         sums[LAST] = (None, product(1, LAST))
         for step in range(LAST - 2, LAST + 1):
             finish(step, copied[step], sums[step][1])

@@ -35,11 +35,13 @@ SLOT = 16 * WIDE
 STEPS = [(0, 0, JB), (0, JB, JB), (0, 256, WIDE), (0, 512, WIDE), (0, 768, WIDE),
          (1, 256, WIDE), (1, 512, WIDE), (1, 768, WIDE), (1, 0, JB), (1, JB, JB)]
 LAST = len(STEPS) - 1
-W1_STEP, W4_STEP = 2, 3
+W1_STEP = 2
 W2_RAW = BIG
 W4_RAW = 2 * BIG + BIG // 8
 HALVES = W4_RAW + BIG
 ASIDE = HALVES + BIG + BIG // 4 + BIG // 2
+ASIDE_STEPS = (6, 7)
+W4_PIECES = 4
 SLOTS = HALVES + 2 * BIG + BIG // 4
 
 
@@ -64,6 +66,9 @@ def tile_list_islanding_separation_kernel(
         def slot(step):
             return SLOTS + step * SLOT + (3 * SLOT // 4 if step > 1 else 0) + (SLOT // 2 if step > 2 else 0)
 
+        def early(piece):
+            return (W2_RAW + BIG // 8, slot(LAST + 1))[piece // 2] + piece % 2 * BIG // 2
+
         list8 = keep.tile([P, S // 16], U16, name="list8")
         list1 = keep.tile([P, S // 16], U16, name="list1")
         tab_sc = kept([P, T], U8, "tab_sc")
@@ -84,8 +89,9 @@ def tile_list_islanding_separation_kernel(
         for t in range(PACK):
             nc.tensor.transpose(gain[:, t, :], gain_rows[:, t:K_PASS:PACK], identity[:])
 
-        gain_s = kept([P, BLOCKS, PACK], F32, "gain_s")
-        nc.scalar.copy(out=gain_s[:], in_=gain[:, :, 0:BLOCKS].rearrange("p t b -> p b t"))
+        gain_s = kept([P, JB * PACK], F32, "gain_s")
+        nc.scalar.copy(out=gain_s[:].rearrange("p (u c) -> p u c", c=PACK),
+                       in_=gain[:, :, BLOCKS - 1].unsqueeze(1).to_broadcast([P, JB, PACK]))
 
         def load_w1(tile, b, a, c0=0, c1=K_PASS):
             rows = w1[a * K_PASS : (a + 1) * K_PASS, b * K_PASS + c0 : b * K_PASS + c1]
@@ -181,6 +187,7 @@ def tile_list_islanding_separation_kernel(
         nc.sync.dma_start(out=w3_w[:].bitcast(I32), in_=w3_words.rearrange("b p c -> p b c").bitcast(I32))
 
         w4_sc = kept([P, BLOCKS, N], U8, "w4_sc")
+        w4_codes = kept([P, BLOCKS, N], U32, "w4_codes")
         late = {}
 
         def round_late(a, bf):
@@ -230,20 +237,21 @@ def tile_list_islanding_separation_kernel(
             return values.rearrange("p (u c) -> p u c", c=PACK)
 
         def aside(step):
-            return JB if STEPS[step][2] == WIDE or step == LAST - 1 else 0
+            return JB if step in ASIDE_STEPS else 0
 
         def gain_sine(step, sin_d):
             b, j0, width = STEPS[step]
             cut = aside(step) * PACK
-            if step == 1:
-                z[step] = placed([P, 2 * width * PACK], BF16, "z1", ASIDE)
+            if step + 1 == ASIDE_STEPS[0]:
+                z[step] = placed([P, 2 * width * PACK], BF16, "z_before", ASIDE)
+            elif step in range(W4_PIECES):
+                z[step] = placed([P, 2 * width * PACK], BF16, "z_early%d" % step, early(step))
             else:
-                z[step] = work.tile([P, 2 * width * PACK - cut], BF16, name="z", align_bytes=64)
+                z[step] = work.tile([P, 2 * width * PACK - cut], BF16, name="z", align_bytes=64, bufs=2)
             if cut:
                 z_aside[step] = placed([P, cut], BF16, "z_aside%d" % step, ASIDE)
                 nc.gpsimd.tensor_tensor(
-                    out=by_entry(z_aside[step][:]), in0=by_entry(sin_d[:, 0:cut]),
-                    in1=gain_s[:, b, :].unsqueeze(1).to_broadcast([P, aside(step), PACK]), op=ALU.mult)
+                    out=z_aside[step][:], in0=sin_d[:, 0:cut], in1=gain_s[:], op=ALU.mult)
             if cut < width * PACK:
                 nc.vector.tensor_tensor(
                     out=by_entry(z[step][:, 0 : width * PACK - cut]), in0=by_entry(sin_d[:, cut:]),
@@ -284,7 +292,7 @@ def tile_list_islanding_separation_kernel(
                     if side == 0:
                         w, w_sc = w3_w[:, b, 2 * n * P : 2 * (n + 1) * P].bitcast(FP4X4), late["w3_sc"][:, b, cols]
                     else:
-                        w, w_sc = late["w4"][:, b, cols].bitcast(FP8X4), w4_sc[:, b, cols]
+                        w, w_sc = w4_codes[:, b, cols].bitcast(FP8X4), w4_sc[:, b, cols]
                     nc.tensor.matmul_mx(
                         out=y[:, n, :], lhsT=w, lhsT_scale=w_sc,
                         rhs=z_codes[side, b, j0].bitcast(FP8X4), rhs_scale=z_sc[side, b, j0],
@@ -304,6 +312,17 @@ def tile_list_islanding_separation_kernel(
             nc.vector.tensor_tensor(out=res[:], in0=yc[:], in1=ys_sb[:], op=ALU.mult)
             nc.sync.dma_start(out=out[:, j0 : j0 + width].rearrange("(n p) j -> p n j", p=P), in_=res[:])
 
+        def round_w4(piece):
+            b, n0 = piece // 2, piece % 2 * P
+            late["w4_bf", piece] = placed([P, P, PACK], BF16, "w4_bf%d" % piece, early(piece))
+            nc.gpsimd.tensor_scalar(out=late["w4_bf", piece][:], in0=w4_raw[:, b, :, n0 : n0 + P].rearrange("p i c -> p c i"),
+                                    scalar1=1.0, scalar2=0.0, op0=ALU.mult, op1=ALU.add)
+
+        def quantize_w4(piece):
+            b, cols = piece // 2, slice(piece % 2 * P, (piece % 2 + 1) * P)
+            nc.vector.quantize_mx(out=w4_codes[:, b, cols].bitcast(FP8X4), scales=w4_sc[:, b, cols],
+                                  in_=late["w4_bf", piece][:].rearrange("p c i -> p (c i)"))
+
         def side_work(step):
             if step == 0:
                 rows = placed([P, 2, K_PASS], U8, "late_sc", slot(0) + SLOT // 4)
@@ -318,20 +337,13 @@ def tile_list_islanding_separation_kernel(
                                       in_=w3_scales[:, r:ROWS:4, :].rearrange("b d n -> d b n").bitcast(I32))
             if step == 1:
                 round_late(1, placed([P, PACK * K_PASS], BF16, "w1_bf_late1", slot(step) + SLOT // 2))
-            if step == 2:
-                late["w4_bf"] = placed([P, BLOCKS, N * PACK], BF16, "w4_bf", slot(step) + SLOT // 2)
-                nc.vector.tensor_copy(out=late["w4_bf"][:].rearrange("p b (c e i) -> p b c i e", e=4, i=PACK),
-                                      in_=w4_raw[:].rearrange("p b i (c e) -> p b c i e", e=4))
             if step in (0, W1_STEP):
                 a = step // W1_STEP
                 w1_codes[1, a] = placed([P, K_PASS], U32, "w1_codes_late%d" % a, slot(step) + (SLOT // 2, -SLOT // 4)[a])[:]
                 w1_sc[1, a] = kept([P, K_PASS], U8, "w1_sc_late%d" % a)[:]
                 nc.vector.quantize_mx(out=w1_codes[1, a].bitcast(FP8X4), scales=w1_sc[1, a], in_=late["w1_bf", a][:])
-            if step == W4_STEP:
-                late["w4"] = placed([P, BLOCKS, N], U32, "w4_codes", slot(step) + SLOT // 2)
-                nc.vector.quantize_mx(out=late["w4"][:].rearrange("p b n -> p (b n)").bitcast(FP8X4),
-                                      scales=w4_sc[:].rearrange("p b n -> p (b n)"),
-                                      in_=late["w4_bf"][:].rearrange("p b c -> p (b c)"))
+            if step - 2 in range(W4_PIECES):
+                quantize_w4(step - 2)
 
         sums, copied = {}, {}
         for step in range(LAST):
@@ -340,13 +352,17 @@ def tile_list_islanding_separation_kernel(
             gain_sine(step, sin_d)
             due = step - 1 in sums and width == WIDE
             if due:
-                copied[step - 1] = copy_out(step - 1, sums[step - 1][0], nc.scalar.copy if step == LAST - 2 else nc.vector.tensor_copy)
+                copied[step - 1] = copy_out(step - 1, sums[step - 1][0], nc.scalar.copy)
             gain_cosine(step, sq)
             if due:
                 finish(step - 1, copied[step - 1], sums[step - 1][1])
             side_work(step)
-            if step < LAST - 1:
+            if step > 0 and STEPS[step - 1][0] == 0:
+                quantize_step(step - 1)
+            if b == BLOCKS - 1 and step < LAST - 1:
                 quantize_step(step)
+            if step - 1 in range(W4_PIECES):
+                round_w4(step - 1)
             if b == BLOCKS - 1 and step < LAST - 1:
                 yc = product(1, step)
                 sums[step] = (product(0, step), yc)

@@ -27,22 +27,21 @@ JB = 128
 WIDE = 256
 ROWS = 16
 QUAD = 32
-HALF = 8
-W2_SC = S
-STAGED = W2_SC + K_PASS
+OCT = 8
+V2_SC = S
+W2_SC = 2 * S
+W3_SC = W2_SC + K_PASS
+STAGED = W3_SC + BLOCKS * N
 BIG = 4 * T
 SLOT = 16 * WIDE
 STEPS = [(0, 0, JB), (0, JB, JB), (0, 256, WIDE), (0, 512, WIDE), (0, 768, WIDE),
          (1, 256, WIDE), (1, 512, WIDE), (1, 768, WIDE), (1, 0, JB), (1, JB, JB)]
 LAST = len(STEPS) - 1
-W1_STEP = 2
-W2_RAW = BIG
-W4_RAW = 2 * BIG + BIG // 8
-HALVES = W4_RAW + BIG
-ASIDE = HALVES + BIG + BIG // 4 + BIG // 2
 ASIDE_STEPS = (6, 7)
 W4_PIECES = 4
-SLOTS = HALVES + 2 * BIG + BIG // 4
+AT_W1, AT_TAB0, AT_TAB1, AT_HALVES, AT_TAB2 = 0, BIG, 2 * BIG, 3 * BIG, 4 * BIG
+AT_SIN = 5 * BIG
+AT_Z = AT_SIN + len(STEPS) * SLOT
 
 
 def tile_list_islanding_separation_kernel(
@@ -63,128 +62,131 @@ def tile_list_islanding_separation_kernel(
         def placed(shape, dtype, name, offset):
             return shared.tile(shape, dtype, name=name, align_bytes=64, offset=offset)
 
-        def slot(step):
-            return SLOTS + step * SLOT + (3 * SLOT // 4 if step > 1 else 0) + (SLOT // 2 if step > 2 else 0)
+        def sin_slot(step):
+            return AT_SIN + step * SLOT
 
-        def early(piece):
-            return (W2_RAW + BIG // 8, slot(LAST + 1))[piece // 2] + piece % 2 * BIG // 2
+        def z_slot(step):
+            return AT_Z + sum(16 * STEPS[s][2] for s in range(step))
 
         list8 = keep.tile([P, S // 16], U16, name="list8")
         list1 = keep.tile([P, S // 16], U16, name="list1")
         tab_sc = kept([P, T], U8, "tab_sc")
         tab2_sc = kept([P, T], U8, "tab2_sc")
         w2_sc_raw = kept([P, K_PASS], U8, "w2_sc_raw")
-        planes = kept([P, STAGED], U8, "planes")
-        for tile in (tab_sc, w2_sc_raw):
-            nc.vector.memset(tile[:].bitcast(I32), 0)
-
+        late_sc = kept([P, STAGED - W2_SC], U8, "late_sc")
         gain_rows = kept([P, K_PASS], F32, "gain_rows")
         identity = kept([P, P], F32, "identity")
-        nc.vector.memset(gain_rows[:], 0.0)
-        for side, g in enumerate((gs, gc)):
-            nc.gpsimd.dma_start(out=gain_rows[side * BLOCKS : (side + 1) * BLOCKS, :],
-                                in_=g.rearrange("(b c) -> b c", b=BLOCKS))
+        for tile in (tab2_sc, w2_sc_raw, late_sc):
+            nc.vector.memset(tile[:].bitcast(I32), 0)
+        nc.gpsimd.memset(tab_sc[:].bitcast(I32), 0)
+        nc.gpsimd.memset(gain_rows[:], 0.0)
+
         make_identity(nc, identity[:])
-        gain = psum_y.tile([P, PACK, P], F32, name="gain", bufs=1)
-        for t in range(PACK):
-            nc.tensor.transpose(gain[:, t, :], gain_rows[:, t:K_PASS:PACK], identity[:])
 
-        gain_s = kept([P, JB * PACK], F32, "gain_s")
-        nc.scalar.copy(out=gain_s[:].rearrange("p (u c) -> p u c", c=PACK),
-                       in_=gain[:, :, BLOCKS - 1].unsqueeze(1).to_broadcast([P, JB, PACK]))
-
-        def load_w1(tile, b, a, c0=0, c1=K_PASS):
-            rows = w1[a * K_PASS : (a + 1) * K_PASS, b * K_PASS + c0 : b * K_PASS + c1]
+        def load_w1(tile, b, a):
+            rows = w1[a * K_PASS : (a + 1) * K_PASS, b * K_PASS : (b + 1) * K_PASS]
             nc.sync.dma_start(out=tile[:], in_=rows.rearrange("(p i) c -> p i c", i=PACK))
 
         def load_words(tile, words):
             nc.sync.dma_start(out=tile[:], in_=words.rearrange("p t i -> p (t i)").bitcast(I32))
 
         nc.sync.dma_start(list1[:], offs2)
-        for d in (0, 2, 1, 3):
-            rows = tab2_scales[0, 4 * d : 4 * d + 4].bitcast(I32)
-            queue = nc.sync if d == 0 else nc.scalar
-            queue.dma_start(out=tab2_sc[QUAD * d : QUAD * (d + 1), :].bitcast(I32),
-                            in_=rows.unsqueeze(0).to_broadcast([QUAD // 4, 4, T // 4]))
         nc.sync.dma_start(list8[:], offs)
-        w1_first = kept([P, PACK, K_PASS], F32, "w1_first")
-        load_w1(w1_first, 0, 0)
-        for e in range(2):
-            nc.sync.dma_start(out=tab_sc[e:P:HALF, :].bitcast(I32),
-                              in_=tab_scales[:, e:ROWS:2, :].rearrange("a g t -> g a t").bitcast(I32))
-        for e in range(2):
-            nc.sync.dma_start(out=w2_sc_raw[e:P:HALF, :].bitcast(I32),
-                              in_=w2_scales[0, e:ROWS:2, :].rearrange("g (b c) -> g b c", b=BLOCKS).bitcast(I32))
-        tab_w = [placed([P, T], I32, "tab_w0", 0), placed([P, T], I32, "tab_w1", slot(LAST + 1))]
         w2_raw = kept([P, 2 * H], U8, "w2_raw")
-        load_words(tab_w[0], tab_words[0])
         nc.sync.dma_start(out=w2_raw[:].bitcast(I32), in_=w2_words[0].bitcast(I32))
+        nc.sync.dma_start(out=tab2_sc[0:P:OCT, :].bitcast(I32), in_=tab2_scales[0].bitcast(I32))
+        nc.sync.dma_start(out=tab_sc[0:P:PACK, :].bitcast(I32),
+                          in_=tab_scales.rearrange("a q t -> q a t").bitcast(I32))
+        nc.sync.dma_start(out=w2_sc_raw[0:P:PACK, :].bitcast(I32),
+                          in_=w2_scales[0].rearrange("q (b c) -> q b c", b=BLOCKS).bitcast(I32))
+        w1_first = placed([P, PACK, K_PASS], F32, "w1_first", AT_W1)
+        load_w1(w1_first, 0, 0)
+        tab_w = [placed([P, T], I32, "tab_w0", AT_TAB0), placed([P, T], I32, "tab_w1", AT_TAB1)]
+        load_words(tab_w[0], tab_words[0])
+        for side, g in enumerate((gs, gc)):
+            nc.sync.dma_start(out=gain_rows[side * BLOCKS : (side + 1) * BLOCKS, :],
+                              in_=g.rearrange("(b c) -> b c", b=BLOCKS))
+        gain = psum_y.tile([P, PACK, P], F32, name="gain", bufs=1)
+        for t in range(PACK):
+            nc.tensor.transpose(gain[:, t, :], gain_rows[:, t:K_PASS:PACK], identity[:])
         load_words(tab_w[1], tab_words[1])
-        w1_halves = [placed([P, PACK, K_PASS // 2], F32, "w1_half%d" % h, HALVES + h * (BIG + BIG // 4)) for h in range(2)]
-        for h in range(2):
-            load_w1(w1_halves[h], 0, 1, h * K_PASS // 2, (h + 1) * K_PASS // 2)
+        w1_second = placed([P, PACK, K_PASS], F32, "w1_second", AT_HALVES)
+        load_w1(w1_second, 0, 1)
 
         def pick(dst, window, offsets, j0, j1):
             nc.vector.tensor_copy(out=dst, in_=window.indirect(offsets[:, j0 // 16 : j1 // 16]))
 
         def dealt(bf):
-            return bf.rearrange("p (t m i) -> p m i t", t=PACK, i=PACK)
+            return bf.rearrange("p (t m i) -> p m i t", m=P, i=PACK)
 
         def by_column(raw):
             return raw.rearrange("p i (m t) -> p m i t", t=PACK)
 
-        w1_bf = [placed([P, PACK * K_PASS], BF16, "w1_bf0", W2_RAW), placed([P, PACK * K_PASS], BF16, "w1_bf1", W4_RAW)]
+        w1_bf = [placed([P, PACK * K_PASS], BF16, "w1_bf0", AT_TAB2), [kept([P, 2 * K_PASS], BF16, "w1_bf1_%d" % h) for h in range(2)]]
         nc.scalar.activation(out=dealt(w1_bf[0][:]), in_=by_column(w1_first[:]), func=ACT.Copy, scale=-1.0)
 
-        v_sc_picked = placed([P, S], U8, "v_sc_picked", slot(LAST + 1) + BIG)
+        v_sc = kept([P, S], U8, "v_sc")
         v2_sc = kept([P, S], U8, "v2_sc")
         pick(v2_sc[:], tab2_sc[:], list1, 0, S)
-        pick(v_sc_picked[:], tab_sc[:], list8, 0, S)
-        nc.vector.tensor_copy(out=planes[:, W2_SC:STAGED].rearrange("p (t m) -> p t m", t=PACK),
+        pick(v_sc[:], tab_sc[:], list8, 0, S)
+        w2_sc_dealt = kept([P, K_PASS], U8, "w2_sc_dealt")
+        nc.vector.tensor_copy(out=w2_sc_dealt[:].rearrange("p (t m) -> p t m", t=PACK),
                               in_=w2_sc_raw[:].rearrange("p (m t) -> p t m", t=PACK))
-        nc.vector.tensor_copy(out=planes[:, 0:S].bitcast(I32), in_=v_sc_picked[:].bitcast(I32))
-        for row in (0, HALF, 1, HALF + 1):
-            nc.scalar.dma_start(out=planes[row + 2 : P : QUAD, :].bitcast(I32),
-                                in_=planes[row + 16 : P : QUAD, :].bitcast(I32))
+        planes = placed([P, STAGED], U8, "planes", AT_W1)
+        for c0, rows in ((V2_SC, v2_sc), (0, v_sc), (W2_SC, w2_sc_dealt)):
+            nc.vector.tensor_copy(out=planes[:, c0 : c0 + rows.shape[1]].bitcast(I32), in_=rows[:].bitcast(I32))
+        for first, c1 in ((0, W3_SC), (PACK, S)):
+            for r in range(1, PACK):
+                nc.scalar.dma_start(out=planes[first + r : P : QUAD, 0:c1].bitcast(I32),
+                                    in_=planes[first + OCT * r : P : QUAD, 0:c1].bitcast(I32))
 
         w1_codes, w1_sc = {}, {}
 
-        def quantize_w1(a):
-            if a == 0:
-                w1_codes[0, a] = placed([P, K_PASS], U32, "w1_codes0", slot(LAST + 1) + BIG)[:]
-            else:
-                w1_codes[0, a] = kept([P, K_PASS], U32, "w1_codes1")[:]
-            w1_sc[0, a] = kept([P, K_PASS], U8, "w1_sc%d" % a)[:]
-            nc.vector.quantize_mx(out=w1_codes[0, a].bitcast(FP8X4), scales=w1_sc[0, a], in_=w1_bf[a][:])
+        def quantize_w1(b, a, codes, bf):
+            w1_codes[b, a] = codes[:]
+            w1_sc[b, a] = kept([P, K_PASS], U8, "w1_sc%d%d" % (b, a))[:]
+            nc.vector.quantize_mx(out=w1_codes[b, a].bitcast(FP8X4), scales=w1_sc[b, a], in_=bf[:])
 
-        quantize_w1(0)
+        quantize_w1(0, 0, kept([P, K_PASS], U32, "w1_codes0"), w1_bf[0])
+        tab2_w = placed([P, T], I32, "tab2_w", AT_TAB2)
+        load_words(tab2_w, tab2_words[0])
 
         w2_w = kept([P, 2 * H], U8, "w2_w")
         nc.scalar.copy(out=w2_w[:].bitcast(U16).rearrange("p (b t m) -> p b t m", b=BLOCKS, t=PACK),
                        in_=w2_raw[:].bitcast(U16).rearrange("p (b m t) -> p b t m", b=BLOCKS, t=PACK))
-        tab2_w = placed([P, T], I32, "tab2_w", W2_RAW + BIG // 8)
-        load_words(tab2_w, tab2_words[0])
-        for h in range(2):
-            nc.scalar.activation(out=dealt(w1_bf[1][:])[:, h * P // 2 : (h + 1) * P // 2],
-                                 in_=by_column(w1_halves[h][:]), func=ACT.Copy, scale=-1.0)
+        gain_s = kept([P, JB * PACK], F32, "gain_s")
+        nc.scalar.copy(out=gain_s[:].rearrange("p (u c) -> p u c", c=PACK),
+                       in_=gain[:, :, BLOCKS - 1].unsqueeze(1).to_broadcast([P, JB, PACK]))
+        nc.scalar.activation(out=dealt(w1_bf[1][0][:]), in_=by_column(w1_second[:])[:, :, :, 0:2], func=ACT.Copy, scale=-1.0)
 
         v_w = []
         for a in range(PASSES):
             v_w.append(kept([P, S], U32, "v_w%d" % a))
             pick(v_w[a][:], tab_w[a][:].bitcast(U32), list8, 0, S)
-        quantize_w1(1)
+        nc.vector.tensor_scalar(out=dealt(w1_bf[1][1][:]), in0=by_column(w1_second[:])[:, :, :, 2:PACK],
+                                scalar1=-1.0, scalar2=None, op0=ALU.mult)
+        w1_codes[0, 1], w1_sc[0, 1] = kept([P, K_PASS], U32, "w1_codes1")[:], kept([P, K_PASS], U8, "w1_sc01")[:]
+        for h in range(2):
+            cols = slice(h * K_PASS // 2, (h + 1) * K_PASS // 2)
+            nc.vector.quantize_mx(out=w1_codes[0, 1][:, cols].bitcast(FP8X4), scales=w1_sc[0, 1][:, cols], in_=w1_bf[1][h][:])
         v2_w = kept([P, S], U32, "v2_w")
         for j0, j1 in ((0, JB), (JB, WIDE), (WIDE, S)):
             pick(v2_w[:, j0:j1], tab2_w[:].bitcast(U32), list1, j0, j1)
 
-        w1_late = [placed([P, PACK, K_PASS], F32, "w1_late%d" % a, (BIG // 8, slot(LAST + 1))[a]) for a in range(PASSES)]
+        nc.sync.dma_start(out=planes[PACK:P:OCT, W3_SC:STAGED].bitcast(I32).rearrange("q (b n) -> q b n", b=BLOCKS),
+                          in_=w3_scales.rearrange("b q n -> q b n").bitcast(I32))
+        w1_late = [placed([P, PACK, K_PASS], F32, "w1_late%d" % a, (AT_TAB0, AT_TAB1)[a]) for a in range(PASSES)]
         for a in range(PASSES):
             load_w1(w1_late[a], 1, a)
-        w4_raw = placed([P, BLOCKS, PACK, N], F32, "w4_raw", W4_RAW)
+        for r in range(PACK):
+            nc.sync.dma_start(out=late_sc[r:P:QUAD, :].bitcast(I32),
+                              in_=planes[PACK + OCT * r : P : QUAD, W2_SC:STAGED].bitcast(I32))
+        w4_raw = placed([P, BLOCKS, PACK, N], F32, "w4_raw", AT_HALVES)
         nc.sync.dma_start(out=w4_raw[:], in_=w4.rearrange("(b p i) n -> p b i n", p=P, i=PACK))
-        w2_sc = [planes[:, W2_SC:STAGED]]
-        w3_w = placed([P, BLOCKS, 2 * N], U8, "w3_w", HALVES + BIG // 8)
+        w3_w = kept([P, BLOCKS, 2 * N], U8, "w3_w")
         nc.sync.dma_start(out=w3_w[:].bitcast(I32), in_=w3_words.rearrange("b p c -> p b c").bitcast(I32))
+        w2_sc = [planes[:, W2_SC:W3_SC], late_sc[:, 0:K_PASS]]
+        w3_sc = late_sc[:, K_PASS:]
 
         w4_sc = kept([P, BLOCKS, N], U8, "w4_sc")
         w4_codes = kept([P, BLOCKS, N], U32, "w4_codes")
@@ -198,24 +200,25 @@ def tile_list_islanding_separation_kernel(
         round_late(0, kept([P, PACK * K_PASS], BF16, "w1_bf_late0"))
 
         def first_pass(bank, kind, b, j, start, stop):
-            c = slice(j, j + JB)
             for t in range(PACK):
                 m = slice(t * P, (t + 1) * P)
                 if kind < PASSES:
                     operands = dict(lhsT=w1_codes[b, kind][:, m].bitcast(FP8X4), lhsT_scale=w1_sc[b, kind][:, m],
-                                    rhs=v_w[kind][:, c].bitcast(FP8X4), rhs_scale=planes[HALF * kind : P, c])
+                                    rhs=v_w[kind][:, j : j + JB].bitcast(FP8X4),
+                                    rhs_scale=planes[PACK * kind : P, j : j + JB])
                 else:
                     r0 = b * K_PASS + t * P
                     operands = dict(lhsT=w2_w[:, 2 * r0 : 2 * (r0 + P)].bitcast(FP4X4), lhsT_scale=w2_sc[b][:, m],
-                                    rhs=v2_w[:, c].bitcast(FP8X4), rhs_scale=v2_sc[:, c])
+                                    rhs=v2_w[:, j : j + JB].bitcast(FP8X4),
+                                    rhs_scale=planes[:, V2_SC + j : V2_SC + j + JB])
                 nc.tensor.matmul_mx(out=bank[:, t, :], start=(start and t == 0), stop=(stop and t == PACK - 1),
                                     **operands)
 
         def angles(step):
             b, j0, width = STEPS[step]
-            sin_d = kept([P, width * PACK], F32, "sin_d%d" % step)
+            sin_d = work.tile([P, width * PACK], F32, name="sin_d", bufs=4)
             sq = work.tile([P, width * PACK], F32, name="sq", bufs=5)
-            sin_h = placed([P, width * PACK], F32, "sin_h%d" % step, slot(step) + SLOT // 2 - 8 * width)
+            sin_h = placed([P, width * PACK], F32, "sin_h%d" % step, sin_slot(step))
             for jj in range(width // JB):
                 bank = psum_d.tile([P, PACK, JB], F32, name="bank")
                 order = (0, 1, 2) if step == 0 else (0, 2, 1)
@@ -239,31 +242,24 @@ def tile_list_islanding_separation_kernel(
         def aside(step):
             return JB if step in ASIDE_STEPS else 0
 
+        z, z_aside, z_codes, z_sc = {}, {}, {}, {}
+
         def gain_sine(step, sin_d):
             b, j0, width = STEPS[step]
             cut = aside(step) * PACK
-            if step + 1 == ASIDE_STEPS[0]:
-                z[step] = placed([P, 2 * width * PACK], BF16, "z_before", ASIDE)
-            elif step in range(W4_PIECES):
-                z[step] = placed([P, 2 * width * PACK], BF16, "z_early%d" % step, early(step))
-            else:
-                z[step] = work.tile([P, 2 * width * PACK - cut], BF16, name="z", align_bytes=64, bufs=2)
+            z[step] = placed([P, 2 * width * PACK - cut], BF16, "z%d" % step, z_slot(step))
             if cut:
-                z_aside[step] = placed([P, cut], BF16, "z_aside%d" % step, ASIDE)
-                nc.gpsimd.tensor_tensor(
-                    out=z_aside[step][:], in0=sin_d[:, 0:cut], in1=gain_s[:], op=ALU.mult)
-            if cut < width * PACK:
-                nc.vector.tensor_tensor(
-                    out=by_entry(z[step][:, 0 : width * PACK - cut]), in0=by_entry(sin_d[:, cut:]),
-                    in1=gain_of(0, b, width - aside(step)), op=ALU.mult)
+                z_aside[step] = placed([P, cut], BF16, "z_aside%d" % step, z_slot(ASIDE_STEPS[0] - 1))
+                nc.gpsimd.tensor_tensor(out=z_aside[step][:], in0=sin_d[:, 0:cut], in1=gain_s[:], op=ALU.mult)
+            nc.vector.tensor_tensor(
+                out=by_entry(z[step][:, 0 : width * PACK - cut]), in0=by_entry(sin_d[:, cut:]),
+                in1=gain_of(0, b, width - aside(step)), op=ALU.mult)
 
         def gain_cosine(step, sq):
             b, j0, width = STEPS[step]
             nc.vector.scalar_tensor_tensor(
                 out=by_entry(z[step][:, (width - aside(step)) * PACK :]), in0=by_entry(sq[:]), scalar=1.0,
                 in1=gain_of(1, b, width), op0=ALU.subtract, op1=ALU.mult)
-
-        z, z_aside, z_codes, z_sc = {}, {}, {}, {}
 
         def quantize_z(step, c0, c1, values):
             b, j0, width = STEPS[step]
@@ -290,7 +286,8 @@ def tile_list_islanding_separation_kernel(
                 cols = slice(n * P, (n + 1) * P)
                 for b in range(BLOCKS):
                     if side == 0:
-                        w, w_sc = w3_w[:, b, 2 * n * P : 2 * (n + 1) * P].bitcast(FP4X4), late["w3_sc"][:, b, cols]
+                        w = w3_w[:, b, 2 * n * P : 2 * (n + 1) * P].bitcast(FP4X4)
+                        w_sc = w3_sc[:, b * N + n * P : b * N + (n + 1) * P]
                     else:
                         w, w_sc = w4_codes[:, b, cols].bitcast(FP8X4), w4_sc[:, b, cols]
                     nc.tensor.matmul_mx(
@@ -299,22 +296,21 @@ def tile_list_islanding_separation_kernel(
                         start=(b == 0), stop=(b == BLOCKS - 1))
             return y
 
-        def copy_out(step, ys, copy):
-            width = STEPS[step][2]
-            name = "ys_sb%d" % step
-            ys_sb = placed([P, N // P, width], F32, name, HALVES + BIG // 4 + 8 * STEPS[step][1])
-            copy(out=ys_sb[:], in_=ys[:])
+        def copy_out(step, ys):
+            j0, width = STEPS[step][1:]
+            ys_sb = placed([P, N // P, width], F32, "ys_sb%d" % step, AT_TAB2 + 8 * j0)
+            nc.scalar.copy(out=ys_sb[:], in_=ys[:])
             return ys_sb
 
         def finish(step, ys_sb, yc):
             j0, width = STEPS[step][1:]
-            res = placed([P, N // P, width], F32, "res%d" % step, 8 * j0)
+            res = placed([P, N // P, width], F32, "res%d" % step, AT_TAB0 + 8 * j0)
             nc.vector.tensor_tensor(out=res[:], in0=yc[:], in1=ys_sb[:], op=ALU.mult)
             nc.sync.dma_start(out=out[:, j0 : j0 + width].rearrange("(n p) j -> p n j", p=P), in_=res[:])
 
         def round_w4(piece):
             b, n0 = piece // 2, piece % 2 * P
-            late["w4_bf", piece] = placed([P, P, PACK], BF16, "w4_bf%d" % piece, early(piece))
+            late["w4_bf", piece] = placed([P, P, PACK], BF16, "w4_bf%d" % piece, z_slot(piece))
             nc.gpsimd.tensor_scalar(out=late["w4_bf", piece][:], in0=w4_raw[:, b, :, n0 : n0 + P].rearrange("p i c -> p c i"),
                                     scalar1=1.0, scalar2=0.0, op0=ALU.mult, op1=ALU.add)
 
@@ -324,24 +320,11 @@ def tile_list_islanding_separation_kernel(
                                   in_=late["w4_bf", piece][:].rearrange("p c i -> p (c i)"))
 
         def side_work(step):
-            if step == 0:
-                rows = placed([P, 2, K_PASS], U8, "late_sc", slot(0) + SLOT // 4)
-                nc.gpsimd.memset(rows[:].bitcast(I32), 0)
-                for q in range(0, P, QUAD):
-                    nc.sync.dma_start(out=rows[q : q + 4, 0, :].bitcast(I32),
-                                      in_=planes[q + HALF : q + HALF + 4, W2_SC:STAGED].bitcast(I32))
-                w2_sc.append(rows[:, 0, :])
-                late["w3_sc"] = rows[:, 1, :].rearrange("p (b n) -> p b n", b=BLOCKS)
-                for r in range(4):
-                    nc.sync.dma_start(out=late["w3_sc"][r:P:QUAD, :, :].bitcast(I32),
-                                      in_=w3_scales[:, r:ROWS:4, :].rearrange("b d n -> d b n").bitcast(I32))
             if step == 1:
-                round_late(1, placed([P, PACK * K_PASS], BF16, "w1_bf_late1", slot(step) + SLOT // 2))
-            if step in (0, W1_STEP):
-                a = step // W1_STEP
-                w1_codes[1, a] = placed([P, K_PASS], U32, "w1_codes_late%d" % a, slot(step) + (SLOT // 2, -SLOT // 4)[a])[:]
-                w1_sc[1, a] = kept([P, K_PASS], U8, "w1_sc_late%d" % a)[:]
-                nc.vector.quantize_mx(out=w1_codes[1, a].bitcast(FP8X4), scales=w1_sc[1, a], in_=late["w1_bf", a][:])
+                round_late(1, placed([P, PACK * K_PASS], BF16, "w1_bf_late1", sin_slot(step)))
+            if step in (0, 2):
+                a = step // 2
+                quantize_w1(1, a, placed([P, K_PASS], U32, "w1_codes_late%d" % a, sin_slot(step)), late["w1_bf", a])
             if step - 2 in range(W4_PIECES):
                 quantize_w4(step - 2)
 
@@ -352,7 +335,7 @@ def tile_list_islanding_separation_kernel(
             gain_sine(step, sin_d)
             due = step - 1 in sums and width == WIDE
             if due:
-                copied[step - 1] = copy_out(step - 1, sums[step - 1][0], nc.scalar.copy)
+                copied[step - 1] = copy_out(step - 1, sums[step - 1][0])
             gain_cosine(step, sq)
             if due:
                 finish(step - 1, copied[step - 1], sums[step - 1][1])
@@ -373,10 +356,10 @@ def tile_list_islanding_separation_kernel(
         yc = product(1, LAST - 1, both[:, 1])
         sums[LAST - 1] = (product(0, LAST - 1, both[:, 0]), yc)
         for step in (LAST - 2, LAST - 1):
-            copied[step] = copy_out(step, sums[step][0], nc.scalar.copy)
+            copied[step] = copy_out(step, sums[step][0])
         quantize_z(LAST, 0, JB, z[LAST][:, 0 : JB * PACK])
         gain_cosine(LAST, sq)
-        copied[LAST] = copy_out(LAST, product(0, LAST), nc.scalar.copy)
+        copied[LAST] = copy_out(LAST, product(0, LAST))
         quantize_z(LAST, JB, 2 * JB, z[LAST][:, JB * PACK :])
         sums[LAST] = (None, product(1, LAST))
         for step in range(LAST - 2, LAST + 1):

@@ -298,7 +298,8 @@ def tile_list_islanding_separation_kernel(
 
         def copy_out(step, ys):
             j0, width = STEPS[step][1:]
-            ys_sb = placed([P, N // P, width], F32, "ys_sb%d" % step, AT_TAB2 + 8 * j0)
+            held = step + 2 < LAST
+            ys_sb = placed([P, N // P, width], F32, "ys_sb%d" % step, sin_slot(step + 2) if held else AT_TAB2 + 8 * j0)
             nc.scalar.copy(out=ys_sb[:], in_=ys[:])
             return ys_sb
 
@@ -333,12 +334,12 @@ def tile_list_islanding_separation_kernel(
             b, j0, width = STEPS[step]
             sin_d, sq = angles(step)
             gain_sine(step, sin_d)
-            due = step - 1 in sums and width == WIDE
+            due = step - 2 in sums
             if due:
-                copied[step - 1] = copy_out(step - 1, sums[step - 1][0])
+                copied[step - 2] = copy_out(step - 2, sums[step - 2][0])
             gain_cosine(step, sq)
             if due:
-                finish(step - 1, copied[step - 1], sums[step - 1][1])
+                finish(step - 2, copied[step - 2], sums[step - 2][1])
             side_work(step)
             if step > 0 and STEPS[step - 1][0] == 0:
                 quantize_step(step - 1)
@@ -361,6 +362,6 @@ def tile_list_islanding_separation_kernel(
         gain_cosine(LAST, sq)
         copied[LAST] = copy_out(LAST, product(0, LAST))
         quantize_z(LAST, JB, 2 * JB, z[LAST][:, JB * PACK :])
-        sums[LAST] = (None, product(1, LAST))
+        sums[LAST] = (None, product(1, LAST, psum_d.tile([P, N // P, JB], F32, name="bank")))
         for step in range(LAST - 2, LAST + 1):
             finish(step, copied[step], sums[step][1])

@@ -42,6 +42,7 @@ W4_PIECES = 4
 AT_W1, AT_TAB0, AT_TAB1, AT_HALVES, AT_TAB2 = 0, BIG, 2 * BIG, 3 * BIG, 4 * BIG
 AT_SIN = 5 * BIG
 AT_Z = AT_SIN + len(STEPS) * SLOT
+AT_BF = AT_Z + 2 * 16 * S
 
 
 def tile_list_islanding_separation_kernel(
@@ -122,7 +123,8 @@ def tile_list_islanding_separation_kernel(
         def by_column(raw):
             return raw.rearrange("p i (m t) -> p m i t", t=PACK)
 
-        w1_bf = [placed([P, PACK * K_PASS], BF16, "w1_bf0", AT_TAB2), [kept([P, 2 * K_PASS], BF16, "w1_bf1_%d" % h) for h in range(2)]]
+        w1_bf = [placed([P, PACK * K_PASS], BF16, "w1_bf0", AT_TAB2),
+                 [placed([P, 2 * K_PASS], BF16, "w1_bf1_%d" % h, AT_BF + h * BIG // 4) for h in range(2)]]
         nc.scalar.activation(out=dealt(w1_bf[0][:]), in_=by_column(w1_first[:]), func=ACT.Copy, scale=-1.0)
 
         v_sc = kept([P, S], U8, "v_sc")
@@ -183,7 +185,7 @@ def tile_list_islanding_separation_kernel(
                               in_=planes[PACK + OCT * r : P : QUAD, W2_SC:STAGED].bitcast(I32))
         w4_raw = placed([P, BLOCKS, PACK, N], F32, "w4_raw", AT_HALVES)
         nc.sync.dma_start(out=w4_raw[:], in_=w4.rearrange("(b p i) n -> p b i n", p=P, i=PACK))
-        w3_w = kept([P, BLOCKS, 2 * N], U8, "w3_w")
+        w3_w = placed([P, BLOCKS, 2 * N], U8, "w3_w", AT_BF)
         nc.sync.dma_start(out=w3_w[:].bitcast(I32), in_=w3_words.rearrange("b p c -> p b c").bitcast(I32))
         w2_sc = [planes[:, W2_SC:W3_SC], late_sc[:, 0:K_PASS]]
         w3_sc = late_sc[:, K_PASS:]

@@ -41,7 +41,7 @@ ASIDE_STEPS = (6, 7)
 W4_PIECES = 4
 AT_W1, AT_TAB0, AT_TAB1, AT_HALVES, AT_TAB2 = 0, BIG, 2 * BIG, 3 * BIG, 4 * BIG
 AT_SIN = 5 * BIG
-AT_Z = AT_SIN + len(STEPS) * SLOT
+AT_Z = AT_SIN + (len(STEPS) + 1) * SLOT
 AT_BF = AT_Z + 2 * 16 * S
 
 
@@ -64,7 +64,7 @@ def tile_list_islanding_separation_kernel(
             return shared.tile(shape, dtype, name=name, align_bytes=64, offset=offset)
 
         def sin_slot(step):
-            return AT_SIN + step * SLOT
+            return AT_SIN + step * SLOT + (SLOT // 2 if step > 1 else 0)
 
         def z_slot(step):
             return AT_Z + sum(16 * STEPS[s][2] for s in range(step))
@@ -191,7 +191,7 @@ def tile_list_islanding_separation_kernel(
         w3_sc = late_sc[:, K_PASS:]
 
         w4_sc = kept([P, BLOCKS, N], U8, "w4_sc")
-        w4_codes = kept([P, BLOCKS, N], U32, "w4_codes")
+        w4_codes = {}
         late = {}
 
         def round_late(a, bf):
@@ -266,7 +266,12 @@ def tile_list_islanding_separation_kernel(
         def quantize_z(step, c0, c1, values):
             b, j0, width = STEPS[step]
             if (0, b, j0) not in z_codes:
-                codes = kept([P, 2 * width], U32, "z_codes%d" % step)
+                if aside(step):
+                    codes = placed([P, 2 * width], U32, "z_codes%d" % step, sin_slot(step) + SLOT // 2)
+                elif b == 0:
+                    codes = placed([P, 2 * width], U32, "z_codes%d" % step, sin_slot(step + 1) + (PACK * P if step else 0))
+                else:
+                    codes = kept([P, 2 * width], U32, "z_codes%d" % step)
                 scales = kept([P, 2 * width], U8, "z_sc%d" % step)
                 z_codes["all", step], z_sc["all", step] = codes, scales
                 for side in range(2):
@@ -291,7 +296,7 @@ def tile_list_islanding_separation_kernel(
                         w = w3_w[:, b, 2 * n * P : 2 * (n + 1) * P].bitcast(FP4X4)
                         w_sc = w3_sc[:, b * N + n * P : b * N + (n + 1) * P]
                     else:
-                        w, w_sc = w4_codes[:, b, cols].bitcast(FP8X4), w4_sc[:, b, cols]
+                        w, w_sc = w4_codes[2 * b + n][:].bitcast(FP8X4), w4_sc[:, b, cols]
                     nc.tensor.matmul_mx(
                         out=y[:, n, :], lhsT=w, lhsT_scale=w_sc,
                         rhs=z_codes[side, b, j0].bitcast(FP8X4), rhs_scale=z_sc[side, b, j0],
@@ -308,7 +313,7 @@ def tile_list_islanding_separation_kernel(
         def finish(step, ys_sb, yc):
             j0, width = STEPS[step][1:]
             res = placed([P, N // P, width], F32, "res%d" % step, AT_TAB0 + 8 * j0)
-            nc.vector.tensor_tensor(out=res[:], in0=yc[:], in1=ys_sb[:], op=ALU.mult)
+            nc.vector.tensor_tensor(out=res[:], in0=ys_sb[:], in1=yc[:], op=ALU.mult)
             nc.sync.dma_start(out=out[:, j0 : j0 + width].rearrange("(n p) j -> p n j", p=P), in_=res[:])
 
         def round_w4(piece):
@@ -319,15 +324,16 @@ def tile_list_islanding_separation_kernel(
 
         def quantize_w4(piece):
             b, cols = piece // 2, slice(piece % 2 * P, (piece % 2 + 1) * P)
-            nc.vector.quantize_mx(out=w4_codes[:, b, cols].bitcast(FP8X4), scales=w4_sc[:, b, cols],
+            w4_codes[piece] = placed([P, P], U32, "w4_codes%d" % piece, sin_slot(piece + 2))
+            nc.vector.quantize_mx(out=w4_codes[piece][:].bitcast(FP8X4), scales=w4_sc[:, b, cols],
                                   in_=late["w4_bf", piece][:].rearrange("p c i -> p (c i)"))
 
         def side_work(step):
             if step == 1:
-                round_late(1, placed([P, PACK * K_PASS], BF16, "w1_bf_late1", sin_slot(step)))
+                round_late(1, placed([P, PACK * K_PASS], BF16, "w1_bf_late1", sin_slot(step) + SLOT // 4))
             if step in (0, 2):
                 a = step // 2
-                quantize_w1(1, a, placed([P, K_PASS], U32, "w1_codes_late%d" % a, sin_slot(step)), late["w1_bf", a])
+                quantize_w1(1, a, placed([P, K_PASS], U32, "w1_codes_late%d" % a, sin_slot(step) + a * SLOT // 2), late["w1_bf", a])
             if step - 2 in range(W4_PIECES):
                 quantize_w4(step - 2)
 

import math
from contextlib import ExitStack

import concourse.mybir as mybir
from concourse.masks import make_identity

K, K2, T, S, H, N = 1024, 512, 2048, 1024, 1024, 256
FLOPS = 2 * S * (K * H + K2 * H + 2 * H * N)

F32 = mybir.dt.float32
BF16 = mybir.dt.bfloat16
I32 = mybir.dt.int32
U32 = mybir.dt.uint32
U16 = mybir.dt.uint16
U8 = mybir.dt.uint8
FP8X4 = mybir.dt.float8_e4m3fn_x4
FP4X4 = mybir.dt.float4_e2m1fn_x4
ACT = mybir.ActivationFunctionType
ALU = mybir.AluOpType

P = 128
PACK = 4
K_PASS = P * PACK
PASSES = K // K_PASS
BLOCKS = H // K_PASS
JB = 128
WIDE = 256
ROWS = 16
QUAD = 32
OCT = 8
V2_SC = S
W2_SC = 2 * S
W3_SC = W2_SC + K_PASS
STAGED = W3_SC + BLOCKS * N
BIG = 4 * T
SLOT = 16 * WIDE
STEPS = [(0, 0, JB), (0, JB, JB), (0, 256, WIDE), (0, 512, WIDE), (0, 768, WIDE),
         (1, 256, WIDE), (1, 512, WIDE), (1, 768, WIDE), (1, 0, JB), (1, JB, JB)]
LAST = len(STEPS) - 1
ASIDE_STEPS = (6, 7)
W4_PIECES = 4
AT_W1, AT_TAB0, AT_TAB1, AT_HALVES, AT_TAB2 = 0, BIG, 2 * BIG, 3 * BIG, 4 * BIG
AT_SIN = 5 * BIG
AT_Z = AT_SIN + (len(STEPS) + 1) * SLOT
AT_BF = AT_Z + 2 * 16 * S


def tile_list_islanding_separation_kernel(
    tc, tab_words, tab_scales, tab2_words, tab2_scales, offs, offs2, w1,
    w2_words, w2_scales, w3_words, w3_scales, w4, gs, gc, out,
):
    nc = tc.nc
    with ExitStack() as ctx:
        keep = ctx.enter_context(tc.tile_pool(name="keep", bufs=1))
        shared = ctx.enter_context(tc.tile_pool(name="shared", bufs=1))
        work = ctx.enter_context(tc.tile_pool(name="work", bufs=4))
        psum_d = ctx.enter_context(tc.psum_pool(name="psum_d", bufs=3))
        psum_y = ctx.enter_context(tc.psum_pool(name="psum_y", bufs=4))

        def kept(shape, dtype, name):
            return keep.tile(shape, dtype, name=name, align_bytes=64)

        def placed(shape, dtype, name, offset):
            return shared.tile(shape, dtype, name=name, align_bytes=64, offset=offset)

        def sin_slot(step):
            return AT_SIN + step * SLOT + (SLOT // 2 if step > 1 else 0)

        def z_slot(step):
            return AT_Z + sum(16 * STEPS[s][2] for s in range(step))

        list8 = keep.tile([P, S // 16], U16, name="list8")
        list1 = keep.tile([P, S // 16], U16, name="list1")
        tab_sc = kept([P, T], U8, "tab_sc")
        tab2_sc = kept([P, T], U8, "tab2_sc")
        w2_sc_raw = kept([P, K_PASS], U8, "w2_sc_raw")
        late_sc = kept([P, STAGED - W2_SC], U8, "late_sc")
        gain_rows = kept([P, K_PASS], F32, "gain_rows")
        identity = kept([P, P], F32, "identity")
        for tile in (tab2_sc, w2_sc_raw, late_sc):
            nc.vector.memset(tile[:].bitcast(I32), 0)
        nc.gpsimd.memset(tab_sc[:].bitcast(I32), 0)
        nc.gpsimd.memset(gain_rows[:], 0.0)

        make_identity(nc, identity[:])

        def load_w1(tile, b, a):
            rows = w1[a * K_PASS : (a + 1) * K_PASS, b * K_PASS : (b + 1) * K_PASS]
            nc.sync.dma_start(out=tile[:], in_=rows.rearrange("(p i) c -> p i c", i=PACK))

        def load_words(tile, words):
            nc.sync.dma_start(out=tile[:], in_=words.rearrange("p t i -> p (t i)").bitcast(I32))

        nc.sync.dma_start(list1[:], offs2)
        nc.sync.dma_start(list8[:], offs)
        w2_raw = kept([P, 2 * H], U8, "w2_raw")
        nc.sync.dma_start(out=w2_raw[:].bitcast(I32), in_=w2_words[0].bitcast(I32))
        nc.sync.dma_start(out=tab2_sc[0:P:OCT, :].bitcast(I32), in_=tab2_scales[0].bitcast(I32))
        nc.sync.dma_start(out=tab_sc[0:P:PACK, :].bitcast(I32),
                          in_=tab_scales.rearrange("a q t -> q a t").bitcast(I32))
        nc.sync.dma_start(out=w2_sc_raw[0:P:PACK, :].bitcast(I32),
                          in_=w2_scales[0].rearrange("q (b c) -> q b c", b=BLOCKS).bitcast(I32))
        w1_first = placed([P, PACK, K_PASS], F32, "w1_first", AT_W1)
        load_w1(w1_first, 0, 0)
        tab_w = [placed([P, T], I32, "tab_w0", AT_TAB0), placed([P, T], I32, "tab_w1", AT_TAB1)]
        load_words(tab_w[0], tab_words[0])
        for side, g in enumerate((gs, gc)):
            nc.sync.dma_start(out=gain_rows[side * BLOCKS : (side + 1) * BLOCKS, :],
                              in_=g.rearrange("(b c) -> b c", b=BLOCKS))
        gain = psum_y.tile([P, PACK, P], F32, name="gain", bufs=1)
        for t in range(PACK):
            nc.tensor.transpose(gain[:, t, :], gain_rows[:, t:K_PASS:PACK], identity[:])
        load_words(tab_w[1], tab_words[1])
        w1_second = placed([P, PACK, K_PASS], F32, "w1_second", AT_HALVES)
        load_w1(w1_second, 0, 1)

        def pick(dst, window, offsets, j0, j1):
            nc.vector.tensor_copy(out=dst, in_=window.indirect(offsets[:, j0 // 16 : j1 // 16]))

        def dealt(bf):
            return bf.rearrange("p (t m i) -> p m i t", m=P, i=PACK)

        def by_column(raw):
            return raw.rearrange("p i (m t) -> p m i t", t=PACK)

        w1_bf = [placed([P, PACK * K_PASS], BF16, "w1_bf0", AT_TAB2),
                 [placed([P, 2 * K_PASS], BF16, "w1_bf1_%d" % h, AT_BF + h * BIG // 4) for h in range(2)]]
        nc.scalar.activation(out=dealt(w1_bf[0][:]), in_=by_column(w1_first[:]), func=ACT.Copy, scale=-1.0)

        v_sc = kept([P, S], U8, "v_sc")
        v2_sc = kept([P, S], U8, "v2_sc")
        pick(v2_sc[:], tab2_sc[:], list1, 0, S)
        pick(v_sc[:], tab_sc[:], list8, 0, S)
        w2_sc_dealt = kept([P, K_PASS], U8, "w2_sc_dealt")
        nc.vector.tensor_copy(out=w2_sc_dealt[:].rearrange("p (t m) -> p t m", t=PACK),
                              in_=w2_sc_raw[:].rearrange("p (m t) -> p t m", t=PACK))
        planes = placed([P, STAGED], U8, "planes", AT_W1)
        for c0, rows in ((V2_SC, v2_sc), (0, v_sc), (W2_SC, w2_sc_dealt)):
            nc.vector.tensor_copy(out=planes[:, c0 : c0 + rows.shape[1]].bitcast(I32), in_=rows[:].bitcast(I32))
        for first, c1 in ((0, W3_SC), (PACK, S)):
            for r in range(1, PACK):
                nc.scalar.dma_start(out=planes[first + r : P : QUAD, 0:c1].bitcast(I32),
                                    in_=planes[first + OCT * r : P : QUAD, 0:c1].bitcast(I32))

        w1_codes, w1_sc = {}, {}

        def quantize_w1(b, a, codes, bf):
            w1_codes[b, a] = codes[:]
            w1_sc[b, a] = kept([P, K_PASS], U8, "w1_sc%d%d" % (b, a))[:]
            nc.vector.quantize_mx(out=w1_codes[b, a].bitcast(FP8X4), scales=w1_sc[b, a], in_=bf[:])

        quantize_w1(0, 0, kept([P, K_PASS], U32, "w1_codes0"), w1_bf[0])
        tab2_w = placed([P, T], I32, "tab2_w", AT_TAB2)
        load_words(tab2_w, tab2_words[0])

        w2_w = kept([P, 2 * H], U8, "w2_w")
        nc.scalar.copy(out=w2_w[:].bitcast(U16).rearrange("p (b t m) -> p b t m", b=BLOCKS, t=PACK),
                       in_=w2_raw[:].bitcast(U16).rearrange("p (b m t) -> p b t m", b=BLOCKS, t=PACK))
        gain_s = kept([P, JB * PACK], F32, "gain_s")
        nc.scalar.copy(out=gain_s[:].rearrange("p (u c) -> p u c", c=PACK),
                       in_=gain[:, :, BLOCKS - 1].unsqueeze(1).to_broadcast([P, JB, PACK]))
        nc.scalar.activation(out=dealt(w1_bf[1][0][:]), in_=by_column(w1_second[:])[:, :, :, 0:2], func=ACT.Copy, scale=-1.0)

        v_w = []
        for a in range(PASSES):
            v_w.append(kept([P, S], U32, "v_w%d" % a))
            pick(v_w[a][:], tab_w[a][:].bitcast(U32), list8, 0, S)
        nc.vector.tensor_scalar(out=dealt(w1_bf[1][1][:]), in0=by_column(w1_second[:])[:, :, :, 2:PACK],
                                scalar1=-1.0, scalar2=None, op0=ALU.mult)
        w1_codes[0, 1], w1_sc[0, 1] = kept([P, K_PASS], U32, "w1_codes1")[:], kept([P, K_PASS], U8, "w1_sc01")[:]
        for h in range(2):
            cols = slice(h * K_PASS // 2, (h + 1) * K_PASS // 2)
            nc.vector.quantize_mx(out=w1_codes[0, 1][:, cols].bitcast(FP8X4), scales=w1_sc[0, 1][:, cols], in_=w1_bf[1][h][:])
        v2_w = kept([P, S], U32, "v2_w")
        for j0, j1 in ((0, JB), (JB, WIDE), (WIDE, S)):
            pick(v2_w[:, j0:j1], tab2_w[:].bitcast(U32), list1, j0, j1)

        nc.sync.dma_start(out=planes[PACK:P:OCT, W3_SC:STAGED].bitcast(I32).rearrange("q (b n) -> q b n", b=BLOCKS),
                          in_=w3_scales.rearrange("b q n -> q b n").bitcast(I32))
        w1_late = [placed([P, PACK, K_PASS], F32, "w1_late%d" % a, (AT_TAB0, AT_TAB1)[a]) for a in range(PASSES)]
        for a in range(PASSES):
            load_w1(w1_late[a], 1, a)
        for r in range(PACK):
            nc.sync.dma_start(out=late_sc[r:P:QUAD, :].bitcast(I32),
                              in_=planes[PACK + OCT * r : P : QUAD, W2_SC:STAGED].bitcast(I32))
        w4_raw = placed([P, BLOCKS, PACK, N], F32, "w4_raw", AT_HALVES)
        nc.sync.dma_start(out=w4_raw[:], in_=w4.rearrange("(b p i) n -> p b i n", p=P, i=PACK))
        w3_w = placed([P, BLOCKS, 2 * N], U8, "w3_w", AT_BF)
        nc.sync.dma_start(out=w3_w[:].bitcast(I32), in_=w3_words.rearrange("b p c -> p b c").bitcast(I32))
        w2_sc = [planes[:, W2_SC:W3_SC], late_sc[:, 0:K_PASS]]
        w3_sc = late_sc[:, K_PASS:]

        w4_sc = kept([P, BLOCKS, N], U8, "w4_sc")
        w4_codes = {}
        late = {}

        def round_late(a, bf):
            late["w1_bf", a] = bf
            nc.vector.tensor_scalar(out=dealt(bf[:]), in0=by_column(w1_late[a][:]),
                                    scalar1=-1.0, scalar2=None, op0=ALU.mult)

        round_late(0, kept([P, PACK * K_PASS], BF16, "w1_bf_late0"))

        def first_pass(bank, kind, b, j, start, stop):
            for t in range(PACK):
                m = slice(t * P, (t + 1) * P)
                if kind < PASSES:
                    operands = dict(lhsT=w1_codes[b, kind][:, m].bitcast(FP8X4), lhsT_scale=w1_sc[b, kind][:, m],
                                    rhs=v_w[kind][:, j : j + JB].bitcast(FP8X4),
                                    rhs_scale=planes[PACK * kind : P, j : j + JB])
                else:
                    r0 = b * K_PASS + t * P
                    operands = dict(lhsT=w2_w[:, 2 * r0 : 2 * (r0 + P)].bitcast(FP4X4), lhsT_scale=w2_sc[b][:, m],
                                    rhs=v2_w[:, j : j + JB].bitcast(FP8X4),
                                    rhs_scale=planes[:, V2_SC + j : V2_SC + j + JB])
                nc.tensor.matmul_mx(out=bank[:, t, :], start=(start and t == 0), stop=(stop and t == PACK - 1),
                                    **operands)

        def angles(step):
            b, j0, width = STEPS[step]
            sin_d = work.tile([P, width * PACK], F32, name="sin_d", bufs=4)
            sq = work.tile([P, width * PACK], F32, name="sq", bufs=5)
            sin_h = placed([P, width * PACK], F32, "sin_h%d" % step, sin_slot(step))
            for jj in range(width // JB):
                bank = psum_d.tile([P, PACK, JB], F32, name="bank")
                order = (0, 1, 2) if step == 0 else (0, 2, 1)
                for kind in order:
                    first_pass(bank, kind, b, j0 + jj * JB, kind == order[0], kind == order[-1])
                cols = slice(jj * JB * PACK, (jj + 1) * JB * PACK)
                minus_d = bank[:].rearrange("p t j -> p j t")
                nc.scalar.activation(out=sin_h[:, cols].rearrange("p (j t) -> p j t", t=PACK), in_=minus_d,
                                     func=ACT.Sin, scale=0.5)
                nc.scalar.activation(out=sin_d[:, cols].rearrange("p (j t) -> p j t", t=PACK), in_=minus_d,
                                     func=ACT.Sin)
            nc.scalar.activation(out=sq[:], in_=sin_h[:], func=ACT.Square, scale=math.sqrt(2.0))
            return sin_d, sq

        def gain_of(side, b, width):
            return gain[:, :, side * BLOCKS + b].unsqueeze(1).to_broadcast([P, width, PACK])

        def by_entry(values):
            return values.rearrange("p (u c) -> p u c", c=PACK)

        def aside(step):
            return JB if step in ASIDE_STEPS else 0

        z, z_aside, z_codes, z_sc = {}, {}, {}, {}

        def gain_sine(step, sin_d):
            b, j0, width = STEPS[step]
            cut = aside(step) * PACK
            z[step] = placed([P, 2 * width * PACK - cut], BF16, "z%d" % step, z_slot(step))
            if cut:
                z_aside[step] = placed([P, cut], BF16, "z_aside%d" % step, z_slot(ASIDE_STEPS[0] - 1))
                nc.gpsimd.tensor_tensor(out=z_aside[step][:], in0=sin_d[:, 0:cut], in1=gain_s[:], op=ALU.mult)
            nc.vector.tensor_tensor(
                out=by_entry(z[step][:, 0 : width * PACK - cut]), in0=by_entry(sin_d[:, cut:]),
                in1=gain_of(0, b, width - aside(step)), op=ALU.mult)

        def gain_cosine(step, sq):
            b, j0, width = STEPS[step]
            nc.vector.scalar_tensor_tensor(
                out=by_entry(z[step][:, (width - aside(step)) * PACK :]), in0=by_entry(sq[:]), scalar=1.0,
                in1=gain_of(1, b, width), op0=ALU.subtract, op1=ALU.mult)

        def quantize_z(step, c0, c1, values):
            b, j0, width = STEPS[step]
            if (0, b, j0) not in z_codes:
                if aside(step):
                    codes = placed([P, 2 * width], U32, "z_codes%d" % step, sin_slot(step) + SLOT // 2)
                elif b == 0:
                    codes = placed([P, 2 * width], U32, "z_codes%d" % step, sin_slot(step + 1) + (PACK * P if step else 0))
                else:
                    codes = kept([P, 2 * width], U32, "z_codes%d" % step)
                scales = kept([P, 2 * width], U8, "z_sc%d" % step)
                z_codes["all", step], z_sc["all", step] = codes, scales
                for side in range(2):
                    z_codes[side, b, j0] = codes[:, side * width : (side + 1) * width]
                    z_sc[side, b, j0] = scales[:, side * width : (side + 1) * width]
            nc.vector.quantize_mx(out=z_codes["all", step][:, c0:c1].bitcast(FP8X4), scales=z_sc["all", step][:, c0:c1],
                                  in_=values)

        def quantize_step(step):
            quantize_z(step, aside(step), 2 * STEPS[step][2], z[step][:])
            if aside(step):
                quantize_z(step, 0, aside(step), z_aside[step][:])

        def product(side, step, y=None):
            j0, width = STEPS[step][1:]
            if y is None:
                y = psum_y.tile([P, N // P, width], F32, name="y")
            for n in range(N // P):
                cols = slice(n * P, (n + 1) * P)
                for b in range(BLOCKS):
                    if side == 0:
                        w = w3_w[:, b, 2 * n * P : 2 * (n + 1) * P].bitcast(FP4X4)
                        w_sc = w3_sc[:, b * N + n * P : b * N + (n + 1) * P]
                    else:
                        w, w_sc = w4_codes[2 * b + n][:].bitcast(FP8X4), w4_sc[:, b, cols]
                    nc.tensor.matmul_mx(
                        out=y[:, n, :], lhsT=w, lhsT_scale=w_sc,
                        rhs=z_codes[side, b, j0].bitcast(FP8X4), rhs_scale=z_sc[side, b, j0],
                        start=(b == 0), stop=(b == BLOCKS - 1))
            return y

        def copy_out(step, ys):
            j0, width = STEPS[step][1:]
            held = step + 2 < LAST
            ys_sb = placed([P, N // P, width], F32, "ys_sb%d" % step, sin_slot(step + 2) if held else AT_TAB2 + 8 * j0)
            nc.scalar.copy(out=ys_sb[:], in_=ys[:])
            return ys_sb

        def finish(step, ys_sb, yc):
            j0, width = STEPS[step][1:]
            res = placed([P, N // P, width], F32, "res%d" % step, AT_TAB0 + 8 * j0)
            nc.vector.tensor_tensor(out=res[:], in0=ys_sb[:], in1=yc[:], op=ALU.mult)
            nc.sync.dma_start(out=out[:, j0 : j0 + width].rearrange("(n p) j -> p n j", p=P), in_=res[:])

        def round_w4(piece):
            b, n0 = piece // 2, piece % 2 * P
            late["w4_bf", piece] = placed([P, P, PACK], BF16, "w4_bf%d" % piece, z_slot(piece))
            nc.gpsimd.tensor_scalar(out=late["w4_bf", piece][:], in0=w4_raw[:, b, :, n0 : n0 + P].rearrange("p i c -> p c i"),
                                    scalar1=1.0, scalar2=0.0, op0=ALU.mult, op1=ALU.add)

        def quantize_w4(piece):
            b, cols = piece // 2, slice(piece % 2 * P, (piece % 2 + 1) * P)
            w4_codes[piece] = placed([P, P], U32, "w4_codes%d" % piece, sin_slot(piece + 2))
            nc.vector.quantize_mx(out=w4_codes[piece][:].bitcast(FP8X4), scales=w4_sc[:, b, cols],
                                  in_=late["w4_bf", piece][:].rearrange("p c i -> p (c i)"))

        def side_work(step):
            if step == 1:
                round_late(1, placed([P, PACK * K_PASS], BF16, "w1_bf_late1", sin_slot(step) + SLOT // 4))
            if step in (0, 2):
                a = step // 2
                quantize_w1(1, a, placed([P, K_PASS], U32, "w1_codes_late%d" % a, sin_slot(step) + a * SLOT // 2), late["w1_bf", a])
            if step - 2 in range(W4_PIECES):
                quantize_w4(step - 2)

        sums, copied = {}, {}
        for step in range(LAST):
            b, j0, width = STEPS[step]
            sin_d, sq = angles(step)
            gain_sine(step, sin_d)
            due = step - 2 in sums
            if due:
                copied[step - 2] = copy_out(step - 2, sums[step - 2][0])
            gain_cosine(step, sq)
            if due:
                finish(step - 2, copied[step - 2], sums[step - 2][1])
            side_work(step)
            if step > 0 and STEPS[step - 1][0] == 0:
                quantize_step(step - 1)
            if b == BLOCKS - 1 and step < LAST - 1:
                quantize_step(step)
            if step - 1 in range(W4_PIECES):
                round_w4(step - 1)
            if b == BLOCKS - 1 and step < LAST - 1:
                yc = product(1, step)
                sums[step] = (product(0, step), yc)
        sin_d, sq = angles(LAST)
        gain_sine(LAST, sin_d)
        quantize_step(LAST - 1)
        both = psum_y.tile([P, 2, N // P, JB], F32, name="y")
        yc = product(1, LAST - 1, both[:, 1])
        sums[LAST - 1] = (product(0, LAST - 1, both[:, 0]), yc)
        for step in (LAST - 2, LAST - 1):
            copied[step] = copy_out(step, sums[step][0])
        quantize_z(LAST, 0, JB, z[LAST][:, 0 : JB * PACK])
        gain_cosine(LAST, sq)
        copied[LAST] = copy_out(LAST, product(0, LAST))
        quantize_z(LAST, JB, 2 * JB, z[LAST][:, JB * PACK :])
        sums[LAST] = (None, product(1, LAST, psum_d.tile([P, N // P, JB], F32, name="bank")))
        for step in range(LAST - 2, LAST + 1):
            finish(step, copied[step], sums[step][1])
